import numpy as np
import ml_dtypes


def mxq(x, axis, fmt="e4m3"):
    dtype, down = {"e4m3": (ml_dtypes.float8_e4m3fn, 7), "e5m2": (ml_dtypes.float8_e5m2, 14)}[fmt]
    v = np.moveaxis(np.asarray(x, np.float32).astype(ml_dtypes.bfloat16).astype(np.float64), axis, -1)
    blocks = v.reshape(v.shape[:-1] + (-1, 32))
    amax = np.abs(blocks).max(-1, keepdims=True)
    byte = np.maximum(np.where(amax > 0, np.frexp(amax)[1] - 1 + 127, 0) - down, 1)
    scale = np.exp2(byte - 127.0)
    codes = (blocks / scale).astype(np.float32).astype(dtype).astype(np.float64)
    return np.moveaxis((codes * scale).reshape(v.shape), -1, axis)


WIDE = False


def mx_kscale(k):
    if not WIDE:
        return np.ones(k)
    levels = np.array([10, -10, 5, -5, 0])
    if k % 512:
        return np.exp2(np.random.permutation(np.resize(levels, k // 32))).repeat(32)
    a = np.empty((k // 512, 16))
    for p in range(k // 512):
        a[p, :8] = np.random.permutation(np.resize(levels, 8))
        for g in range(8):
            far = levels[np.abs(levels - a[p, g]) >= 10]
            a[p, g + 8] = far[np.random.randint(len(far))]
    return np.exp2(a.ravel()).repeat(32)


def f64(x):
    return np.asarray(x).astype(np.float64)


def striped(idx):
    return np.tile(idx.reshape(-1, 16).T, (8, 1)).astype(np.uint16)


def unstriped(offs):
    return offs[:16].T.reshape(-1).astype(np.int64)


E2M1 = np.array([0.0, 0.5, 1.0, 1.5, 2.0, 3.0, 4.0, 6.0, -0.0, -0.5, -1.0, -1.5, -2.0, -3.0, -4.0, -6.0])


def pack_weight(w, fmt):
    k, n = w.shape
    w = f64(np.asarray(w, np.float32).astype(ml_dtypes.bfloat16)).reshape(k // 32, 32, n)
    amax = np.abs(w).max(1)
    if fmt == "e4m3":
        byte = np.frexp(amax)[1] - 1 + 127 - 7
    else:
        mant, ex = np.frexp(amax / 6.0)
        byte = np.where(mant > 0.5, ex, ex - 1) + 127
    byte = np.clip(np.where(amax > 0, byte, 1), 1, 254)
    scaled = (w * np.exp2(127.0 - byte)[:, None, :]).reshape(k, n).astype(np.float32)
    by_word = np.ascontiguousarray(scaled.reshape(k // 512, 128, 4, n).transpose(0, 1, 3, 2))
    if fmt == "e4m3":
        words = by_word.astype(ml_dtypes.float8_e4m3fn).view(np.uint8)
    else:
        c = by_word.astype(ml_dtypes.float4_e2m1fn).view(np.uint8) & 0xF
        words = (c[..., 0::2] | (c[..., 1::2] << 4)).reshape(k // 512, 128, 2 * n)
    return np.ascontiguousarray(words), np.ascontiguousarray(byte.astype(np.uint8).reshape(k // 512, 16, n))


def unpack_weight(words, scales, fmt):
    g, _, n = scales.shape
    words = np.ascontiguousarray(words).reshape(g, 128, n, -1)
    if fmt == "e4m3":
        vals = words.view(ml_dtypes.float8_e4m3fn).astype(np.float64)
    else:
        nib = np.empty((g, 128, n, 4), np.uint8)
        nib[..., 0::2] = words & 0xF
        nib[..., 1::2] = words >> 4
        vals = E2M1[nib]
    vals = vals * np.repeat(np.exp2(scales.astype(np.float64) - 127.0), 8, axis=1)[..., None]
    return vals.transpose(0, 1, 3, 2).reshape(g * 512, n)


def gelu(v):
    return 0.5 * v * (1.0 + np.tanh(np.sqrt(2.0 / np.pi) * (v + 0.044715 * v**3)))


K, T, S, H, N = 512, 2048, 1024, 1024, 256

def setup_inputs():
    n = np.random.standard_normal
    s = mx_kscale(K)[:, None]
    u = mx_kscale(H)[:, None]
    tab_words, tab_scales = pack_weight(n((K, T)) * s, "e4m3")
    w1_words, w1_scales = pack_weight(0.4 * n((K, H)) / np.sqrt(K) / s, "e2m1")
    w2 = 0.4 * n((K, H)) / np.sqrt(K) / s
    w3_words, w3_scales = pack_weight(n((K, H)) / np.sqrt(K) / s * u.T, "e4m3")
    w4 = n((H, N)) / np.sqrt(H) / u
    return {"tab_words": tab_words, "tab_scales": tab_scales,
            "offs": striped(np.random.permutation(T)[:S]),
            "offs2": striped(np.random.permutation(T)[:S]),
            "offs3": striped(np.random.permutation(T)[:S]),
            "w1_words": w1_words, "w1_scales": w1_scales,
            "w2": w2.astype(np.float32),
            "w3_words": w3_words, "w3_scales": w3_scales,
            "w4": w4.astype(np.float32),
            "b1": (0.3 * n(H)).astype(np.float32),
            "b3": (0.3 * n(H) * u[:, 0]).astype(np.float32),
            "b4": (0.3 * n(N)).astype(np.float32)}

def reference(tab_words, tab_scales, offs, offs2, offs3, w1_words, w1_scales, w2, w3_words, w3_scales, w4, b1, b3, b4):
    v1 = unpack_weight(tab_words, tab_scales, "e4m3")[:, unstriped(offs)]
    v2 = unpack_weight(tab_words, tab_scales, "e4m3")[:, unstriped(offs2)]
    v3 = unpack_weight(tab_words, tab_scales, "e4m3")[:, unstriped(offs3)]
    w1 = unpack_weight(w1_words, w1_scales, "e2m1")
    w3 = unpack_weight(w3_words, w3_scales, "e4m3")
    e = w1.T @ v1 + mxq(f64(w2), 0, "e4m3").T @ v2
    d = w3.T @ v3
    h = np.exp(e + f64(b1)[:, None]) * (d + f64(b3)[:, None])
    y = mxq(f64(w4), 0, "e4m3").T @ mxq(h, 0, "e4m3")
    return y + f64(b4)[:, None]

@@ -1,0 +1,301 @@
+from contextlib import ExitStack
+
+import concourse.mybir as mybir
+
+K, T, S, H, N = 512, 2048, 1024, 1024, 256
+FLOPS = 2 * (3 * K * H * S + H * N * S)
+
+F32 = mybir.dt.float32
+BF16 = mybir.dt.bfloat16
+I32 = mybir.dt.int32
+U32 = mybir.dt.uint32
+U16 = mybir.dt.uint16
+U8 = mybir.dt.uint8
+FP8X4 = mybir.dt.float8_e4m3fn_x4
+FP4X4 = mybir.dt.float4_e2m1fn_x4
+ACT = mybir.ActivationFunctionType
+ALU = mybir.AluOpType
+
+P = 128
+PACK = 4
+BANK = 512
+HALVES = S // BANK
+PASSES = H // (P * PACK)
+W3_PLANE = 4
+TAIL = ((0, 256), (256, 384), (384, 512))
+ORDER = ("down", "up", "own")
+
+
+def load_scale_rows(queue, plane, rows, first, quadrants=range(4)):
+    for q in quadrants:
+        queue.dma_start(
+            out=plane[32 * q + first : 32 * q + first + 4, :].bitcast(I32),
+            in_=rows[4 * q : 4 * q + 4, :].bitcast(I32),
+        )
+
+
+def tile_list_codon_context_rate_kernel(
+    tc, tab_words, tab_scales, offs, offs2, offs3, w1_words, w1_scales, w2, w3_words, w3_scales, w4, b1, b3, b4, out
+):
+    nc = tc.nc
+    with ExitStack() as ctx:
+        keep = ctx.enter_context(tc.tile_pool(name="keep", bufs=1))
+        psum = ctx.enter_context(tc.psum_pool(name="psum", bufs=1))
+
+        def held(shape, dtype, name, tag=None):
+            return keep.tile(shape, dtype, name=name, tag=tag or name, align_bytes=64)
+
+        tab_plane = held([P, T], U8, "tab_plane")
+        nc.vector.memset(tab_plane[:].bitcast(I32), 0)
+        w13_plane_raw = held([P, H], U8, "w13_plane_raw")
+        nc.gpsimd.memset(w13_plane_raw[:].bitcast(I32), 0)
+        warm_in = held([P, 1], F32, "warm_in")
+        warm_out = held([P, 1], F32, "warm_out")
+        nc.vector.memset(warm_in[:], 0.0)
+        nc.scalar.activation(warm_out[:], warm_in[:], ACT.Exp)
+
+        lists = {}
+        for name, src in (("down", offs3), ("up", offs2), ("own", offs)):
+            lists[name] = keep.tile([P, S // 16], U16, name="list_" + name)
+            nc.sync.dma_start(lists[name][:], src)
+
+        w2_rows = w2.rearrange("(p i) c -> p i c", i=PACK)
+        tab = held([P, T], I32, "tab", "warm_out")
+        w13_raw = held([P, H + H // 2], I32, "w13_raw", "warm_in")
+        w3_raw = w13_raw[:, 0:H]
+        w1_raw = w13_raw[:, H : H + H // 2].bitcast(U8)
+        b1_sb = held([P, PASSES, PACK], F32, "b1_sb")
+        b3_sb = held([P, PASSES, PACK], F32, "b3_sb")
+        b4_sb = held([P, N // P], F32, "b4_sb")
+        w2_raw = {}
+
+        def load_w2(b):
+            w2_raw[b] = held([P, PACK, BANK], F32, "w2_raw%d" % b, "float_weights")
+            (nc.sync if b else nc.scalar).dma_start(out=w2_raw[b][:], in_=w2_rows[:, :, b * BANK : (b + 1) * BANK])
+
+        load_scale_rows(nc.sync, tab_plane, tab_scales[0], 0)
+        load_w2(0)
+        load_scale_rows(nc.sync, w13_plane_raw, w3_scales[0], W3_PLANE)
+        load_scale_rows(nc.sync, w13_plane_raw, w1_scales[0], 0, range(2))
+        nc.sync.dma_start(out=tab[:], in_=tab_words[0].rearrange("p t i -> p (t i)").bitcast(I32))
+        load_scale_rows(nc.sync, w13_plane_raw, w1_scales[0], 0, range(2, 4))
+        nc.sync.dma_start(out=w3_raw, in_=w3_words[0].rearrange("p c i -> p (c i)").bitcast(I32))
+        nc.sync.dma_start(out=w13_raw[:, H : H + H // 2], in_=w1_words[0].bitcast(I32))
+        nc.gpsimd.dma_start(out=b3_sb[:], in_=b3.rearrange("(b p t) -> p b t", p=P, t=PACK))
+        nc.gpsimd.dma_start(out=b1_sb[:], in_=b1.rearrange("(b p t) -> p b t", p=P, t=PACK))
+        with nc.allow_non_contiguous_dma(reason="one bias value a partition"):
+            nc.gpsimd.dma_start(out=b4_sb[:], in_=b4.rearrange("(c p) -> p c", p=P))
+
+        late_words = {}
+        picked_words = {}
+        picked_plane = {}
+
+        def gather_scales(name, half):
+            dst = late_planes[:, ORDER.index(name), :] if half else held([P, BANK], U8, "plane_%s%d" % (name, half))[:]
+            cols = lists[name][:, half * BANK // 16 : (half + 1) * BANK // 16]
+            nc.vector.tensor_copy(dst, tab_plane[:].indirect(cols))
+            picked_plane[name, half] = dst
+
+        def gather_words(name, half):
+            dst = late_words[name] if half else held([P, BANK], U32, "words_%s%d" % (name, half))[:]
+            cols = lists[name][:, half * BANK // 16 : (half + 1) * BANK // 16]
+            nc.vector.tensor_copy(dst, tab[:].bitcast(U32).indirect(cols))
+            picked_words[name, half] = dst
+
+        M = H // PACK
+        w13_plane = held([P, H], U8, "w13_plane")
+        w3_dealt = held([P, H], I32, "w3_dealt")
+        w1_dealt = held([P, 2 * H], U8, "w1_dealt")
+
+        def deal_scales():
+            nc.vector.tensor_copy(
+                out=w13_plane[:].rearrange("p (t c i) -> p c t i", t=PACK, i=16),
+                in_=w13_plane_raw[:].rearrange("p (c i t) -> p c t i", t=PACK, i=16),
+            )
+
+        def deal_w3():
+            nc.vector.tensor_copy(
+                out=w3_dealt[:].rearrange("p (t c i) -> p c t i", t=PACK, i=4),
+                in_=w3_raw.rearrange("p (c i t) -> p c t i", t=PACK, i=4),
+            )
+
+        def deal_w1():
+            nc.vector.tensor_copy(
+                out=w1_dealt[:].rearrange("p (t c i e) -> p c t i e", t=PACK, i=8, e=2),
+                in_=w1_raw.rearrange("p (c i t e) -> p c t i e", t=PACK, i=8, e=2),
+            )
+
+        w2_bf = [held([P, PACK * P * PACK], BF16, "w2_bf%d" % b) for b in range(PASSES)]
+        w2_codes = [held([P, BANK], U32, "w2_codes%d" % b) for b in range(PASSES)]
+        w2_plane = [held([P, BANK], U8, "w2_plane%d" % b) for b in range(PASSES)]
+
+        def cast_w2(b):
+            nc.scalar.copy(
+                out=w2_bf[b][:].rearrange("p (t m i) -> p m i t", t=PACK, i=PACK),
+                in_=w2_raw[b][:].rearrange("p i (m t) -> p m i t", t=PACK),
+            )
+
+        def quant_w2(b):
+            nc.vector.quantize_mx(out=w2_codes[b][:].bitcast(FP8X4), scales=w2_plane[b][:], in_=w2_bf[b][:])
+
+        w4_bf = held([P, PASSES * N * PACK], BF16, "w4_bf")
+        w4_codes = held([P, PASSES * N], U32, "w4_codes")
+        w4_plane = held([P, PASSES * N], U8, "w4_plane")
+
+        def cast_w4():
+            nc.vector.tensor_copy(
+                out=w4_bf[:].rearrange("p (b c j i) -> p b c i j", b=PASSES, j=4, i=PACK),
+                in_=w4_raw[:].rearrange("p b i (c j) -> p b c i j", j=4),
+            )
+
+        def quant_w4():
+            nc.vector.quantize_mx(out=w4_codes[:].bitcast(FP8X4), scales=w4_plane[:], in_=w4_bf[:])
+
+        down = {}
+        rate = {}
+        h_codes = {}
+        h_plane = {}
+        h_bf = {}
+
+        def stage_d(half, b):
+            dst = held([P, PACK, BANK], F32, "down%d%d" % (half, b))
+            for t in range(PACK):
+                cols = slice(t * M + b * P, t * M + (b + 1) * P)
+                acc = psum.tile([P, BANK], F32, name="acc_d", tag="acc_d", bufs=2)
+                nc.tensor.matmul_mx(
+                    out=acc[:],
+                    lhsT=w3_dealt[:, cols].bitcast(FP8X4),
+                    lhsT_scale=w13_plane[W3_PLANE:P, cols],
+                    rhs=picked_words["down", half].bitcast(FP8X4),
+                    rhs_scale=picked_plane["down", half],
+                    start=True,
+                    stop=True,
+                )
+                nc.scalar.activation(dst[:, t, :], acc[:], ACT.Identity, bias=b3_sb[:, b, t : t + 1])
+            down[half, b] = dst
+
+        def stage_e(half, b, pieces=((0, BANK),)):
+            dst = held([P, PACK, BANK], F32, "rate%d%d" % (half, b))
+            banks = []
+            for t in range(PACK):
+                c0 = t * M + b * P
+                acc = psum.tile([P, BANK], F32, name="acc_e", tag="acc_e", bufs=4)
+                nc.tensor.matmul_mx(
+                    out=acc[:],
+                    lhsT=w2_codes[b][:, t * P : (t + 1) * P].bitcast(FP8X4),
+                    lhsT_scale=w2_plane[b][:, t * P : (t + 1) * P],
+                    rhs=picked_words["up", half].bitcast(FP8X4),
+                    rhs_scale=picked_plane["up", half],
+                    start=True,
+                    stop=False,
+                )
+                nc.tensor.matmul_mx(
+                    out=acc[:],
+                    lhsT=w1_dealt[:, 2 * c0 : 2 * (c0 + P)].bitcast(FP4X4),
+                    lhsT_scale=w13_plane[:, c0 : c0 + P],
+                    rhs=picked_words["own", half].bitcast(FP8X4),
+                    rhs_scale=picked_plane["own", half],
+                    start=False,
+                    stop=True,
+                )
+                banks.append(acc)
+            for j0, j1 in pieces:
+                for t in range(PACK):
+                    nc.scalar.activation(dst[:, t, j0:j1], banks[t][:, j0:j1], ACT.Exp, bias=b1_sb[:, b, t : t + 1])
+            rate[half, b] = dst
+
+        def multiply(half, b, j0, j1):
+            dst = held([P, (j1 - j0) * PACK], BF16, "h_bf%d%d_%d" % (half, b, j0))
+            nc.vector.tensor_tensor(
+                out=dst[:].rearrange("p (c i t) -> p c t i", i=2, t=PACK),
+                in0=rate[half, b][:, :, j0:j1].rearrange("p t (c i) -> p c t i", i=2),
+                in1=down[half, b][:, :, j0:j1].rearrange("p t (c i) -> p c t i", i=2),
+                op=ALU.mult,
+            )
+            h_bf[half, b, j0] = dst
+
+        def quant_h(half, b, j0, j1):
+            codes = held([P, j1 - j0], U32, "h_codes%d%d_%d" % (half, b, j0))
+            plane = held([P, j1 - j0], U8, "h_plane%d%d_%d" % (half, b, j0))
+            nc.vector.quantize_mx(out=codes[:].bitcast(FP8X4), scales=plane[:], in_=h_bf[half, b, j0][:])
+            h_codes[half, b, j0] = codes
+            h_plane[half, b, j0] = plane
+
+        def stage_y(half, j0, j1, last):
+            width = j1 - j0
+            for c in range(N // P):
+                acc = psum.tile([P, BANK], F32, name="acc_y", tag="acc_y", bufs=2)
+                for b in range(PASSES):
+                    cols = slice(b * N + c * P, b * N + (c + 1) * P)
+                    nc.tensor.matmul_mx(
+                        out=acc[:, 0:width],
+                        lhsT=w4_codes[:, cols].bitcast(FP8X4),
+                        lhsT_scale=w4_plane[:, cols],
+                        rhs=h_codes[half, b, j0][:].bitcast(FP8X4),
+                        rhs_scale=h_plane[half, b, j0][:],
+                        start=(b == 0),
+                        stop=(b == PASSES - 1),
+                    )
+                res = held([P, width], F32, "res%d%d_%d" % (half, c, j0))
+                if last and c == 1:
+                    nc.vector.tensor_scalar(res[:], acc[:, 0:width], b4_sb[:, c : c + 1], None, ALU.add)
+                else:
+                    nc.scalar.activation(res[:], acc[:, 0:width], ACT.Identity, bias=b4_sb[:, c : c + 1])
+                nc.sync.dma_start(out=out[c * P : (c + 1) * P, half * BANK + j0 : half * BANK + j1], in_=res[:])
+
+        for name in ("down", "up", "own"):
+            gather_scales(name, 0)
+        cast_w2(0)
+        load_w2(1)
+        gather_words("down", 0)
+        deal_scales()
+        deal_w3()
+        quant_w2(0)
+        stage_d(0, 0)
+        gather_words("up", 0)
+        gather_words("own", 0)
+        deal_w1()
+        stage_d(0, 1)
+        stage_e(0, 0)
+        cast_w2(1)
+        w4_raw = held([P, PASSES, PACK, N], F32, "w4_raw", "float_weights")
+        nc.sync.dma_start(
+            out=w4_raw[:].rearrange("p b i n -> p b (i n)"),
+            in_=w4.rearrange("(b p i) n -> p b (i n)", p=P, i=PACK),
+        )
+        late_planes = held([P, 3, BANK], U8, "late_planes", "warm_in")
+        late_down = held([P, BANK], U32, "late_down", "w2_bf0")
+        late_words["down"] = late_down[:]
+        gather_scales("down", 1)
+        gather_words("down", 1)
+        for name in ("up", "own"):
+            gather_scales(name, 1)
+        quant_w2(1)
+        late_pair = held([P, 2, BANK], U32, "late_pair", "w2_bf1")
+        late_words["up"] = late_pair[:, 0, :]
+        late_words["own"] = late_pair[:, 1, :]
+        stage_e(0, 1)
+        for name in ("up", "own"):
+            gather_words(name, 1)
+        cast_w4()
+        stage_d(1, 0)
+        stage_e(1, 0)
+        multiply(0, 0, 0, BANK)
+        quant_w4()
+        multiply(0, 1, 0, BANK)
+        quant_h(0, 0, 0, BANK)
+        quant_h(0, 1, 0, BANK)
+        stage_d(1, 1)
+        stage_y(0, 0, BANK, False)
+        stage_e(1, 1, TAIL)
+        for j0, j1 in TAIL:
+            multiply(1, 0, j0, j1)
+        for j0, j1 in TAIL:
+            quant_h(1, 0, j0, j1)
+        multiply(1, 1, *TAIL[0])
+        for n, piece in enumerate(TAIL):
+            last = n == len(TAIL) - 1
+            if not last:
+                multiply(1, 1, *TAIL[n + 1])
+            quant_h(1, 1, *piece)
+            stage_y(1, *piece, last)

@@ -21,7 +21,7 @@ PACK = 4
 BANK = 512
 HALVES = S // BANK
 PASSES = H // (P * PACK)
-W3_PLANE = 4
+BANKS = {"acc_d": 2, "acc_e": 4, "acc_y": 2}
 TAIL = ((0, 256), (256, 384), (384, 512))
 ORDER = ("down", "up", "own")
 
@@ -40,6 +40,7 @@ def tile_list_codon_context_rate_kernel(
     nc = tc.nc
     with ExitStack() as ctx:
         keep = ctx.enter_context(tc.tile_pool(name="keep", bufs=1))
+        early = ctx.enter_context(tc.tile_pool(name="early", bufs=1))
         psum = ctx.enter_context(tc.psum_pool(name="psum", bufs=1))
 
         def held(shape, dtype, name, tag=None):
@@ -47,12 +48,18 @@ def tile_list_codon_context_rate_kernel(
 
         tab_plane = held([P, T], U8, "tab_plane")
         nc.vector.memset(tab_plane[:].bitcast(I32), 0)
-        w13_plane_raw = held([P, H], U8, "w13_plane_raw")
-        nc.gpsimd.memset(w13_plane_raw[:].bitcast(I32), 0)
-        warm_in = held([P, 1], F32, "warm_in")
-        warm_out = held([P, 1], F32, "warm_out")
-        nc.vector.memset(warm_in[:], 0.0)
-        nc.scalar.activation(warm_out[:], warm_in[:], ACT.Exp)
+
+        TAB_AT, W2_AT, W4_AT, W1_AT, PLANE_AT, BIAS_AT, W3_AT, END_AT = 0, 8192, 24576, 32768, 35840, 42496, 42624, 46720
+
+        def placed(shape, dtype, name, at):
+            return early.tile(shape, dtype, name=name, offset=at, align_bytes=64)
+
+        w3_plane_raw = placed([P, H], U8, "w3_plane_raw", END_AT)
+        nc.vector.memset(w3_plane_raw[:].bitcast(I32), 0)
+        warm = placed([P, END_AT // 4], F32, "warm", 0)
+        nc.scalar.activation(warm[:, 0:1], w3_plane_raw[:, 0:4].bitcast(F32), ACT.Exp)
+        w1_plane_raw = placed([P, H], U8, "w1_plane_raw", PLANE_AT)
+        nc.vector.memset(w1_plane_raw[:].bitcast(I32), 0)
 
         lists = {}
         for name, src in (("down", offs3), ("up", offs2), ("own", offs)):
@@ -60,31 +67,36 @@ def tile_list_codon_context_rate_kernel(
             nc.sync.dma_start(lists[name][:], src)
 
         w2_rows = w2.rearrange("(p i) c -> p i c", i=PACK)
-        tab = held([P, T], I32, "tab", "warm_out")
-        w13_raw = held([P, H + H // 2], I32, "w13_raw", "warm_in")
-        w3_raw = w13_raw[:, 0:H]
-        w1_raw = w13_raw[:, H : H + H // 2].bitcast(U8)
-        b1_sb = held([P, PASSES, PACK], F32, "b1_sb")
-        b3_sb = held([P, PASSES, PACK], F32, "b3_sb")
-        b4_sb = held([P, N // P], F32, "b4_sb")
+        tab = placed([P, T], I32, "tab", TAB_AT)
+        w3_raw = placed([P, H], I32, "w3_raw", W3_AT)
+        w1_raw = placed([P, H // 2], I32, "w1_raw", W1_AT)
+        bias = placed([P, 24], F32, "bias", BIAS_AT)
+        b1_sb = bias[:, 0:8].rearrange("p (b t) -> p b t", t=PACK)
+        b3_sb = bias[:, 8:16].rearrange("p (b t) -> p b t", t=PACK)
+        b4_sb = bias[:, 16:18]
         w2_raw = {}
 
         def load_w2(b):
-            w2_raw[b] = held([P, PACK, BANK], F32, "w2_raw%d" % b, "float_weights")
-            (nc.sync if b else nc.scalar).dma_start(out=w2_raw[b][:], in_=w2_rows[:, :, b * BANK : (b + 1) * BANK])
+            w2_raw[b] = placed([P, PACK, BANK], F32, "w2_raw%d" % b, W2_AT + 8192 * b)
+            nc.sync.dma_start(out=w2_raw[b][:], in_=w2_rows[:, :, b * BANK : (b + 1) * BANK])
 
         load_scale_rows(nc.sync, tab_plane, tab_scales[0], 0)
-        load_w2(0)
-        load_scale_rows(nc.sync, w13_plane_raw, w3_scales[0], W3_PLANE)
-        load_scale_rows(nc.sync, w13_plane_raw, w1_scales[0], 0, range(2))
         nc.sync.dma_start(out=tab[:], in_=tab_words[0].rearrange("p t i -> p (t i)").bitcast(I32))
-        load_scale_rows(nc.sync, w13_plane_raw, w1_scales[0], 0, range(2, 4))
-        nc.sync.dma_start(out=w3_raw, in_=w3_words[0].rearrange("p c i -> p (c i)").bitcast(I32))
-        nc.sync.dma_start(out=w13_raw[:, H : H + H // 2], in_=w1_words[0].bitcast(I32))
-        nc.gpsimd.dma_start(out=b3_sb[:], in_=b3.rearrange("(b p t) -> p b t", p=P, t=PACK))
-        nc.gpsimd.dma_start(out=b1_sb[:], in_=b1.rearrange("(b p t) -> p b t", p=P, t=PACK))
+        load_w2(0)
+        load_scale_rows(nc.sync, w3_plane_raw, w3_scales[0], 0)
+        nc.sync.dma_start(out=w3_raw[:], in_=w3_words[0].rearrange("p c i -> p (c i)").bitcast(I32))
+        nc.sync.dma_start(out=b3_sb, in_=b3.rearrange("(b p t) -> p b t", p=P, t=PACK))
+        nc.sync.dma_start(out=w1_raw[:], in_=w1_words[0].bitcast(I32))
+        load_scale_rows(nc.sync, w1_plane_raw, w1_scales[0], 0)
+        nc.sync.dma_start(out=b1_sb, in_=b1.rearrange("(b p t) -> p b t", p=P, t=PACK))
+        load_w2(1)
+        w4_raw = placed([P, PASSES, PACK, N], F32, "w4_raw", W4_AT)
+        nc.sync.dma_start(
+            out=w4_raw[:].rearrange("p b i n -> p b (i n)"),
+            in_=w4.rearrange("(b p i) n -> p b (i n)", p=P, i=PACK),
+        )
         with nc.allow_non_contiguous_dma(reason="one bias value a partition"):
-            nc.gpsimd.dma_start(out=b4_sb[:], in_=b4.rearrange("(c p) -> p c", p=P))
+            nc.sync.dma_start(out=b4_sb, in_=b4.rearrange("(c p) -> p c", p=P))
 
         late_words = {}
         picked_words = {}
@@ -97,32 +109,37 @@ def tile_list_codon_context_rate_kernel(
             picked_plane[name, half] = dst
 
         def gather_words(name, half):
-            dst = late_words[name] if half else held([P, BANK], U32, "words_%s%d" % (name, half))[:]
+            if half:
+                dst = late_words[name]
+            elif name == "own":
+                dst = placed([P, BANK], U32, "words_own", END_AT - 1024)[:]
+            else:
+                dst = held([P, BANK], U32, "words_" + name)[:]
             cols = lists[name][:, half * BANK // 16 : (half + 1) * BANK // 16]
             nc.vector.tensor_copy(dst, tab[:].bitcast(U32).indirect(cols))
             picked_words[name, half] = dst
 
         M = H // PACK
-        w13_plane = held([P, H], U8, "w13_plane")
+        w3_plane = held([P, H], U8, "w3_plane")
         w3_dealt = held([P, H], I32, "w3_dealt")
         w1_dealt = held([P, 2 * H], U8, "w1_dealt")
 
-        def deal_scales():
+        def deal_scales(dealt, raw):
             nc.vector.tensor_copy(
-                out=w13_plane[:].rearrange("p (t c i) -> p c t i", t=PACK, i=16),
-                in_=w13_plane_raw[:].rearrange("p (c i t) -> p c t i", t=PACK, i=16),
+                out=dealt[:].rearrange("p (t c i) -> p c t i", t=PACK, i=16),
+                in_=raw[:].rearrange("p (c i t) -> p c t i", t=PACK, i=16),
             )
 
         def deal_w3():
             nc.vector.tensor_copy(
                 out=w3_dealt[:].rearrange("p (t c i) -> p c t i", t=PACK, i=4),
-                in_=w3_raw.rearrange("p (c i t) -> p c t i", t=PACK, i=4),
+                in_=w3_raw[:].rearrange("p (c i t) -> p c t i", t=PACK, i=4),
             )
 
         def deal_w1():
             nc.vector.tensor_copy(
-                out=w1_dealt[:].rearrange("p (t c i e) -> p c t i e", t=PACK, i=8, e=2),
-                in_=w1_raw.rearrange("p (c i t e) -> p c t i e", t=PACK, i=8, e=2),
+                out=w1_dealt[:].bitcast(U16).rearrange("p (t c i) -> p c t i", t=PACK, i=8),
+                in_=w1_raw[:].bitcast(U16).rearrange("p (c i t) -> p c t i", t=PACK, i=8),
             )
 
         w2_bf = [held([P, PACK * P * PACK], BF16, "w2_bf%d" % b) for b in range(PASSES)]
@@ -143,7 +160,7 @@ def tile_list_codon_context_rate_kernel(
         w4_plane = held([P, PASSES * N], U8, "w4_plane")
 
         def cast_w4():
-            nc.vector.tensor_copy(
+            nc.scalar.copy(
                 out=w4_bf[:].rearrange("p (b c j i) -> p b c i j", b=PASSES, j=4, i=PACK),
                 in_=w4_raw[:].rearrange("p b i (c j) -> p b c i j", j=4),
             )
@@ -165,7 +182,7 @@ def tile_list_codon_context_rate_kernel(
                 nc.tensor.matmul_mx(
                     out=acc[:],
                     lhsT=w3_dealt[:, cols].bitcast(FP8X4),
-                    lhsT_scale=w13_plane[W3_PLANE:P, cols],
+                    lhsT_scale=w3_plane[:, cols],
                     rhs=picked_words["down", half].bitcast(FP8X4),
                     rhs_scale=picked_plane["down", half],
                     start=True,
@@ -192,7 +209,7 @@ def tile_list_codon_context_rate_kernel(
                 nc.tensor.matmul_mx(
                     out=acc[:],
                     lhsT=w1_dealt[:, 2 * c0 : 2 * (c0 + P)].bitcast(FP4X4),
-                    lhsT_scale=w13_plane[:, c0 : c0 + P],
+                    lhsT_scale=w1_plane[:, c0 : c0 + P],
                     rhs=picked_words["own", half].bitcast(FP8X4),
                     rhs_scale=picked_plane["own", half],
                     start=False,
@@ -221,10 +238,10 @@ def tile_list_codon_context_rate_kernel(
             h_codes[half, b, j0] = codes
             h_plane[half, b, j0] = plane
 
-        def stage_y(half, j0, j1, last):
+        def stage_y(half, j0, j1, last, tag="acc_y"):
             width = j1 - j0
             for c in range(N // P):
-                acc = psum.tile([P, BANK], F32, name="acc_y", tag="acc_y", bufs=2)
+                acc = psum.tile([P, BANK], F32, name="acc_y", tag=tag, bufs=BANKS[tag])
                 for b in range(PASSES):
                     cols = slice(b * N + c * P, b * N + (c + 1) * P)
                     nc.tensor.matmul_mx(
@@ -243,51 +260,44 @@ def tile_list_codon_context_rate_kernel(
                     nc.scalar.activation(res[:], acc[:, 0:width], ACT.Identity, bias=b4_sb[:, c : c + 1])
                 nc.sync.dma_start(out=out[c * P : (c + 1) * P, half * BANK + j0 : half * BANK + j1], in_=res[:])
 
-        for name in ("down", "up", "own"):
+        for name in ORDER:
             gather_scales(name, 0)
         cast_w2(0)
-        load_w2(1)
         gather_words("down", 0)
-        deal_scales()
-        deal_w3()
-        quant_w2(0)
-        stage_d(0, 0)
         gather_words("up", 0)
+        deal_scales(w3_plane, w3_plane_raw)
+        deal_w3()
+        stage_d(0, 0)
         gather_words("own", 0)
+        quant_w2(0)
         deal_w1()
+        w1_plane = placed([P, H], U8, "w1_plane", W1_AT)
+        deal_scales(w1_plane, w1_plane_raw)
         stage_d(0, 1)
         stage_e(0, 0)
         cast_w2(1)
-        w4_raw = held([P, PASSES, PACK, N], F32, "w4_raw", "float_weights")
-        nc.sync.dma_start(
-            out=w4_raw[:].rearrange("p b i n -> p b (i n)"),
-            in_=w4.rearrange("(b p i) n -> p b (i n)", p=P, i=PACK),
-        )
-        late_planes = held([P, 3, BANK], U8, "late_planes", "warm_in")
-        late_down = held([P, BANK], U32, "late_down", "w2_bf0")
-        late_words["down"] = late_down[:]
+        late_planes = placed([P, 3, BANK], U8, "late_planes", PLANE_AT - 1024)
+        late_codes = placed([P, 3, BANK], U32, "late_codes", PLANE_AT + 512)
+        for n, name in enumerate(ORDER):
+            late_words[name] = late_codes[:, n, :]
         gather_scales("down", 1)
         gather_words("down", 1)
+        quant_w2(1)
+        stage_d(1, 0)
+        stage_e(0, 1)
+        cast_w4()
         for name in ("up", "own"):
             gather_scales(name, 1)
-        quant_w2(1)
-        late_pair = held([P, 2, BANK], U32, "late_pair", "w2_bf1")
-        late_words["up"] = late_pair[:, 0, :]
-        late_words["own"] = late_pair[:, 1, :]
-        stage_e(0, 1)
-        for name in ("up", "own"):
             gather_words(name, 1)
-        cast_w4()
-        stage_d(1, 0)
         stage_e(1, 0)
-        multiply(0, 0, 0, BANK)
-        quant_w4()
-        multiply(0, 1, 0, BANK)
-        quant_h(0, 0, 0, BANK)
-        quant_h(0, 1, 0, BANK)
         stage_d(1, 1)
-        stage_y(0, 0, BANK, False)
+        multiply(0, 0, 0, BANK)
+        quant_h(0, 0, 0, BANK)
+        multiply(0, 1, 0, BANK)
+        quant_w4()
+        quant_h(0, 1, 0, BANK)
         stage_e(1, 1, TAIL)
+        stage_y(0, 0, BANK, False, "acc_d")
         for j0, j1 in TAIL:
             multiply(1, 0, j0, j1)
         for j0, j1 in TAIL:
@@ -298,4 +308,4 @@ def tile_list_codon_context_rate_kernel(
             if not last:
                 multiply(1, 1, *TAIL[n + 1])
             quant_h(1, 1, *piece)
-            stage_y(1, *piece, last)
+            stage_y(1, *piece, last, ("acc_y", "acc_e", "acc_e")[n])

@@ -143,14 +143,20 @@ def tile_list_codon_context_rate_kernel(
             )
 
         w2_bf = [held([P, PACK * P * PACK], BF16, "w2_bf%d" % b) for b in range(PASSES)]
-        w2_codes = [held([P, BANK], U32, "w2_codes%d" % b) for b in range(PASSES)]
+        w2_codes = [placed([P, BANK], U32, "w2_codes0", W3_AT), held([P, BANK], U32, "w2_codes1")]
         w2_plane = [held([P, BANK], U8, "w2_plane%d" % b) for b in range(PASSES)]
 
         def cast_w2(b):
-            nc.scalar.copy(
-                out=w2_bf[b][:].rearrange("p (t m i) -> p m i t", t=PACK, i=PACK),
-                in_=w2_raw[b][:].rearrange("p i (m t) -> p m i t", t=PACK),
-            )
+            if b == 0:
+                nc.scalar.copy(
+                    out=w2_bf[b][:].rearrange("p (t m i) -> p m i t", t=PACK, i=PACK),
+                    in_=w2_raw[b][:].rearrange("p i (m t) -> p m i t", t=PACK),
+                )
+            else:
+                dst = w2_bf[b][:].rearrange("p (t m i) -> p t m i", t=PACK, i=PACK)
+                src = w2_raw[b][:].rearrange("p i (m t) -> p t m i", t=PACK)
+                for t in range(PACK):
+                    nc.gpsimd.tensor_copy(out=dst[:, t], in_=src[:, t])
 
         def quant_w2(b):
             nc.vector.quantize_mx(out=w2_codes[b][:].bitcast(FP8X4), scales=w2_plane[b][:], in_=w2_bf[b][:])
@@ -160,10 +166,10 @@ def tile_list_codon_context_rate_kernel(
         w4_plane = held([P, PASSES * N], U8, "w4_plane")
 
         def cast_w4():
-            nc.scalar.copy(
-                out=w4_bf[:].rearrange("p (b c j i) -> p b c i j", b=PASSES, j=4, i=PACK),
-                in_=w4_raw[:].rearrange("p b i (c j) -> p b c i j", j=4),
-            )
+            dst = w4_bf[:].rearrange("p (b n i) -> p b n i", b=PASSES, i=PACK)
+            src = w4_raw[:].rearrange("p b i n -> p b n i")
+            for b in range(PASSES):
+                nc.gpsimd.tensor_copy(out=dst[:, b], in_=src[:, b])
 
         def quant_w4():
             nc.vector.quantize_mx(out=w4_codes[:].bitcast(FP8X4), scales=w4_plane[:], in_=w4_bf[:])
@@ -277,20 +283,23 @@ def tile_list_codon_context_rate_kernel(
         stage_e(0, 0)
         cast_w2(1)
         late_planes = placed([P, 3, BANK], U8, "late_planes", PLANE_AT - 1024)
-        late_codes = placed([P, 3, BANK], U32, "late_codes", PLANE_AT + 512)
-        for n, name in enumerate(ORDER):
-            late_words[name] = late_codes[:, n, :]
+        late_down = placed([P, BANK], U32, "late_down", PLANE_AT + 512)
+        late_words["down"] = late_down[:]
         gather_scales("down", 1)
         gather_words("down", 1)
+        gather_scales("up", 1)
+        gather_scales("own", 1)
         quant_w2(1)
+        late_pair = held([P, 2, BANK], U32, "late_pair", "w2_bf1")
+        late_words["up"] = late_pair[:, 0, :]
+        late_words["own"] = late_pair[:, 1, :]
         stage_d(1, 0)
         stage_e(0, 1)
         cast_w4()
         for name in ("up", "own"):
-            gather_scales(name, 1)
             gather_words(name, 1)
-        stage_e(1, 0)
         stage_d(1, 1)
+        stage_e(1, 0)
         multiply(0, 0, 0, BANK)
         quant_h(0, 0, 0, BANK)
         multiply(0, 1, 0, BANK)

@@ -155,8 +155,12 @@ def tile_list_codon_context_rate_kernel(
             else:
                 dst = w2_bf[b][:].rearrange("p (t m i) -> p t m i", t=PACK, i=PACK)
                 src = w2_raw[b][:].rearrange("p i (m t) -> p t m i", t=PACK)
-                for t in range(PACK):
+                for t in range(PACK // 2):
                     nc.gpsimd.tensor_copy(out=dst[:, t], in_=src[:, t])
+                nc.scalar.copy(
+                    out=dst[:, PACK // 2 :].rearrange("p t m i -> p m i t"),
+                    in_=src[:, PACK // 2 :].rearrange("p t m i -> p m i t"),
+                )
 
         def quant_w2(b):
             nc.vector.quantize_mx(out=w2_codes[b][:].bitcast(FP8X4), scales=w2_plane[b][:], in_=w2_bf[b][:])
@@ -241,8 +245,10 @@ def tile_list_codon_context_rate_kernel(
             codes = held([P, j1 - j0], U32, "h_codes%d%d_%d" % (half, b, j0))
             plane = held([P, j1 - j0], U8, "h_plane%d%d_%d" % (half, b, j0))
             nc.vector.quantize_mx(out=codes[:].bitcast(FP8X4), scales=plane[:], in_=h_bf[half, b, j0][:])
-            h_codes[half, b, j0] = codes
-            h_plane[half, b, j0] = plane
+            for a0, a1 in ((0, BANK),) + TAIL:
+                if j0 <= a0 and a1 <= j1:
+                    h_codes[half, b, a0, a1] = codes[:, a0 - j0 : a1 - j0]
+                    h_plane[half, b, a0, a1] = plane[:, a0 - j0 : a1 - j0]
 
         def stage_y(half, j0, j1, last, tag="acc_y"):
             width = j1 - j0
@@ -254,8 +260,8 @@ def tile_list_codon_context_rate_kernel(
                         out=acc[:, 0:width],
                         lhsT=w4_codes[:, cols].bitcast(FP8X4),
                         lhsT_scale=w4_plane[:, cols],
-                        rhs=h_codes[half, b, j0][:].bitcast(FP8X4),
-                        rhs_scale=h_plane[half, b, j0][:],
+                        rhs=h_codes[half, b, j0, j1].bitcast(FP8X4),
+                        rhs_scale=h_plane[half, b, j0, j1],
                         start=(b == 0),
                         stop=(b == PASSES - 1),
                     )
@@ -264,7 +270,8 @@ def tile_list_codon_context_rate_kernel(
                     nc.vector.tensor_scalar(res[:], acc[:, 0:width], b4_sb[:, c : c + 1], None, ALU.add)
                 else:
                     nc.scalar.activation(res[:], acc[:, 0:width], ACT.Identity, bias=b4_sb[:, c : c + 1])
-                nc.sync.dma_start(out=out[c * P : (c + 1) * P, half * BANK + j0 : half * BANK + j1], in_=res[:])
+                queue = nc.scalar if last and c == 0 else nc.sync
+                queue.dma_start(out=out[c * P : (c + 1) * P, half * BANK + j0 : half * BANK + j1], in_=res[:])
 
         for name in ORDER:
             gather_scales(name, 0)
@@ -307,11 +314,9 @@ def tile_list_codon_context_rate_kernel(
         quant_h(0, 1, 0, BANK)
         stage_e(1, 1, TAIL)
         stage_y(0, 0, BANK, False, "acc_d")
-        for j0, j1 in TAIL:
-            multiply(1, 0, j0, j1)
-        for j0, j1 in TAIL:
-            quant_h(1, 0, j0, j1)
+        multiply(1, 0, 0, BANK)
         multiply(1, 1, *TAIL[0])
+        quant_h(1, 0, 0, BANK)
         for n, piece in enumerate(TAIL):
             last = n == len(TAIL) - 1
             if not last:

@@ -19,15 +19,13 @@ ALU = mybir.AluOpType
 P = 128
 PACK = 4
 BANK = 512
-HALVES = S // BANK
 PASSES = H // (P * PACK)
-BANKS = {"acc_d": 2, "acc_e": 4, "acc_y": 2}
+M = H // PACK
 TAIL = ((0, 256), (256, 384), (384, 512))
-ORDER = ("down", "up", "own")
 
 
-def load_scale_rows(queue, plane, rows, first, quadrants=range(4)):
-    for q in quadrants:
+def load_scale_rows(queue, plane, rows, first):
+    for q in range(4):
         queue.dma_start(
             out=plane[32 * q + first : 32 * q + first + 4, :].bitcast(I32),
             in_=rows[4 * q : 4 * q + 4, :].bitcast(I32),
@@ -40,100 +38,91 @@ def tile_list_codon_context_rate_kernel(
     nc = tc.nc
     with ExitStack() as ctx:
         keep = ctx.enter_context(tc.tile_pool(name="keep", bufs=1))
-        early = ctx.enter_context(tc.tile_pool(name="early", bufs=1))
+        shared = ctx.enter_context(tc.tile_pool(name="shared", bufs=1))
         psum = ctx.enter_context(tc.psum_pool(name="psum", bufs=1))
 
-        def held(shape, dtype, name, tag=None):
-            return keep.tile(shape, dtype, name=name, tag=tag or name, align_bytes=64)
+        def held(shape, dtype, name):
+            return keep.tile(shape, dtype, name=name, align_bytes=64)
+
+        def placed(shape, dtype, name, at):
+            return shared.tile(shape, dtype, name=name, offset=at, align_bytes=64)
+
+        def bank(n):
+            return psum.tile([P, BANK], F32, name="bank%d" % n, tag="bank%d" % n)
 
         tab_plane = held([P, T], U8, "tab_plane")
         nc.vector.memset(tab_plane[:].bitcast(I32), 0)
-
-        TAB_AT, W2_AT, W4_AT, W1_AT, PLANE_AT, BIAS_AT, W3_AT, END_AT = 0, 8192, 24576, 32768, 35840, 42496, 42624, 46720
-
-        def placed(shape, dtype, name, at):
-            return early.tile(shape, dtype, name=name, offset=at, align_bytes=64)
-
-        w3_plane_raw = placed([P, H], U8, "w3_plane_raw", END_AT)
-        nc.vector.memset(w3_plane_raw[:].bitcast(I32), 0)
-        warm = placed([P, END_AT // 4], F32, "warm", 0)
-        nc.scalar.activation(warm[:, 0:1], w3_plane_raw[:, 0:4].bitcast(F32), ACT.Exp)
-        w1_plane_raw = placed([P, H], U8, "w1_plane_raw", PLANE_AT)
+        w3_plane_raw = held([P, H], U8, "w3_plane_raw")
+        nc.gpsimd.memset(w3_plane_raw[:].bitcast(I32), 0)
+        w1_plane_raw = held([P, H], U8, "w1_plane_raw")
         nc.vector.memset(w1_plane_raw[:].bitcast(I32), 0)
+        W1_AT, BF0_AT, BF1_AT = 0, 2048, 6144
 
         lists = {}
-        for name, src in (("down", offs3), ("up", offs2), ("own", offs)):
+
+        def load_list(name, src):
             lists[name] = keep.tile([P, S // 16], U16, name="list_" + name)
             nc.sync.dma_start(lists[name][:], src)
 
         w2_rows = w2.rearrange("(p i) c -> p i c", i=PACK)
-        tab = placed([P, T], I32, "tab", TAB_AT)
-        w3_raw = placed([P, H], I32, "w3_raw", W3_AT)
+        tab = held([P, T], I32, "tab")
+        w3_raw = held([P, H], I32, "w3_raw")
         w1_raw = placed([P, H // 2], I32, "w1_raw", W1_AT)
-        bias = placed([P, 24], F32, "bias", BIAS_AT)
-        b1_sb = bias[:, 0:8].rearrange("p (b t) -> p b t", t=PACK)
-        b3_sb = bias[:, 8:16].rearrange("p (b t) -> p b t", t=PACK)
-        b4_sb = bias[:, 16:18]
-        w2_raw = {}
+        b1_sb = held([P, PASSES, PACK], F32, "b1_sb")
+        b3_sb = held([P, PASSES, PACK], F32, "b3_sb")
+        b4_sb = held([P, N // P], F32, "b4_sb")
+        w2_raw = [held([P, PACK, BANK], F32, "w2_raw%d" % b) for b in range(PASSES)]
+        w4_raw = held([P, PASSES, PACK, N], F32, "w4_raw")
 
-        def load_w2(b):
-            w2_raw[b] = placed([P, PACK, BANK], F32, "w2_raw%d" % b, W2_AT + 8192 * b)
-            nc.sync.dma_start(out=w2_raw[b][:], in_=w2_rows[:, :, b * BANK : (b + 1) * BANK])
-
+        load_list("down", offs3)
+        load_list("up", offs2)
+        load_list("own", offs)
         load_scale_rows(nc.sync, tab_plane, tab_scales[0], 0)
         nc.sync.dma_start(out=tab[:], in_=tab_words[0].rearrange("p t i -> p (t i)").bitcast(I32))
-        load_w2(0)
         load_scale_rows(nc.sync, w3_plane_raw, w3_scales[0], 0)
         nc.sync.dma_start(out=w3_raw[:], in_=w3_words[0].rearrange("p c i -> p (c i)").bitcast(I32))
-        nc.sync.dma_start(out=b3_sb, in_=b3.rearrange("(b p t) -> p b t", p=P, t=PACK))
+        nc.sync.dma_start(out=w2_raw[0][:], in_=w2_rows[:, :, 0:BANK])
+        nc.sync.dma_start(out=b3_sb[:], in_=b3.rearrange("(b p t) -> p b t", p=P, t=PACK))
         nc.sync.dma_start(out=w1_raw[:], in_=w1_words[0].bitcast(I32))
         load_scale_rows(nc.sync, w1_plane_raw, w1_scales[0], 0)
-        nc.sync.dma_start(out=b1_sb, in_=b1.rearrange("(b p t) -> p b t", p=P, t=PACK))
-        load_w2(1)
-        w4_raw = placed([P, PASSES, PACK, N], F32, "w4_raw", W4_AT)
+        nc.sync.dma_start(out=w2_raw[1][:], in_=w2_rows[:, :, BANK : 2 * BANK])
+        nc.sync.dma_start(out=b1_sb[:], in_=b1.rearrange("(b p t) -> p b t", p=P, t=PACK))
         nc.sync.dma_start(
             out=w4_raw[:].rearrange("p b i n -> p b (i n)"),
             in_=w4.rearrange("(b p i) n -> p b (i n)", p=P, i=PACK),
         )
         with nc.allow_non_contiguous_dma(reason="one bias value a partition"):
-            nc.sync.dma_start(out=b4_sb, in_=b4.rearrange("(c p) -> p c", p=P))
+            nc.sync.dma_start(out=b4_sb[:], in_=b4.rearrange("(c p) -> p c", p=P))
 
-        late_words = {}
-        picked_words = {}
-        picked_plane = {}
+        w2_bf = [placed([P, PACK * P * PACK], BF16, "w2_bf%d" % b, at) for b, at in enumerate((BF0_AT, BF1_AT))]
+        late_at = {
+            ("words", "down"): W1_AT,
+            ("plane", "down"): BF0_AT,
+            ("plane", "up"): BF0_AT + 512,
+            ("plane", "own"): BF0_AT + 1024,
+            ("words", "up"): BF0_AT + 2048,
+            ("words", "own"): BF1_AT,
+        }
+        picked = {}
 
-        def gather_scales(name, half):
-            dst = late_planes[:, ORDER.index(name), :] if half else held([P, BANK], U8, "plane_%s%d" % (name, half))[:]
+        def gather(kind, name, half):
+            dtype = U32 if kind == "words" else U8
+            label = "%s_%s%d" % (kind, name, half)
+            dst = placed([P, BANK], dtype, label, late_at[kind, name]) if half else held([P, BANK], dtype, label)
+            window = tab[:].bitcast(U32) if kind == "words" else tab_plane[:]
             cols = lists[name][:, half * BANK // 16 : (half + 1) * BANK // 16]
-            nc.vector.tensor_copy(dst, tab_plane[:].indirect(cols))
-            picked_plane[name, half] = dst
+            nc.vector.tensor_copy(dst[:], window.indirect(cols))
+            picked[kind, name, half] = dst[:]
 
-        def gather_words(name, half):
-            if half:
-                dst = late_words[name]
-            elif name == "own":
-                dst = placed([P, BANK], U32, "words_own", END_AT - 1024)[:]
-            else:
-                dst = held([P, BANK], U32, "words_" + name)[:]
-            cols = lists[name][:, half * BANK // 16 : (half + 1) * BANK // 16]
-            nc.vector.tensor_copy(dst, tab[:].bitcast(U32).indirect(cols))
-            picked_words[name, half] = dst
-
-        M = H // PACK
         w3_plane = held([P, H], U8, "w3_plane")
+        w1_plane = held([P, H], U8, "w1_plane")
         w3_dealt = held([P, H], I32, "w3_dealt")
         w1_dealt = held([P, 2 * H], U8, "w1_dealt")
 
-        def deal_scales(dealt, raw):
-            nc.vector.tensor_copy(
-                out=dealt[:].rearrange("p (t c i) -> p c t i", t=PACK, i=16),
-                in_=raw[:].rearrange("p (c i t) -> p c t i", t=PACK, i=16),
-            )
-
-        def deal_w3():
-            nc.vector.tensor_copy(
-                out=w3_dealt[:].rearrange("p (t c i) -> p c t i", t=PACK, i=4),
-                in_=w3_raw[:].rearrange("p (c i t) -> p c t i", t=PACK, i=4),
+        def deal(dealt, raw):
+            nc.gpsimd.tensor_copy(
+                out=dealt[:].rearrange("p (t m) -> p t m", t=PACK),
+                in_=raw[:].rearrange("p (m t) -> p t m", t=PACK),
             )
 
         def deal_w1():
@@ -142,24 +131,18 @@ def tile_list_codon_context_rate_kernel(
                 in_=w1_raw[:].bitcast(U16).rearrange("p (c i t) -> p c t i", t=PACK, i=8),
             )
 
-        w2_bf = [held([P, PACK * P * PACK], BF16, "w2_bf%d" % b) for b in range(PASSES)]
-        w2_codes = [placed([P, BANK], U32, "w2_codes0", W3_AT), held([P, BANK], U32, "w2_codes1")]
+        w2_codes = [held([P, BANK], U32, "w2_codes%d" % b) for b in range(PASSES)]
         w2_plane = [held([P, BANK], U8, "w2_plane%d" % b) for b in range(PASSES)]
 
-        def cast_w2(b):
-            if b == 0:
+        def cast_w2(b, on_gpsimd):
+            dst = w2_bf[b][:].rearrange("p (t m i) -> p t m i", t=PACK, i=PACK)
+            src = w2_raw[b][:].rearrange("p i (m t) -> p t m i", t=PACK)
+            for t in range(on_gpsimd):
+                nc.gpsimd.tensor_copy(out=dst[:, t], in_=src[:, t])
+            if on_gpsimd < PACK:
                 nc.scalar.copy(
-                    out=w2_bf[b][:].rearrange("p (t m i) -> p m i t", t=PACK, i=PACK),
-                    in_=w2_raw[b][:].rearrange("p i (m t) -> p m i t", t=PACK),
-                )
-            else:
-                dst = w2_bf[b][:].rearrange("p (t m i) -> p t m i", t=PACK, i=PACK)
-                src = w2_raw[b][:].rearrange("p i (m t) -> p t m i", t=PACK)
-                for t in range(PACK // 2):
-                    nc.gpsimd.tensor_copy(out=dst[:, t], in_=src[:, t])
-                nc.scalar.copy(
-                    out=dst[:, PACK // 2 :].rearrange("p t m i -> p m i t"),
-                    in_=src[:, PACK // 2 :].rearrange("p t m i -> p m i t"),
+                    out=dst[:, on_gpsimd:].rearrange("p t m i -> p m i t"),
+                    in_=src[:, on_gpsimd:].rearrange("p t m i -> p m i t"),
                 )
 
         def quant_w2(b):
@@ -173,7 +156,8 @@ def tile_list_codon_context_rate_kernel(
             dst = w4_bf[:].rearrange("p (b n i) -> p b n i", b=PASSES, i=PACK)
             src = w4_raw[:].rearrange("p b i n -> p b n i")
             for b in range(PASSES):
-                nc.gpsimd.tensor_copy(out=dst[:, b], in_=src[:, b])
+                for c in range(0, N, P):
+                    nc.gpsimd.tensor_copy(out=dst[:, b, c : c + P], in_=src[:, b, c : c + P])
 
         def quant_w4():
             nc.vector.quantize_mx(out=w4_codes[:].bitcast(FP8X4), scales=w4_plane[:], in_=w4_bf[:])
@@ -188,13 +172,13 @@ def tile_list_codon_context_rate_kernel(
             dst = held([P, PACK, BANK], F32, "down%d%d" % (half, b))
             for t in range(PACK):
                 cols = slice(t * M + b * P, t * M + (b + 1) * P)
-                acc = psum.tile([P, BANK], F32, name="acc_d", tag="acc_d", bufs=2)
+                acc = bank(t)
                 nc.tensor.matmul_mx(
                     out=acc[:],
                     lhsT=w3_dealt[:, cols].bitcast(FP8X4),
                     lhsT_scale=w3_plane[:, cols],
-                    rhs=picked_words["down", half].bitcast(FP8X4),
-                    rhs_scale=picked_plane["down", half],
+                    rhs=picked["words", "down", half].bitcast(FP8X4),
+                    rhs_scale=picked["plane", "down", half],
                     start=True,
                     stop=True,
                 )
@@ -206,13 +190,13 @@ def tile_list_codon_context_rate_kernel(
             banks = []
             for t in range(PACK):
                 c0 = t * M + b * P
-                acc = psum.tile([P, BANK], F32, name="acc_e", tag="acc_e", bufs=4)
+                acc = bank(t)
                 nc.tensor.matmul_mx(
                     out=acc[:],
                     lhsT=w2_codes[b][:, t * P : (t + 1) * P].bitcast(FP8X4),
                     lhsT_scale=w2_plane[b][:, t * P : (t + 1) * P],
-                    rhs=picked_words["up", half].bitcast(FP8X4),
-                    rhs_scale=picked_plane["up", half],
+                    rhs=picked["words", "up", half].bitcast(FP8X4),
+                    rhs_scale=picked["plane", "up", half],
                     start=True,
                     stop=False,
                 )
@@ -220,8 +204,8 @@ def tile_list_codon_context_rate_kernel(
                     out=acc[:],
                     lhsT=w1_dealt[:, 2 * c0 : 2 * (c0 + P)].bitcast(FP4X4),
                     lhsT_scale=w1_plane[:, c0 : c0 + P],
-                    rhs=picked_words["own", half].bitcast(FP8X4),
-                    rhs_scale=picked_plane["own", half],
+                    rhs=picked["words", "own", half].bitcast(FP8X4),
+                    rhs_scale=picked["plane", "own", half],
                     start=False,
                     stop=True,
                 )
@@ -232,7 +216,9 @@ def tile_list_codon_context_rate_kernel(
             rate[half, b] = dst
 
         def multiply(half, b, j0, j1):
-            dst = held([P, (j1 - j0) * PACK], BF16, "h_bf%d%d_%d" % (half, b, j0))
+            label = "h_bf%d%d_%d" % (half, b, j0)
+            shape = [P, (j1 - j0) * PACK]
+            dst = placed(shape, BF16, label, BF1_AT + 2048) if (half, b) == (0, 0) else held(shape, BF16, label)
             nc.vector.tensor_tensor(
                 out=dst[:].rearrange("p (c i t) -> p c t i", i=2, t=PACK),
                 in0=rate[half, b][:, :, j0:j1].rearrange("p t (c i) -> p c t i", i=2),
@@ -250,10 +236,10 @@ def tile_list_codon_context_rate_kernel(
                     h_codes[half, b, a0, a1] = codes[:, a0 - j0 : a1 - j0]
                     h_plane[half, b, a0, a1] = plane[:, a0 - j0 : a1 - j0]
 
-        def stage_y(half, j0, j1, last, tag="acc_y"):
+        def stage_y(half, j0, j1, first_bank, on_vector):
             width = j1 - j0
             for c in range(N // P):
-                acc = psum.tile([P, BANK], F32, name="acc_y", tag=tag, bufs=BANKS[tag])
+                acc = bank(first_bank + c)
                 for b in range(PASSES):
                     cols = slice(b * N + c * P, b * N + (c + 1) * P)
                     nc.tensor.matmul_mx(
@@ -266,60 +252,51 @@ def tile_list_codon_context_rate_kernel(
                         stop=(b == PASSES - 1),
                     )
                 res = held([P, width], F32, "res%d%d_%d" % (half, c, j0))
-                if last and c == 1:
+                if c in on_vector:
                     nc.vector.tensor_scalar(res[:], acc[:, 0:width], b4_sb[:, c : c + 1], None, ALU.add)
+                    queue = nc.sync
                 else:
                     nc.scalar.activation(res[:], acc[:, 0:width], ACT.Identity, bias=b4_sb[:, c : c + 1])
-                queue = nc.scalar if last and c == 0 else nc.sync
+                    queue = nc.scalar if on_vector else nc.sync
                 queue.dma_start(out=out[c * P : (c + 1) * P, half * BANK + j0 : half * BANK + j1], in_=res[:])
 
-        for name in ORDER:
-            gather_scales(name, 0)
-        cast_w2(0)
-        gather_words("down", 0)
-        gather_words("up", 0)
-        deal_scales(w3_plane, w3_plane_raw)
-        deal_w3()
-        stage_d(0, 0)
-        gather_words("own", 0)
-        quant_w2(0)
+        for kind in ("plane", "words"):
+            for name in ("down", "up", "own"):
+                gather(kind, name, 0)
+        deal(w3_plane, w3_plane_raw)
+        deal(w3_dealt, w3_raw)
+        cast_w2(0, 2)
+        deal(w1_plane, w1_plane_raw)
         deal_w1()
-        w1_plane = placed([P, H], U8, "w1_plane", W1_AT)
-        deal_scales(w1_plane, w1_plane_raw)
+        gather("words", "down", 1)
+        quant_w2(0)
+        stage_d(0, 0)
         stage_d(0, 1)
         stage_e(0, 0)
-        cast_w2(1)
-        late_planes = placed([P, 3, BANK], U8, "late_planes", PLANE_AT - 1024)
-        late_down = placed([P, BANK], U32, "late_down", PLANE_AT + 512)
-        late_words["down"] = late_down[:]
-        gather_scales("down", 1)
-        gather_words("down", 1)
-        gather_scales("up", 1)
-        gather_scales("own", 1)
+        cast_w2(1, PACK)
+        for name in ("down", "up", "own"):
+            gather("plane", name, 1)
+        gather("words", "up", 1)
         quant_w2(1)
-        late_pair = held([P, 2, BANK], U32, "late_pair", "w2_bf1")
-        late_words["up"] = late_pair[:, 0, :]
-        late_words["own"] = late_pair[:, 1, :]
+        gather("words", "own", 1)
+        cast_w4()
         stage_d(1, 0)
         stage_e(0, 1)
-        cast_w4()
-        for name in ("up", "own"):
-            gather_words(name, 1)
-        stage_d(1, 1)
         stage_e(1, 0)
         multiply(0, 0, 0, BANK)
-        quant_h(0, 0, 0, BANK)
         multiply(0, 1, 0, BANK)
-        quant_w4()
+        quant_h(0, 0, 0, BANK)
         quant_h(0, 1, 0, BANK)
-        stage_e(1, 1, TAIL)
-        stage_y(0, 0, BANK, False, "acc_d")
+        stage_d(1, 1)
+        stage_e(1, 1)
         multiply(1, 0, 0, BANK)
-        multiply(1, 1, *TAIL[0])
+        quant_w4()
+        stage_y(0, 0, BANK, 4, ())
         quant_h(1, 0, 0, BANK)
+        multiply(1, 1, *TAIL[0])
         for n, piece in enumerate(TAIL):
             last = n == len(TAIL) - 1
             if not last:
                 multiply(1, 1, *TAIL[n + 1])
             quant_h(1, 1, *piece)
-            stage_y(1, *piece, last, ("acc_y", "acc_e", "acc_e")[n])
+            stage_y(1, *piece, (6, 4, 6)[n], (1,) if last else ())

@@ -22,6 +22,7 @@ BANK = 512
 PASSES = H // (P * PACK)
 M = H // PACK
 TAIL = ((0, 256), (256, 384), (384, 512))
+W3_ROW = 4
 
 
 def load_scale_rows(queue, plane, rows, first):
@@ -51,12 +52,10 @@ def tile_list_codon_context_rate_kernel(
             return psum.tile([P, BANK], F32, name="bank%d" % n, tag="bank%d" % n)
 
         tab_plane = held([P, T], U8, "tab_plane")
-        nc.vector.memset(tab_plane[:].bitcast(I32), 0)
-        w3_plane_raw = held([P, H], U8, "w3_plane_raw")
-        nc.gpsimd.memset(w3_plane_raw[:].bitcast(I32), 0)
-        w1_plane_raw = held([P, H], U8, "w1_plane_raw")
-        nc.vector.memset(w1_plane_raw[:].bitcast(I32), 0)
-        W1_AT, BF0_AT, BF1_AT = 0, 2048, 6144
+        nc.gpsimd.memset(tab_plane[:].bitcast(I32), 0)
+        w_plane_raw = held([P, H], U8, "w_plane_raw")
+        nc.vector.memset(w_plane_raw[:].bitcast(I32), 0)
+        W1_AT, BF1_AT, TAB_AT = 1536, 4608, 8704
 
         lists = {}
 
@@ -65,7 +64,7 @@ def tile_list_codon_context_rate_kernel(
             nc.sync.dma_start(lists[name][:], src)
 
         w2_rows = w2.rearrange("(p i) c -> p i c", i=PACK)
-        tab = held([P, T], I32, "tab")
+        tab = placed([P, T], I32, "tab", TAB_AT)
         w3_raw = held([P, H], I32, "w3_raw")
         w1_raw = placed([P, H // 2], I32, "w1_raw", W1_AT)
         b1_sb = held([P, PASSES, PACK], F32, "b1_sb")
@@ -78,13 +77,13 @@ def tile_list_codon_context_rate_kernel(
         load_list("up", offs2)
         load_list("own", offs)
         load_scale_rows(nc.sync, tab_plane, tab_scales[0], 0)
-        nc.sync.dma_start(out=tab[:], in_=tab_words[0].rearrange("p t i -> p (t i)").bitcast(I32))
-        load_scale_rows(nc.sync, w3_plane_raw, w3_scales[0], 0)
-        nc.sync.dma_start(out=w3_raw[:], in_=w3_words[0].rearrange("p c i -> p (c i)").bitcast(I32))
         nc.sync.dma_start(out=w2_raw[0][:], in_=w2_rows[:, :, 0:BANK])
+        load_scale_rows(nc.sync, w_plane_raw, w3_scales[0], W3_ROW)
+        nc.sync.dma_start(out=w3_raw[:], in_=w3_words[0].rearrange("p c i -> p (c i)").bitcast(I32))
+        nc.sync.dma_start(out=tab[:], in_=tab_words[0].rearrange("p t i -> p (t i)").bitcast(I32))
+        load_scale_rows(nc.sync, w_plane_raw, w1_scales[0], 0)
         nc.sync.dma_start(out=b3_sb[:], in_=b3.rearrange("(b p t) -> p b t", p=P, t=PACK))
         nc.sync.dma_start(out=w1_raw[:], in_=w1_words[0].bitcast(I32))
-        load_scale_rows(nc.sync, w1_plane_raw, w1_scales[0], 0)
         nc.sync.dma_start(out=w2_raw[1][:], in_=w2_rows[:, :, BANK : 2 * BANK])
         nc.sync.dma_start(out=b1_sb[:], in_=b1.rearrange("(b p t) -> p b t", p=P, t=PACK))
         nc.sync.dma_start(
@@ -94,28 +93,32 @@ def tile_list_codon_context_rate_kernel(
         with nc.allow_non_contiguous_dma(reason="one bias value a partition"):
             nc.sync.dma_start(out=b4_sb[:], in_=b4.rearrange("(c p) -> p c", p=P))
 
-        w2_bf = [placed([P, PACK * P * PACK], BF16, "w2_bf%d" % b, at) for b, at in enumerate((BF0_AT, BF1_AT))]
-        late_at = {
-            ("words", "down"): W1_AT,
-            ("plane", "down"): BF0_AT,
-            ("plane", "up"): BF0_AT + 512,
-            ("plane", "own"): BF0_AT + 1024,
-            ("words", "up"): BF0_AT + 2048,
-            ("words", "own"): BF1_AT,
+        w2_bf = [held([P, PACK * P * PACK], BF16, "w2_bf0"), placed([P, PACK * P * PACK], BF16, "w2_bf1", BF1_AT)]
+        words_at = {
+            ("down", 1): W1_AT - 1536,
+            ("up", 1): W1_AT + 1024,
+            ("own", 1): BF1_AT,
         }
         picked = {}
 
-        def gather(kind, name, half):
-            dtype = U32 if kind == "words" else U8
-            label = "%s_%s%d" % (kind, name, half)
-            dst = placed([P, BANK], dtype, label, late_at[kind, name]) if half else held([P, BANK], dtype, label)
-            window = tab[:].bitcast(U32) if kind == "words" else tab_plane[:]
-            cols = lists[name][:, half * BANK // 16 : (half + 1) * BANK // 16]
-            nc.vector.tensor_copy(dst[:], window.indirect(cols))
-            picked[kind, name, half] = dst[:]
+        def gather_plane(name, halves):
+            label = "plane_%s%d" % (name, halves[0])
+            shape = [P, len(halves) * BANK]
+            dst = placed(shape, U8, label, W1_AT + 512) if halves[0] else held(shape, U8, label)
+            cols = lists[name][:, halves[0] * BANK // 16 : (halves[-1] + 1) * BANK // 16]
+            nc.vector.tensor_copy(dst[:], tab_plane[:].indirect(cols))
+            for n, half in enumerate(halves):
+                picked["plane", name, half] = dst[:, n * BANK : (n + 1) * BANK]
 
-        w3_plane = held([P, H], U8, "w3_plane")
-        w1_plane = held([P, H], U8, "w1_plane")
+        def gather_words(name, half):
+            label = "words_%s%d" % (name, half)
+            at = words_at.get((name, half))
+            dst = held([P, BANK], U32, label) if at is None else placed([P, BANK], U32, label, at)
+            cols = lists[name][:, half * BANK // 16 : (half + 1) * BANK // 16]
+            nc.vector.tensor_copy(dst[:], tab[:].bitcast(U32).indirect(cols))
+            picked["words", name, half] = dst[:]
+
+        w_plane = held([P, H], U8, "w_plane")
         w3_dealt = held([P, H], I32, "w3_dealt")
         w1_dealt = held([P, 2 * H], U8, "w1_dealt")
 
@@ -149,15 +152,22 @@ def tile_list_codon_context_rate_kernel(
             nc.vector.quantize_mx(out=w2_codes[b][:].bitcast(FP8X4), scales=w2_plane[b][:], in_=w2_bf[b][:])
 
         w4_bf = held([P, PASSES * N * PACK], BF16, "w4_bf")
-        w4_codes = held([P, PASSES * N], U32, "w4_codes")
+        w4_codes = placed([P, PASSES * N], U32, "w4_codes", TAB_AT)
         w4_plane = held([P, PASSES * N], U8, "w4_plane")
 
-        def cast_w4():
-            dst = w4_bf[:].rearrange("p (b n i) -> p b n i", b=PASSES, i=PACK)
-            src = w4_raw[:].rearrange("p b i n -> p b n i")
-            for b in range(PASSES):
+        def cast_w4(b):
+            dst = w4_bf[:, b * N * PACK : (b + 1) * N * PACK]
+            if b == 0:
                 for c in range(0, N, P):
-                    nc.gpsimd.tensor_copy(out=dst[:, b, c : c + P], in_=src[:, b, c : c + P])
+                    nc.gpsimd.tensor_copy(
+                        out=dst[:, c * PACK : (c + P) * PACK].rearrange("p (n i) -> p n i", i=PACK),
+                        in_=w4_raw[:, b, :, c : c + P].rearrange("p i n -> p n i"),
+                    )
+            else:
+                nc.vector.tensor_copy(
+                    out=dst.rearrange("p (c n i) -> p c i n", i=PACK, n=4),
+                    in_=w4_raw[:, b].rearrange("p i (c n) -> p c i n", n=4),
+                )
 
         def quant_w4():
             nc.vector.quantize_mx(out=w4_codes[:].bitcast(FP8X4), scales=w4_plane[:], in_=w4_bf[:])
@@ -176,7 +186,7 @@ def tile_list_codon_context_rate_kernel(
                 nc.tensor.matmul_mx(
                     out=acc[:],
                     lhsT=w3_dealt[:, cols].bitcast(FP8X4),
-                    lhsT_scale=w3_plane[:, cols],
+                    lhsT_scale=w_plane[W3_ROW:P, cols],
                     rhs=picked["words", "down", half].bitcast(FP8X4),
                     rhs_scale=picked["plane", "down", half],
                     start=True,
@@ -203,7 +213,7 @@ def tile_list_codon_context_rate_kernel(
                 nc.tensor.matmul_mx(
                     out=acc[:],
                     lhsT=w1_dealt[:, 2 * c0 : 2 * (c0 + P)].bitcast(FP4X4),
-                    lhsT_scale=w1_plane[:, c0 : c0 + P],
+                    lhsT_scale=w_plane[:, c0 : c0 + P],
                     rhs=picked["words", "own", half].bitcast(FP8X4),
                     rhs_scale=picked["plane", "own", half],
                     start=False,
@@ -218,7 +228,7 @@ def tile_list_codon_context_rate_kernel(
         def multiply(half, b, j0, j1):
             label = "h_bf%d%d_%d" % (half, b, j0)
             shape = [P, (j1 - j0) * PACK]
-            dst = placed(shape, BF16, label, BF1_AT + 2048) if (half, b) == (0, 0) else held(shape, BF16, label)
+            dst = held(shape, BF16, label) if half else placed(shape, BF16, label, TAB_AT + 4096 * b)
             nc.vector.tensor_tensor(
                 out=dst[:].rearrange("p (c i t) -> p c t i", i=2, t=PACK),
                 in0=rate[half, b][:, :, j0:j1].rearrange("p t (c i) -> p c t i", i=2),
@@ -260,37 +270,39 @@ def tile_list_codon_context_rate_kernel(
                     queue = nc.scalar if on_vector else nc.sync
                 queue.dma_start(out=out[c * P : (c + 1) * P, half * BANK + j0 : half * BANK + j1], in_=res[:])
 
-        for kind in ("plane", "words"):
-            for name in ("down", "up", "own"):
-                gather(kind, name, 0)
-        deal(w3_plane, w3_plane_raw)
+        gather_plane("down", (0, 1))
+        gather_plane("up", (0, 1))
+        gather_plane("own", (0,))
+        cast_w2(0, 0)
         deal(w3_dealt, w3_raw)
-        cast_w2(0, 2)
-        deal(w1_plane, w1_plane_raw)
-        deal_w1()
-        gather("words", "down", 1)
+        deal(w_plane, w_plane_raw)
         quant_w2(0)
+        gather_words("down", 0)
         stage_d(0, 0)
         stage_d(0, 1)
-        stage_e(0, 0)
         cast_w2(1, PACK)
-        for name in ("down", "up", "own"):
-            gather("plane", name, 1)
-        gather("words", "up", 1)
+        gather_words("up", 0)
+        gather_words("own", 0)
+        deal_w1()
+        gather_words("down", 1)
+        gather_plane("own", (1,))
+        gather_words("up", 1)
         quant_w2(1)
-        gather("words", "own", 1)
-        cast_w4()
+        stage_e(0, 0)
         stage_d(1, 0)
         stage_e(0, 1)
+        gather_words("own", 1)
+        cast_w4(0)
         stage_e(1, 0)
         multiply(0, 0, 0, BANK)
-        multiply(0, 1, 0, BANK)
+        cast_w4(1)
         quant_h(0, 0, 0, BANK)
+        multiply(0, 1, 0, BANK)
+        quant_w4()
         quant_h(0, 1, 0, BANK)
         stage_d(1, 1)
-        stage_e(1, 1)
+        stage_e(1, 1, ((0, BANK // 2), (BANK // 2, BANK)))
         multiply(1, 0, 0, BANK)
-        quant_w4()
         stage_y(0, 0, BANK, 4, ())
         quant_h(1, 0, 0, BANK)
         multiply(1, 1, *TAIL[0])

@@ -53,9 +53,11 @@ def tile_list_codon_context_rate_kernel(
 
         tab_plane = held([P, T], U8, "tab_plane")
         nc.gpsimd.memset(tab_plane[:].bitcast(I32), 0)
-        w_plane_raw = held([P, H], U8, "w_plane_raw")
-        nc.vector.memset(w_plane_raw[:].bitcast(I32), 0)
-        W1_AT, BF1_AT, TAB_AT = 1536, 4608, 8704
+        RAW_AT, W4_AT, LAST_AT, W4BF_AT = 1536, 12288, 24576, 32768
+        raw = placed([P, 3 * H], U8, "raw", RAW_AT)
+        w1_raw = raw[:, 0 : 2 * H]
+        w_plane_raw = raw[:, 2 * H : 3 * H]
+        nc.vector.memset(w_plane_raw.bitcast(I32), 0)
 
         lists = {}
 
@@ -64,147 +66,119 @@ def tile_list_codon_context_rate_kernel(
             nc.sync.dma_start(lists[name][:], src)
 
         w2_rows = w2.rearrange("(p i) c -> p i c", i=PACK)
-        tab = placed([P, T], I32, "tab", TAB_AT)
+        tab = held([P, T], I32, "tab")
         w3_raw = held([P, H], I32, "w3_raw")
-        w1_raw = placed([P, H // 2], I32, "w1_raw", W1_AT)
         b1_sb = held([P, PASSES, PACK], F32, "b1_sb")
         b3_sb = held([P, PASSES, PACK], F32, "b3_sb")
         b4_sb = held([P, N // P], F32, "b4_sb")
         w2_raw = [held([P, PACK, BANK], F32, "w2_raw%d" % b) for b in range(PASSES)]
-        w4_raw = held([P, PASSES, PACK, N], F32, "w4_raw")
+        w4_raw = placed([P, PASSES, PACK, N], F32, "w4_raw", W4_AT)
 
         load_list("down", offs3)
         load_list("up", offs2)
         load_list("own", offs)
         load_scale_rows(nc.sync, tab_plane, tab_scales[0], 0)
-        nc.sync.dma_start(out=w2_raw[0][:], in_=w2_rows[:, :, 0:BANK])
-        load_scale_rows(nc.sync, w_plane_raw, w3_scales[0], W3_ROW)
-        nc.sync.dma_start(out=w3_raw[:], in_=w3_words[0].rearrange("p c i -> p (c i)").bitcast(I32))
-        nc.sync.dma_start(out=tab[:], in_=tab_words[0].rearrange("p t i -> p (t i)").bitcast(I32))
+        for b in range(PASSES):
+            nc.sync.dma_start(out=w2_raw[b][:], in_=w2_rows[:, :, b * BANK : (b + 1) * BANK])
         load_scale_rows(nc.sync, w_plane_raw, w1_scales[0], 0)
-        nc.sync.dma_start(out=b3_sb[:], in_=b3.rearrange("(b p t) -> p b t", p=P, t=PACK))
-        nc.sync.dma_start(out=w1_raw[:], in_=w1_words[0].bitcast(I32))
-        nc.sync.dma_start(out=w2_raw[1][:], in_=w2_rows[:, :, BANK : 2 * BANK])
+        nc.sync.dma_start(out=tab[:], in_=tab_words[0].rearrange("p t i -> p (t i)").bitcast(I32))
+        nc.sync.dma_start(out=w1_raw.bitcast(I32), in_=w1_words[0].bitcast(I32))
+        load_scale_rows(nc.sync, w_plane_raw, w3_scales[0], W3_ROW)
         nc.sync.dma_start(out=b1_sb[:], in_=b1.rearrange("(b p t) -> p b t", p=P, t=PACK))
         nc.sync.dma_start(
             out=w4_raw[:].rearrange("p b i n -> p b (i n)"),
             in_=w4.rearrange("(b p i) n -> p b (i n)", p=P, i=PACK),
         )
+        nc.sync.dma_start(out=w3_raw[:], in_=w3_words[0].rearrange("p c i -> p (c i)").bitcast(I32))
+        nc.sync.dma_start(out=b3_sb[:], in_=b3.rearrange("(b p t) -> p b t", p=P, t=PACK))
         with nc.allow_non_contiguous_dma(reason="one bias value a partition"):
             nc.sync.dma_start(out=b4_sb[:], in_=b4.rearrange("(c p) -> p c", p=P))
 
-        w2_bf = [held([P, PACK * P * PACK], BF16, "w2_bf0"), placed([P, PACK * P * PACK], BF16, "w2_bf1", BF1_AT)]
-        words_at = {
-            ("down", 1): W1_AT - 1536,
-            ("up", 1): W1_AT + 1024,
-            ("own", 1): BF1_AT,
-        }
+        words_at = {("up", 1): RAW_AT - 1536, ("own", 1): RAW_AT + 512, ("down", 0): RAW_AT + 2560}
         picked = {}
 
-        def gather_plane(name, halves):
-            label = "plane_%s%d" % (name, halves[0])
+        def gather(kind, name, halves):
+            label = "%s_%s%d" % (kind, name, halves[0])
             shape = [P, len(halves) * BANK]
-            dst = placed(shape, U8, label, W1_AT + 512) if halves[0] else held(shape, U8, label)
+            dtype = U32 if kind == "words" else U8
+            at = words_at.get((name, halves[0])) if kind == "words" else None
+            dst = held(shape, dtype, label) if at is None else placed(shape, dtype, label, at)
+            window = tab[:].bitcast(U32) if kind == "words" else tab_plane[:]
             cols = lists[name][:, halves[0] * BANK // 16 : (halves[-1] + 1) * BANK // 16]
-            nc.vector.tensor_copy(dst[:], tab_plane[:].indirect(cols))
+            nc.vector.tensor_copy(dst[:], window.indirect(cols))
             for n, half in enumerate(halves):
-                picked["plane", name, half] = dst[:, n * BANK : (n + 1) * BANK]
-
-        def gather_words(name, half):
-            label = "words_%s%d" % (name, half)
-            at = words_at.get((name, half))
-            dst = held([P, BANK], U32, label) if at is None else placed([P, BANK], U32, label, at)
-            cols = lists[name][:, half * BANK // 16 : (half + 1) * BANK // 16]
-            nc.vector.tensor_copy(dst[:], tab[:].bitcast(U32).indirect(cols))
-            picked["words", name, half] = dst[:]
+                picked[kind, name, half] = dst[:, n * BANK : (n + 1) * BANK]
 
         w_plane = held([P, H], U8, "w_plane")
         w3_dealt = held([P, H], I32, "w3_dealt")
         w1_dealt = held([P, 2 * H], U8, "w1_dealt")
 
-        def deal(dealt, raw):
-            nc.gpsimd.tensor_copy(
-                out=dealt[:].rearrange("p (t m) -> p t m", t=PACK),
-                in_=raw[:].rearrange("p (m t) -> p t m", t=PACK),
+        def deal_plane():
+            nc.vector.tensor_copy(
+                out=w_plane[:].rearrange("p (t c i) -> p c t i", t=PACK, i=16),
+                in_=w_plane_raw.rearrange("p (c i t) -> p c t i", t=PACK, i=16),
+            )
+
+        def deal_w3():
+            nc.vector.tensor_copy(
+                out=w3_dealt[:].rearrange("p (t c i) -> p c t i", t=PACK, i=4),
+                in_=w3_raw[:].rearrange("p (c i t) -> p c t i", t=PACK, i=4),
             )
 
         def deal_w1():
             nc.vector.tensor_copy(
                 out=w1_dealt[:].bitcast(U16).rearrange("p (t c i) -> p c t i", t=PACK, i=8),
-                in_=w1_raw[:].bitcast(U16).rearrange("p (c i t) -> p c t i", t=PACK, i=8),
+                in_=w1_raw.bitcast(U16).rearrange("p (c i t) -> p c t i", t=PACK, i=8),
             )
 
-        w2_codes = [held([P, BANK], U32, "w2_codes%d" % b) for b in range(PASSES)]
-        w2_plane = [held([P, BANK], U8, "w2_plane%d" % b) for b in range(PASSES)]
+        w2_bf = held([P, H * PACK], BF16, "w2_bf")
+        w2_codes = held([P, H], U32, "w2_codes")
+        w2_plane = held([P, H], U8, "w2_plane")
 
-        def cast_w2(b, on_gpsimd):
-            dst = w2_bf[b][:].rearrange("p (t m i) -> p t m i", t=PACK, i=PACK)
-            src = w2_raw[b][:].rearrange("p i (m t) -> p t m i", t=PACK)
-            for t in range(on_gpsimd):
-                nc.gpsimd.tensor_copy(out=dst[:, t], in_=src[:, t])
-            if on_gpsimd < PACK:
-                nc.scalar.copy(
-                    out=dst[:, on_gpsimd:].rearrange("p t m i -> p m i t"),
-                    in_=src[:, on_gpsimd:].rearrange("p t m i -> p m i t"),
-                )
+        def cast_w2(b):
+            nc.scalar.copy(
+                out=w2_bf[:, b * BANK * PACK : (b + 1) * BANK * PACK].rearrange("p (t m i) -> p m i t", t=PACK, i=PACK),
+                in_=w2_raw[b][:].rearrange("p i (m t) -> p m i t", t=PACK),
+            )
 
-        def quant_w2(b):
-            nc.vector.quantize_mx(out=w2_codes[b][:].bitcast(FP8X4), scales=w2_plane[b][:], in_=w2_bf[b][:])
+        def quant_w2():
+            nc.vector.quantize_mx(out=w2_codes[:].bitcast(FP8X4), scales=w2_plane[:], in_=w2_bf[:])
 
-        w4_bf = held([P, PASSES * N * PACK], BF16, "w4_bf")
-        w4_codes = placed([P, PASSES * N], U32, "w4_codes", TAB_AT)
+        w4_bf = placed([P, PASSES * N * PACK], BF16, "w4_bf", W4BF_AT)
+        w4_codes = held([P, PASSES * N], U32, "w4_codes")
         w4_plane = held([P, PASSES * N], U8, "w4_plane")
 
-        def cast_w4(b):
-            dst = w4_bf[:, b * N * PACK : (b + 1) * N * PACK]
-            if b == 0:
-                for c in range(0, N, P):
-                    nc.gpsimd.tensor_copy(
-                        out=dst[:, c * PACK : (c + P) * PACK].rearrange("p (n i) -> p n i", i=PACK),
-                        in_=w4_raw[:, b, :, c : c + P].rearrange("p i n -> p n i"),
-                    )
-            else:
-                nc.vector.tensor_copy(
-                    out=dst.rearrange("p (c n i) -> p c i n", i=PACK, n=4),
-                    in_=w4_raw[:, b].rearrange("p i (c n) -> p c i n", n=4),
-                )
+        def cast_w4():
+            nc.scalar.copy(
+                out=w4_bf[:].rearrange("p (b c n i) -> p b c i n", b=PASSES, i=PACK, n=4),
+                in_=w4_raw[:].rearrange("p b i (c n) -> p b c i n", n=4),
+            )
 
         def quant_w4():
             nc.vector.quantize_mx(out=w4_codes[:].bitcast(FP8X4), scales=w4_plane[:], in_=w4_bf[:])
 
-        down = {}
         rate = {}
+        rate_at = {(0, 0): W4_AT - 4096, (0, 1): W4_AT + 4096, (1, 0): LAST_AT}
+        h_slices = {}
         h_codes = {}
         h_plane = {}
         h_bf = {}
 
-        def stage_d(half, b):
-            dst = held([P, PACK, BANK], F32, "down%d%d" % (half, b))
-            for t in range(PACK):
-                cols = slice(t * M + b * P, t * M + (b + 1) * P)
-                acc = bank(t)
-                nc.tensor.matmul_mx(
-                    out=acc[:],
-                    lhsT=w3_dealt[:, cols].bitcast(FP8X4),
-                    lhsT_scale=w_plane[W3_ROW:P, cols],
-                    rhs=picked["words", "down", half].bitcast(FP8X4),
-                    rhs_scale=picked["plane", "down", half],
-                    start=True,
-                    stop=True,
-                )
-                nc.scalar.activation(dst[:, t, :], acc[:], ACT.Identity, bias=b3_sb[:, b, t : t + 1])
-            down[half, b] = dst
-
-        def stage_e(half, b, pieces=((0, BANK),)):
-            dst = held([P, PACK, BANK], F32, "rate%d%d" % (half, b))
-            banks = []
-            for t in range(PACK):
+        def stage_e(half, b, slices=range(PACK)):
+            if (half, b) not in rate:
+                label = "rate%d%d" % (half, b)
+                shape = [P, PACK, BANK]
+                at = rate_at.get((half, b))
+                rate[half, b] = held(shape, F32, label) if at is None else placed(shape, F32, label, at)
+            dst = rate[half, b]
+            for t in slices:
                 c0 = t * M + b * P
-                acc = bank(t)
+                c2 = b * BANK + t * P
+                acc = bank(PACK * b + t)
                 nc.tensor.matmul_mx(
                     out=acc[:],
-                    lhsT=w2_codes[b][:, t * P : (t + 1) * P].bitcast(FP8X4),
-                    lhsT_scale=w2_plane[b][:, t * P : (t + 1) * P],
+                    lhsT=w2_codes[:, c2 : c2 + P].bitcast(FP8X4),
+                    lhsT_scale=w2_plane[:, c2 : c2 + P],
                     rhs=picked["words", "up", half].bitcast(FP8X4),
                     rhs_scale=picked["plane", "up", half],
                     start=True,
@@ -219,26 +193,70 @@ def tile_list_codon_context_rate_kernel(
                     start=False,
                     stop=True,
                 )
-                banks.append(acc)
-            for j0, j1 in pieces:
-                for t in range(PACK):
-                    nc.scalar.activation(dst[:, t, j0:j1], banks[t][:, j0:j1], ACT.Exp, bias=b1_sb[:, b, t : t + 1])
-            rate[half, b] = dst
+                nc.scalar.activation(dst[:, t, :], acc[:], ACT.Exp, bias=b1_sb[:, b, t : t + 1])
 
-        def multiply(half, b, j0, j1):
-            label = "h_bf%d%d_%d" % (half, b, j0)
-            shape = [P, (j1 - j0) * PACK]
-            dst = held(shape, BF16, label) if half else placed(shape, BF16, label, TAB_AT + 4096 * b)
+        def product_d(half, b, t, acc):
+            cols = slice(t * M + b * P, t * M + (b + 1) * P)
+            nc.tensor.matmul_mx(
+                out=acc[:],
+                lhsT=w3_dealt[:, cols].bitcast(FP8X4),
+                lhsT_scale=w_plane[W3_ROW:P, cols],
+                rhs=picked["words", "down", half].bitcast(FP8X4),
+                rhs_scale=picked["plane", "down", half],
+                start=True,
+                stop=True,
+            )
+
+        def stage_d(half, b, slices=range(PACK)):
+            if (half, b) not in h_slices:
+                label = "h_slices%d%d" % (half, b)
+                shape = [P, PACK, BANK]
+                first = (half, b) == (0, 0)
+                h_slices[half, b] = placed(shape, BF16, label, W4BF_AT) if first else held(shape, BF16, label)
+            dst = h_slices[half, b]
+            for t in slices:
+                acc = bank(PACK * (1 - b) + t)
+                product_d(half, b, t, acc)
+                nc.vector.scalar_tensor_tensor(
+                    dst[:, t, :], acc[:], b3_sb[:, b, t : t + 1], rate[half, b][:, t, :], ALU.add, ALU.mult
+                )
+
+        last_down = held([P, PACK, BANK], F32, "last_down")
+
+        def stage_last_d(slices):
+            for t in slices:
+                acc = bank(t)
+                product_d(1, 1, t, acc)
+                nc.scalar.activation(last_down[:, t, :], acc[:], ACT.Identity, bias=b3_sb[:, 1, t : t + 1])
+
+        def multiply_last(j0, j1):
+            dst = held([P, (j1 - j0) * PACK], BF16, "h_bf11_%d" % j0)
             nc.vector.tensor_tensor(
                 out=dst[:].rearrange("p (c i t) -> p c t i", i=2, t=PACK),
-                in0=rate[half, b][:, :, j0:j1].rearrange("p t (c i) -> p c t i", i=2),
-                in1=down[half, b][:, :, j0:j1].rearrange("p t (c i) -> p c t i", i=2),
+                in0=rate[1, 1][:, :, j0:j1].rearrange("p t (c i) -> p c t i", i=2),
+                in1=last_down[:, :, j0:j1].rearrange("p t (c i) -> p c t i", i=2),
                 op=ALU.mult,
             )
+            h_bf[1, 1, j0] = dst
+
+        def weave(half, b, j0, j1):
+            dst = held([P, (j1 - j0) * PACK], BF16, "h_bf%d%d_%d" % (half, b, j0))
+            src = h_slices[half, b][:, :, j0:j1]
+            if half == 0:
+                nc.gpsimd.tensor_copy(
+                    out=dst[:].rearrange("p (c t) -> p c t", t=PACK), in_=src.rearrange("p t c -> p c t")
+                )
+            else:
+                nc.scalar.copy(
+                    out=dst[:].rearrange("p (c i t) -> p c t i", i=4, t=PACK),
+                    in_=src.rearrange("p t (c i) -> p c t i", i=4),
+                )
             h_bf[half, b, j0] = dst
 
         def quant_h(half, b, j0, j1):
-            codes = held([P, j1 - j0], U32, "h_codes%d%d_%d" % (half, b, j0))
+            codes = placed(
+                [P, j1 - j0], U32, "h_codes%d%d_%d" % (half, b, j0), LAST_AT + 4 * ((half * PASSES + b) * BANK + j0)
+            )
             plane = held([P, j1 - j0], U8, "h_plane%d%d_%d" % (half, b, j0))
             nc.vector.quantize_mx(out=codes[:].bitcast(FP8X4), scales=plane[:], in_=h_bf[half, b, j0][:])
             for a0, a1 in ((0, BANK),) + TAIL:
@@ -270,45 +288,43 @@ def tile_list_codon_context_rate_kernel(
                     queue = nc.scalar if on_vector else nc.sync
                 queue.dma_start(out=out[c * P : (c + 1) * P, half * BANK + j0 : half * BANK + j1], in_=res[:])
 
-        gather_plane("down", (0, 1))
-        gather_plane("up", (0, 1))
-        gather_plane("own", (0,))
-        cast_w2(0, 0)
-        deal(w3_dealt, w3_raw)
-        deal(w_plane, w_plane_raw)
-        quant_w2(0)
-        gather_words("down", 0)
-        stage_d(0, 0)
-        stage_d(0, 1)
-        cast_w2(1, PACK)
-        gather_words("up", 0)
-        gather_words("own", 0)
+        for name in ("up", "own", "down"):
+            gather("plane", name, (0, 1))
+        cast_w2(0)
+        cast_w2(1)
+        quant_w2()
+        gather("words", "up", (0,))
+        gather("words", "own", (0,))
         deal_w1()
-        gather_words("down", 1)
-        gather_plane("own", (1,))
-        gather_words("up", 1)
-        quant_w2(1)
+        deal_plane()
+        cast_w4()
         stage_e(0, 0)
-        stage_d(1, 0)
         stage_e(0, 1)
-        gather_words("own", 1)
-        cast_w4(0)
-        stage_e(1, 0)
-        multiply(0, 0, 0, BANK)
-        cast_w4(1)
-        quant_h(0, 0, 0, BANK)
-        multiply(0, 1, 0, BANK)
+        gather("words", "up", (1,))
+        gather("words", "own", (1,))
+        gather("words", "down", (0, 1))
+        deal_w3()
         quant_w4()
+        stage_e(1, 0)
+        stage_d(0, 0)
+        weave(0, 0, 0, BANK)
+        for t in range(PACK):
+            stage_d(0, 1, (t,))
+            stage_e(1, 1, (t,))
+        weave(0, 1, 0, BANK)
+        for t in range(PACK):
+            stage_last_d((t,))
+            stage_d(1, 0, (t,))
+        weave(1, 0, 0, BANK)
+        quant_h(0, 0, 0, BANK)
         quant_h(0, 1, 0, BANK)
-        stage_d(1, 1)
-        stage_e(1, 1, ((0, BANK // 2), (BANK // 2, BANK)))
-        multiply(1, 0, 0, BANK)
-        stage_y(0, 0, BANK, 4, ())
+        stage_y(0, 0, BANK, 0, ())
+        multiply_last(*TAIL[0])
+        multiply_last(*TAIL[1])
         quant_h(1, 0, 0, BANK)
-        multiply(1, 1, *TAIL[0])
+        quant_h(1, 1, *TAIL[0])
+        multiply_last(*TAIL[2])
+        quant_h(1, 1, *TAIL[1])
+        quant_h(1, 1, *TAIL[2])
         for n, piece in enumerate(TAIL):
-            last = n == len(TAIL) - 1
-            if not last:
-                multiply(1, 1, *TAIL[n + 1])
-            quant_h(1, 1, *piece)
-            stage_y(1, *piece, (6, 4, 6)[n], (1,) if last else ())
+            stage_y(1, *piece, 2 + 2 * n, (1,) if n == len(TAIL) - 1 else ())

@@ -78,10 +78,10 @@ def tile_list_codon_context_rate_kernel(
         load_list("up", offs2)
         load_list("own", offs)
         load_scale_rows(nc.sync, tab_plane, tab_scales[0], 0)
-        for b in range(PASSES):
-            nc.sync.dma_start(out=w2_raw[b][:], in_=w2_rows[:, :, b * BANK : (b + 1) * BANK])
-        load_scale_rows(nc.sync, w_plane_raw, w1_scales[0], 0)
+        nc.sync.dma_start(out=w2_raw[0][:], in_=w2_rows[:, :, 0:BANK])
         nc.sync.dma_start(out=tab[:], in_=tab_words[0].rearrange("p t i -> p (t i)").bitcast(I32))
+        load_scale_rows(nc.sync, w_plane_raw, w1_scales[0], 0)
+        nc.sync.dma_start(out=w2_raw[1][:], in_=w2_rows[:, :, BANK : 2 * BANK])
         nc.sync.dma_start(out=w1_raw.bitcast(I32), in_=w1_words[0].bitcast(I32))
         load_scale_rows(nc.sync, w_plane_raw, w3_scales[0], W3_ROW)
         nc.sync.dma_start(out=b1_sb[:], in_=b1.rearrange("(b p t) -> p b t", p=P, t=PACK))
@@ -292,10 +292,10 @@ def tile_list_codon_context_rate_kernel(
             gather("plane", name, (0, 1))
         cast_w2(0)
         cast_w2(1)
-        quant_w2()
         gather("words", "up", (0,))
         gather("words", "own", (0,))
         deal_w1()
+        quant_w2()
         deal_plane()
         cast_w4()
         stage_e(0, 0)

@@ -21,13 +21,23 @@ PACK = 4
 BANK = 512
 PASSES = H // (P * PACK)
 M = H // PACK
+LAST = (1, 1)
 TAIL = ((0, 256), (256, 384), (384, 512))
 W3_ROW = 4
 
+WORDS = 4 * BANK
+TRIO_AT = 0
+RAW_AT = TRIO_AT + 3 * WORDS // 4
+BF1_AT = TRIO_AT + 3 * WORDS
+BF0_AT = BF1_AT + 2 * WORDS
+W3_AT = BF0_AT + 2 * WORDS
+TAB_AT = W3_AT + 2 * WORDS
+RATE_AT = TAB_AT + 4 * WORDS
 
-def load_scale_rows(queue, plane, rows, first):
+
+def load_scale_rows(nc, plane, rows, first):
     for q in range(4):
-        queue.dma_start(
+        nc.sync.dma_start(
             out=plane[32 * q + first : 32 * q + first + 4, :].bitcast(I32),
             in_=rows[4 * q : 4 * q + 4, :].bitcast(I32),
         )
@@ -53,61 +63,61 @@ def tile_list_codon_context_rate_kernel(
 
         tab_plane = held([P, T], U8, "tab_plane")
         nc.gpsimd.memset(tab_plane[:].bitcast(I32), 0)
-        RAW_AT, W4_AT, LAST_AT, W4BF_AT = 1536, 12288, 24576, 32768
         raw = placed([P, 3 * H], U8, "raw", RAW_AT)
         w1_raw = raw[:, 0 : 2 * H]
         w_plane_raw = raw[:, 2 * H : 3 * H]
         nc.vector.memset(w_plane_raw.bitcast(I32), 0)
 
-        lists = {}
-
-        def load_list(name, src):
-            lists[name] = keep.tile([P, S // 16], U16, name="list_" + name)
-            nc.sync.dma_start(lists[name][:], src)
-
+        lists = {name: keep.tile([P, S // 16], U16, name="list_" + name) for name in ("down", "up", "own")}
         w2_rows = w2.rearrange("(p i) c -> p i c", i=PACK)
-        tab = held([P, T], I32, "tab")
-        w3_raw = held([P, H], I32, "w3_raw")
+        tab = placed([P, T], I32, "tab", TAB_AT)
+        w3_raw = placed([P, H], I32, "w3_raw", W3_AT)
         b1_sb = held([P, PASSES, PACK], F32, "b1_sb")
         b3_sb = held([P, PASSES, PACK], F32, "b3_sb")
         b4_sb = held([P, N // P], F32, "b4_sb")
         w2_raw = [held([P, PACK, BANK], F32, "w2_raw%d" % b) for b in range(PASSES)]
-        w4_raw = placed([P, PASSES, PACK, N], F32, "w4_raw", W4_AT)
+        w4_raw = held([P, PASSES, PACK, N], F32, "w4_raw")
 
-        load_list("down", offs3)
-        load_list("up", offs2)
-        load_list("own", offs)
-        load_scale_rows(nc.sync, tab_plane, tab_scales[0], 0)
+        for name, src in (("down", offs3), ("up", offs2), ("own", offs)):
+            nc.sync.dma_start(lists[name][:], src)
+        load_scale_rows(nc, tab_plane, tab_scales[0], 0)
         nc.sync.dma_start(out=w2_raw[0][:], in_=w2_rows[:, :, 0:BANK])
         nc.sync.dma_start(out=tab[:], in_=tab_words[0].rearrange("p t i -> p (t i)").bitcast(I32))
-        load_scale_rows(nc.sync, w_plane_raw, w1_scales[0], 0)
+        load_scale_rows(nc, w_plane_raw, w1_scales[0], 0)
         nc.sync.dma_start(out=w2_raw[1][:], in_=w2_rows[:, :, BANK : 2 * BANK])
         nc.sync.dma_start(out=w1_raw.bitcast(I32), in_=w1_words[0].bitcast(I32))
-        load_scale_rows(nc.sync, w_plane_raw, w3_scales[0], W3_ROW)
+        load_scale_rows(nc, w_plane_raw, w3_scales[0], W3_ROW)
         nc.sync.dma_start(out=b1_sb[:], in_=b1.rearrange("(b p t) -> p b t", p=P, t=PACK))
+        nc.sync.dma_start(out=w3_raw[:], in_=w3_words[0].rearrange("p c i -> p (c i)").bitcast(I32))
+        nc.sync.dma_start(out=b3_sb[:], in_=b3.rearrange("(b p t) -> p b t", p=P, t=PACK))
         nc.sync.dma_start(
             out=w4_raw[:].rearrange("p b i n -> p b (i n)"),
             in_=w4.rearrange("(b p i) n -> p b (i n)", p=P, i=PACK),
         )
-        nc.sync.dma_start(out=w3_raw[:], in_=w3_words[0].rearrange("p c i -> p (c i)").bitcast(I32))
-        nc.sync.dma_start(out=b3_sb[:], in_=b3.rearrange("(b p t) -> p b t", p=P, t=PACK))
         with nc.allow_non_contiguous_dma(reason="one bias value a partition"):
             nc.sync.dma_start(out=b4_sb[:], in_=b4.rearrange("(c p) -> p c", p=P))
 
-        words_at = {("up", 1): RAW_AT - 1536, ("own", 1): RAW_AT + 512, ("down", 0): RAW_AT + 2560}
+        words_at = {
+            ("up", 0): BF0_AT,
+            ("own", 0): BF0_AT + WORDS,
+            ("up", 1): TRIO_AT + WORDS,
+            ("own", 1): TRIO_AT + 2 * WORDS,
+            ("down", 0): BF1_AT,
+            ("down", 1): W3_AT,
+        }
         picked = {}
 
-        def gather(kind, name, halves):
-            label = "%s_%s%d" % (kind, name, halves[0])
-            shape = [P, len(halves) * BANK]
-            dtype = U32 if kind == "words" else U8
-            at = words_at.get((name, halves[0])) if kind == "words" else None
-            dst = held(shape, dtype, label) if at is None else placed(shape, dtype, label, at)
-            window = tab[:].bitcast(U32) if kind == "words" else tab_plane[:]
-            cols = lists[name][:, halves[0] * BANK // 16 : (halves[-1] + 1) * BANK // 16]
-            nc.vector.tensor_copy(dst[:], window.indirect(cols))
-            for n, half in enumerate(halves):
-                picked[kind, name, half] = dst[:, n * BANK : (n + 1) * BANK]
+        def gather_plane(name):
+            dst = held([P, S], U8, "plane_%s0" % name)
+            nc.vector.tensor_copy(dst[:], tab_plane[:].indirect(lists[name][:]))
+            for half in range(S // BANK):
+                picked["plane", name, half] = dst[:, half * BANK : (half + 1) * BANK]
+
+        def gather_words(name, half):
+            dst = placed([P, BANK], U32, "words_%s%d" % (name, half), words_at[name, half])
+            entries = lists[name][:, half * BANK // 16 : (half + 1) * BANK // 16]
+            nc.vector.tensor_copy(dst[:], tab[:].bitcast(U32).indirect(entries))
+            picked["words", name, half] = dst[:]
 
         w_plane = held([P, H], U8, "w_plane")
         w3_dealt = held([P, H], I32, "w3_dealt")
@@ -131,34 +141,39 @@ def tile_list_codon_context_rate_kernel(
                 in_=w1_raw.bitcast(U16).rearrange("p (c i t) -> p c t i", t=PACK, i=8),
             )
 
-        w2_bf = held([P, H * PACK], BF16, "w2_bf")
-        w2_codes = held([P, H], U32, "w2_codes")
-        w2_plane = held([P, H], U8, "w2_plane")
+        w2_bf = [placed([P, BANK * PACK], BF16, "w2_bf%d" % b, at) for b, at in enumerate((BF0_AT, BF1_AT))]
+        w2_codes = [held([P, BANK], U32, "w2_codes0"), placed([P, BANK], U32, "w2_codes1", TRIO_AT)]
+        w2_plane = [held([P, BANK], U8, "w2_plane%d" % b) for b in range(PASSES)]
 
         def cast_w2(b):
             nc.scalar.copy(
-                out=w2_bf[:, b * BANK * PACK : (b + 1) * BANK * PACK].rearrange("p (t m i) -> p m i t", t=PACK, i=PACK),
+                out=w2_bf[b][:].rearrange("p (t m i) -> p m i t", t=PACK, i=PACK),
                 in_=w2_raw[b][:].rearrange("p i (m t) -> p m i t", t=PACK),
             )
 
-        def quant_w2():
-            nc.vector.quantize_mx(out=w2_codes[:].bitcast(FP8X4), scales=w2_plane[:], in_=w2_bf[:])
+        def quant_w2(b):
+            nc.vector.quantize_mx(out=w2_codes[b][:].bitcast(FP8X4), scales=w2_plane[b][:], in_=w2_bf[b][:])
 
-        w4_bf = placed([P, PASSES * N * PACK], BF16, "w4_bf", W4BF_AT)
-        w4_codes = held([P, PASSES * N], U32, "w4_codes")
+        w4_bf = placed([P, PASSES * N * PACK], BF16, "w4_bf", TAB_AT)
+        w4_codes = placed([P, PASSES * N], U32, "w4_codes", RATE_AT + 3 * WORDS)
         w4_plane = held([P, PASSES * N], U8, "w4_plane")
 
-        def cast_w4():
-            nc.scalar.copy(
-                out=w4_bf[:].rearrange("p (b c n i) -> p b c i n", b=PASSES, i=PACK, n=4),
-                in_=w4_raw[:].rearrange("p b i (c n) -> p b c i n", n=4),
-            )
+        def cast_w4(b):
+            dst = w4_bf[:, b * N * PACK : (b + 1) * N * PACK]
+            if b == 0:
+                nc.gpsimd.tensor_copy(
+                    out=dst.rearrange("p (n i) -> p n i", i=PACK), in_=w4_raw[:, b].rearrange("p i n -> p n i")
+                )
+            else:
+                nc.scalar.copy(
+                    out=dst.rearrange("p (c n i) -> p c i n", i=PACK, n=4),
+                    in_=w4_raw[:, b].rearrange("p i (c n) -> p c i n", n=4),
+                )
 
         def quant_w4():
             nc.vector.quantize_mx(out=w4_codes[:].bitcast(FP8X4), scales=w4_plane[:], in_=w4_bf[:])
 
         rate = {}
-        rate_at = {(0, 0): W4_AT - 4096, (0, 1): W4_AT + 4096, (1, 0): LAST_AT}
         h_slices = {}
         h_codes = {}
         h_plane = {}
@@ -168,17 +183,15 @@ def tile_list_codon_context_rate_kernel(
             if (half, b) not in rate:
                 label = "rate%d%d" % (half, b)
                 shape = [P, PACK, BANK]
-                at = rate_at.get((half, b))
-                rate[half, b] = held(shape, F32, label) if at is None else placed(shape, F32, label, at)
+                rate[half, b] = placed(shape, F32, label, RATE_AT) if (half, b) == (1, 0) else held(shape, F32, label)
             dst = rate[half, b]
             for t in slices:
                 c0 = t * M + b * P
-                c2 = b * BANK + t * P
                 acc = bank(PACK * b + t)
                 nc.tensor.matmul_mx(
                     out=acc[:],
-                    lhsT=w2_codes[:, c2 : c2 + P].bitcast(FP8X4),
-                    lhsT_scale=w2_plane[:, c2 : c2 + P],
+                    lhsT=w2_codes[b][:, t * P : (t + 1) * P].bitcast(FP8X4),
+                    lhsT_scale=w2_plane[b][:, t * P : (t + 1) * P],
                     rhs=picked["words", "up", half].bitcast(FP8X4),
                     rhs_scale=picked["plane", "up", half],
                     start=True,
@@ -195,7 +208,8 @@ def tile_list_codon_context_rate_kernel(
                 )
                 nc.scalar.activation(dst[:, t, :], acc[:], ACT.Exp, bias=b1_sb[:, b, t : t + 1])
 
-        def product_d(half, b, t, acc):
+        def product_d(half, b, t):
+            acc = bank(PACK * (1 - b) + t)
             cols = slice(t * M + b * P, t * M + (b + 1) * P)
             nc.tensor.matmul_mx(
                 out=acc[:],
@@ -206,42 +220,37 @@ def tile_list_codon_context_rate_kernel(
                 start=True,
                 stop=True,
             )
+            return acc
 
         def stage_d(half, b, slices=range(PACK)):
             if (half, b) not in h_slices:
-                label = "h_slices%d%d" % (half, b)
-                shape = [P, PACK, BANK]
-                first = (half, b) == (0, 0)
-                h_slices[half, b] = placed(shape, BF16, label, W4BF_AT) if first else held(shape, BF16, label)
+                h_slices[half, b] = held([P, PACK, BANK], BF16, "h_slices%d%d" % (half, b))
             dst = h_slices[half, b]
             for t in slices:
-                acc = bank(PACK * (1 - b) + t)
-                product_d(half, b, t, acc)
+                acc = product_d(half, b, t)
                 nc.vector.scalar_tensor_tensor(
                     dst[:, t, :], acc[:], b3_sb[:, b, t : t + 1], rate[half, b][:, t, :], ALU.add, ALU.mult
                 )
 
         last_down = held([P, PACK, BANK], F32, "last_down")
 
-        def stage_last_d(slices):
-            for t in slices:
-                acc = bank(t)
-                product_d(1, 1, t, acc)
-                nc.scalar.activation(last_down[:, t, :], acc[:], ACT.Identity, bias=b3_sb[:, 1, t : t + 1])
+        def stage_last_d(t):
+            acc = product_d(*LAST, t)
+            nc.scalar.activation(last_down[:, t, :], acc[:], ACT.Identity, bias=b3_sb[:, LAST[1], t : t + 1])
 
         def multiply_last(j0, j1):
             dst = held([P, (j1 - j0) * PACK], BF16, "h_bf11_%d" % j0)
             nc.vector.tensor_tensor(
                 out=dst[:].rearrange("p (c i t) -> p c t i", i=2, t=PACK),
-                in0=rate[1, 1][:, :, j0:j1].rearrange("p t (c i) -> p c t i", i=2),
+                in0=rate[LAST][:, :, j0:j1].rearrange("p t (c i) -> p c t i", i=2),
                 in1=last_down[:, :, j0:j1].rearrange("p t (c i) -> p c t i", i=2),
                 op=ALU.mult,
             )
-            h_bf[1, 1, j0] = dst
+            h_bf[(*LAST, j0)] = dst
 
-        def weave(half, b, j0, j1):
-            dst = held([P, (j1 - j0) * PACK], BF16, "h_bf%d%d_%d" % (half, b, j0))
-            src = h_slices[half, b][:, :, j0:j1]
+        def weave(half, b):
+            dst = held([P, BANK * PACK], BF16, "h_bf%d%d_0" % (half, b))
+            src = h_slices[half, b][:]
             if half == 0:
                 nc.gpsimd.tensor_copy(
                     out=dst[:].rearrange("p (c t) -> p c t", t=PACK), in_=src.rearrange("p t c -> p c t")
@@ -251,12 +260,14 @@ def tile_list_codon_context_rate_kernel(
                     out=dst[:].rearrange("p (c i t) -> p c t i", i=4, t=PACK),
                     in_=src.rearrange("p t (c i) -> p c t i", i=4),
                 )
-            h_bf[half, b, j0] = dst
+            h_bf[half, b, 0] = dst
 
         def quant_h(half, b, j0, j1):
-            codes = placed(
-                [P, j1 - j0], U32, "h_codes%d%d_%d" % (half, b, j0), LAST_AT + 4 * ((half * PASSES + b) * BANK + j0)
-            )
+            label = "h_codes%d%d_%d" % (half, b, j0)
+            if (half, b) == LAST:
+                codes = held([P, j1 - j0], U32, label)
+            else:
+                codes = placed([P, j1 - j0], U32, label, RATE_AT + WORDS * (half * PASSES + b))
             plane = held([P, j1 - j0], U8, "h_plane%d%d_%d" % (half, b, j0))
             nc.vector.quantize_mx(out=codes[:].bitcast(FP8X4), scales=plane[:], in_=h_bf[half, b, j0][:])
             for a0, a1 in ((0, BANK),) + TAIL:
@@ -264,7 +275,7 @@ def tile_list_codon_context_rate_kernel(
                     h_codes[half, b, a0, a1] = codes[:, a0 - j0 : a1 - j0]
                     h_plane[half, b, a0, a1] = plane[:, a0 - j0 : a1 - j0]
 
-        def stage_y(half, j0, j1, first_bank, on_vector):
+        def stage_y(half, j0, j1, first_bank, shared_out=False):
             width = j1 - j0
             for c in range(N // P):
                 acc = bank(first_bank + c)
@@ -280,51 +291,56 @@ def tile_list_codon_context_rate_kernel(
                         stop=(b == PASSES - 1),
                     )
                 res = held([P, width], F32, "res%d%d_%d" % (half, c, j0))
-                if c in on_vector:
+                if shared_out and c == 1:
                     nc.vector.tensor_scalar(res[:], acc[:, 0:width], b4_sb[:, c : c + 1], None, ALU.add)
                     queue = nc.sync
                 else:
                     nc.scalar.activation(res[:], acc[:, 0:width], ACT.Identity, bias=b4_sb[:, c : c + 1])
-                    queue = nc.scalar if on_vector else nc.sync
+                    queue = nc.scalar if shared_out else nc.sync
                 queue.dma_start(out=out[c * P : (c + 1) * P, half * BANK + j0 : half * BANK + j1], in_=res[:])
 
         for name in ("up", "own", "down"):
-            gather("plane", name, (0, 1))
+            gather_plane(name)
         cast_w2(0)
         cast_w2(1)
-        gather("words", "up", (0,))
-        gather("words", "own", (0,))
+        quant_w2(0)
+        gather_words("up", 0)
+        gather_words("own", 0)
         deal_w1()
-        quant_w2()
         deal_plane()
-        cast_w4()
         stage_e(0, 0)
+        quant_w2(1)
         stage_e(0, 1)
-        gather("words", "up", (1,))
-        gather("words", "own", (1,))
-        gather("words", "down", (0, 1))
+        gather_words("up", 1)
+        gather_words("own", 1)
+        gather_words("down", 0)
         deal_w3()
-        quant_w4()
+        gather_words("down", 1)
+        cast_w4(0)
         stage_e(1, 0)
+
         stage_d(0, 0)
-        weave(0, 0, 0, BANK)
+        weave(0, 0)
         for t in range(PACK):
             stage_d(0, 1, (t,))
-            stage_e(1, 1, (t,))
-        weave(0, 1, 0, BANK)
+            stage_e(*LAST, (t,))
+        weave(0, 1)
         for t in range(PACK):
-            stage_last_d((t,))
+            stage_last_d(t)
             stage_d(1, 0, (t,))
-        weave(1, 0, 0, BANK)
+        cast_w4(1)
+        weave(1, 0)
+
         quant_h(0, 0, 0, BANK)
+        quant_w4()
         quant_h(0, 1, 0, BANK)
-        stage_y(0, 0, BANK, 0, ())
+        stage_y(0, 0, BANK, 0)
         multiply_last(*TAIL[0])
         multiply_last(*TAIL[1])
         quant_h(1, 0, 0, BANK)
-        quant_h(1, 1, *TAIL[0])
+        quant_h(*LAST, *TAIL[0])
         multiply_last(*TAIL[2])
-        quant_h(1, 1, *TAIL[1])
-        quant_h(1, 1, *TAIL[2])
+        quant_h(*LAST, *TAIL[1])
+        quant_h(*LAST, *TAIL[2])
         for n, piece in enumerate(TAIL):
-            stage_y(1, *piece, 2 + 2 * n, (1,) if n == len(TAIL) - 1 else ())
+            stage_y(1, *piece, 2 + 2 * n, shared_out=(n == len(TAIL) - 1))

@@ -36,10 +36,10 @@ RATE_AT = TAB_AT + 4 * WORDS
 
 
 def load_scale_rows(nc, plane, rows, first):
-    for q in range(4):
+    for r in range(4):
         nc.sync.dma_start(
-            out=plane[32 * q + first : 32 * q + first + 4, :].bitcast(I32),
-            in_=rows[4 * q : 4 * q + 4, :].bitcast(I32),
+            out=plane[first + r : P : 32, :].bitcast(I32),
+            in_=rows[r:16:4, :].bitcast(I32),
         )
 
 

@@ -26,21 +26,26 @@ TAIL = ((0, 256), (256, 384), (384, 512))
 W3_ROW = 4
 
 WORDS = 4 * BANK
-TRIO_AT = 0
-RAW_AT = TRIO_AT + 3 * WORDS // 4
-BF1_AT = TRIO_AT + 3 * WORDS
-BF0_AT = BF1_AT + 2 * WORDS
-W3_AT = BF0_AT + 2 * WORDS
-TAB_AT = W3_AT + 2 * WORDS
-RATE_AT = TAB_AT + 4 * WORDS
+W2_AT = (0, 4 * WORDS)
+TAB_AT = 8 * WORDS
+W3_AT = 12 * WORDS
+ROW_AT = 14 * WORDS
+RAW_AT = ROW_AT + WORDS - BANK
+BF1_AT = 18 * WORDS
 
 
-def load_scale_rows(nc, plane, rows, first):
-    for r in range(4):
+def load_scale_rows(nc, plane, rows, first, which=range(4)):
+    for r in which:
         nc.sync.dma_start(
             out=plane[first + r : P : 32, :].bitcast(I32),
             in_=rows[r:16:4, :].bitcast(I32),
         )
+
+
+def load_bias(nc, dst, bias):
+    runs = bias.rearrange("(b g e) -> g b e", b=PASSES, e=2 * PACK)
+    for v in range(2):
+        nc.sync.dma_start(out=dst[v:P:2, :, 0 : 2 * PACK - 1], in_=runs[:, :, v : v + 2 * PACK - 1])
 
 
 def tile_list_codon_context_rate_kernel(
@@ -71,39 +76,40 @@ def tile_list_codon_context_rate_kernel(
         lists = {name: keep.tile([P, S // 16], U16, name="list_" + name) for name in ("down", "up", "own")}
         w2_rows = w2.rearrange("(p i) c -> p i c", i=PACK)
         tab = placed([P, T], I32, "tab", TAB_AT)
-        w3_raw = placed([P, H], I32, "w3_raw", W3_AT)
-        b1_sb = held([P, PASSES, PACK], F32, "b1_sb")
-        b3_sb = held([P, PASSES, PACK], F32, "b3_sb")
+        w3_raw = held([P, H], I32, "w3_raw")
+        b1_sb = held([P, PASSES, 2 * PACK], F32, "b1_sb")
+        b3_sb = held([P, PASSES, 2 * PACK], F32, "b3_sb")
         b4_sb = held([P, N // P], F32, "b4_sb")
-        w2_raw = [held([P, PACK, BANK], F32, "w2_raw%d" % b) for b in range(PASSES)]
-        w4_raw = held([P, PASSES, PACK, N], F32, "w4_raw")
+        w2_raw = [placed([P, PACK, BANK], F32, "w2_raw%d" % b, W2_AT[b]) for b in range(PASSES)]
+        w4_raw = [held([P, PACK, N], F32, "w4_raw%d" % b) for b in range(PASSES)]
 
-        for name, src in (("down", offs3), ("up", offs2), ("own", offs)):
+        for name, src in (("up", offs2), ("own", offs), ("down", offs3)):
             nc.sync.dma_start(lists[name][:], src)
         load_scale_rows(nc, tab_plane, tab_scales[0], 0)
         nc.sync.dma_start(out=w2_raw[0][:], in_=w2_rows[:, :, 0:BANK])
         nc.sync.dma_start(out=tab[:], in_=tab_words[0].rearrange("p t i -> p (t i)").bitcast(I32))
         load_scale_rows(nc, w_plane_raw, w1_scales[0], 0)
-        nc.sync.dma_start(out=w2_raw[1][:], in_=w2_rows[:, :, BANK : 2 * BANK])
         nc.sync.dma_start(out=w1_raw.bitcast(I32), in_=w1_words[0].bitcast(I32))
-        load_scale_rows(nc, w_plane_raw, w3_scales[0], W3_ROW)
-        nc.sync.dma_start(out=b1_sb[:], in_=b1.rearrange("(b p t) -> p b t", p=P, t=PACK))
+        load_scale_rows(nc, w_plane_raw, w3_scales[0], W3_ROW, (0,))
+        nc.sync.dma_start(out=w2_raw[1][:], in_=w2_rows[:, :, BANK : 2 * BANK])
+        load_scale_rows(nc, w_plane_raw, w3_scales[0], W3_ROW, (1, 2, 3))
         nc.sync.dma_start(out=w3_raw[:], in_=w3_words[0].rearrange("p c i -> p (c i)").bitcast(I32))
-        nc.sync.dma_start(out=b3_sb[:], in_=b3.rearrange("(b p t) -> p b t", p=P, t=PACK))
-        nc.sync.dma_start(
-            out=w4_raw[:].rearrange("p b i n -> p b (i n)"),
-            in_=w4.rearrange("(b p i) n -> p b (i n)", p=P, i=PACK),
-        )
+        load_bias(nc, b1_sb, b1)
+        load_bias(nc, b3_sb, b3)
+        w4_rows = w4.rearrange("(b g t v) n -> b v g t n", b=PASSES, t=PACK, v=2)
+        for b in range(PASSES):
+            for v in range(2):
+                nc.sync.dma_start(out=w4_raw[b][v:P:2], in_=w4_rows[b, v])
         with nc.allow_non_contiguous_dma(reason="one bias value a partition"):
             nc.sync.dma_start(out=b4_sb[:], in_=b4.rearrange("(c p) -> p c", p=P))
 
         words_at = {
-            ("up", 0): BF0_AT,
-            ("own", 0): BF0_AT + WORDS,
-            ("up", 1): TRIO_AT + WORDS,
-            ("own", 1): TRIO_AT + 2 * WORDS,
+            ("up", 0): W2_AT[0],
+            ("own", 0): W2_AT[0] + WORDS,
+            ("up", 1): ROW_AT,
+            ("own", 1): ROW_AT + WORDS + 3 * BANK,
             ("down", 0): BF1_AT,
-            ("down", 1): W3_AT,
+            ("down", 1): BF1_AT + WORDS,
         }
         picked = {}
 
@@ -113,6 +119,12 @@ def tile_list_codon_context_rate_kernel(
             for half in range(S // BANK):
                 picked["plane", name, half] = dst[:, half * BANK : (half + 1) * BANK]
 
+        def gather_late_plane(half):
+            dst = placed([P, BANK], U8, "plane_down%d" % half, ROW_AT + WORDS + half * BANK)
+            entries = lists["down"][:, half * BANK // 16 : (half + 1) * BANK // 16]
+            nc.vector.tensor_copy(dst[:], tab_plane[:].indirect(entries))
+            picked["plane", "down", half] = dst[:]
+
         def gather_words(name, half):
             dst = placed([P, BANK], U32, "words_%s%d" % (name, half), words_at[name, half])
             entries = lists[name][:, half * BANK // 16 : (half + 1) * BANK // 16]
@@ -120,54 +132,54 @@ def tile_list_codon_context_rate_kernel(
             picked["words", name, half] = dst[:]
 
         w_plane = held([P, H], U8, "w_plane")
-        w3_dealt = held([P, H], I32, "w3_dealt")
+        w3_dealt = placed([P, H], I32, "w3_dealt", W3_AT)
         w1_dealt = held([P, 2 * H], U8, "w1_dealt")
 
         def deal_plane():
             nc.vector.tensor_copy(
-                out=w_plane[:].rearrange("p (t c i) -> p c t i", t=PACK, i=16),
-                in_=w_plane_raw.rearrange("p (c i t) -> p c t i", t=PACK, i=16),
+                out=w_plane[:].bitcast(U16).rearrange("p (t c i) -> p c t i", t=PACK, i=8),
+                in_=w_plane_raw.bitcast(U16).rearrange("p (c i t) -> p c t i", t=PACK, i=8),
             )
 
         def deal_w3():
             nc.vector.tensor_copy(
-                out=w3_dealt[:].rearrange("p (t c i) -> p c t i", t=PACK, i=4),
-                in_=w3_raw[:].rearrange("p (c i t) -> p c t i", t=PACK, i=4),
+                out=w3_dealt[:].rearrange("p (t c i v) -> p c t i v", t=PACK, i=2, v=2),
+                in_=w3_raw[:].rearrange("p (c i t v) -> p c t i v", t=PACK, i=2, v=2),
             )
 
         def deal_w1():
             nc.vector.tensor_copy(
-                out=w1_dealt[:].bitcast(U16).rearrange("p (t c i) -> p c t i", t=PACK, i=8),
-                in_=w1_raw.bitcast(U16).rearrange("p (c i t) -> p c t i", t=PACK, i=8),
+                out=w1_dealt[:].bitcast(I32).rearrange("p (t c i) -> p c t i", t=PACK, i=4),
+                in_=w1_raw.bitcast(I32).rearrange("p (c i t) -> p c t i", t=PACK, i=4),
             )
 
-        w2_bf = [placed([P, BANK * PACK], BF16, "w2_bf%d" % b, at) for b, at in enumerate((BF0_AT, BF1_AT))]
-        w2_codes = [held([P, BANK], U32, "w2_codes0"), placed([P, BANK], U32, "w2_codes1", TRIO_AT)]
-        w2_plane = [held([P, BANK], U8, "w2_plane%d" % b) for b in range(PASSES)]
+        w2_bf = [held([P, BANK * PACK], BF16, "w2_bf0"), placed([P, BANK * PACK], BF16, "w2_bf1", BF1_AT)]
+        w2_codes = [held([P, BANK], U32, "w2_codes%d" % b) for b in range(PASSES)]
+        w2_plane = [held([P, BANK], U8, "w2_plane0"), placed([P, BANK], U8, "w2_plane1", ROW_AT + WORDS + 2 * BANK)]
 
         def cast_w2(b):
             nc.scalar.copy(
-                out=w2_bf[b][:].rearrange("p (t m i) -> p m i t", t=PACK, i=PACK),
-                in_=w2_raw[b][:].rearrange("p i (m t) -> p m i t", t=PACK),
+                out=w2_bf[b][:].rearrange("p (t g v i) -> p g t i v", t=PACK, v=2, i=PACK),
+                in_=w2_raw[b][:].rearrange("p i (g t v) -> p g t i v", t=PACK, v=2),
             )
 
         def quant_w2(b):
             nc.vector.quantize_mx(out=w2_codes[b][:].bitcast(FP8X4), scales=w2_plane[b][:], in_=w2_bf[b][:])
 
         w4_bf = placed([P, PASSES * N * PACK], BF16, "w4_bf", TAB_AT)
-        w4_codes = placed([P, PASSES * N], U32, "w4_codes", RATE_AT + 3 * WORDS)
-        w4_plane = held([P, PASSES * N], U8, "w4_plane")
+        w4_codes = held([P, PASSES * N], U32, "w4_codes")
+        w4_plane = placed([P, PASSES * N], U8, "w4_plane", W3_AT + PASSES * BANK)
 
         def cast_w4(b):
             dst = w4_bf[:, b * N * PACK : (b + 1) * N * PACK]
             if b == 0:
                 nc.gpsimd.tensor_copy(
-                    out=dst.rearrange("p (n i) -> p n i", i=PACK), in_=w4_raw[:, b].rearrange("p i n -> p n i")
+                    out=dst.rearrange("p (n i) -> p n i", i=PACK), in_=w4_raw[b][:].rearrange("p i n -> p n i")
                 )
             else:
                 nc.scalar.copy(
                     out=dst.rearrange("p (c n i) -> p c i n", i=PACK, n=4),
-                    in_=w4_raw[:, b].rearrange("p i (c n) -> p c i n", n=4),
+                    in_=w4_raw[b][:].rearrange("p i (c n) -> p c i n", n=4),
                 )
 
         def quant_w4():
@@ -179,15 +191,13 @@ def tile_list_codon_context_rate_kernel(
         h_plane = {}
         h_bf = {}
 
-        def stage_e(half, b, slices=range(PACK)):
+        def stage_e(half, b, group, slices=range(PACK)):
             if (half, b) not in rate:
-                label = "rate%d%d" % (half, b)
-                shape = [P, PACK, BANK]
-                rate[half, b] = placed(shape, F32, label, RATE_AT) if (half, b) == (1, 0) else held(shape, F32, label)
+                rate[half, b] = held([P, PACK, BANK], F32, "rate%d%d" % (half, b))
             dst = rate[half, b]
             for t in slices:
                 c0 = t * M + b * P
-                acc = bank(PACK * b + t)
+                acc = bank(PACK * group + t)
                 nc.tensor.matmul_mx(
                     out=acc[:],
                     lhsT=w2_codes[b][:, t * P : (t + 1) * P].bitcast(FP8X4),
@@ -206,10 +216,10 @@ def tile_list_codon_context_rate_kernel(
                     start=False,
                     stop=True,
                 )
-                nc.scalar.activation(dst[:, t, :], acc[:], ACT.Exp, bias=b1_sb[:, b, t : t + 1])
+                nc.scalar.activation(dst[:, t, :], acc[:], ACT.Exp, bias=b1_sb[:, b, 2 * t : 2 * t + 1])
 
         def product_d(half, b, t):
-            acc = bank(PACK * (1 - b) + t)
+            acc = bank(PACK * (0 if (half, b) == LAST else 1) + t)
             cols = slice(t * M + b * P, t * M + (b + 1) * P)
             nc.tensor.matmul_mx(
                 out=acc[:],
@@ -229,14 +239,14 @@ def tile_list_codon_context_rate_kernel(
             for t in slices:
                 acc = product_d(half, b, t)
                 nc.vector.scalar_tensor_tensor(
-                    dst[:, t, :], acc[:], b3_sb[:, b, t : t + 1], rate[half, b][:, t, :], ALU.add, ALU.mult
+                    dst[:, t, :], acc[:], b3_sb[:, b, 2 * t : 2 * t + 1], rate[half, b][:, t, :], ALU.add, ALU.mult
                 )
 
         last_down = held([P, PACK, BANK], F32, "last_down")
 
         def stage_last_d(t):
             acc = product_d(*LAST, t)
-            nc.scalar.activation(last_down[:, t, :], acc[:], ACT.Identity, bias=b3_sb[:, LAST[1], t : t + 1])
+            nc.scalar.activation(last_down[:, t, :], acc[:], ACT.Identity, bias=b3_sb[:, LAST[1], 2 * t : 2 * t + 1])
 
         def multiply_last(j0, j1):
             dst = held([P, (j1 - j0) * PACK], BF16, "h_bf11_%d" % j0)
@@ -263,12 +273,9 @@ def tile_list_codon_context_rate_kernel(
             h_bf[half, b, 0] = dst
 
         def quant_h(half, b, j0, j1):
-            label = "h_codes%d%d_%d" % (half, b, j0)
-            if (half, b) == LAST:
-                codes = held([P, j1 - j0], U32, label)
-            else:
-                codes = placed([P, j1 - j0], U32, label, RATE_AT + WORDS * (half * PASSES + b))
-            plane = held([P, j1 - j0], U8, "h_plane%d%d_%d" % (half, b, j0))
+            codes = held([P, j1 - j0], U32, "h_codes%d%d_%d" % (half, b, j0))
+            label = "h_plane%d%d_%d" % (half, b, j0)
+            plane = placed([P, BANK], U8, label, W3_AT + b * BANK) if half == 0 else held([P, j1 - j0], U8, label)
             nc.vector.quantize_mx(out=codes[:].bitcast(FP8X4), scales=plane[:], in_=h_bf[half, b, j0][:])
             for a0, a1 in ((0, BANK),) + TAIL:
                 if j0 <= a0 and a1 <= j1:
@@ -299,7 +306,7 @@ def tile_list_codon_context_rate_kernel(
                     queue = nc.scalar if shared_out else nc.sync
                 queue.dma_start(out=out[c * P : (c + 1) * P, half * BANK + j0 : half * BANK + j1], in_=res[:])
 
-        for name in ("up", "own", "down"):
+        for name in ("up", "own"):
             gather_plane(name)
         cast_w2(0)
         cast_w2(1)
@@ -308,26 +315,27 @@ def tile_list_codon_context_rate_kernel(
         gather_words("own", 0)
         deal_w1()
         deal_plane()
-        stage_e(0, 0)
-        quant_w2(1)
-        stage_e(0, 1)
+        stage_e(0, 0, 0)
         gather_words("up", 1)
         gather_words("own", 1)
+        stage_e(1, 0, 1)
+        quant_w2(1)
+        stage_e(0, 1, 0)
+        gather_late_plane(0)
         gather_words("down", 0)
         deal_w3()
+        gather_late_plane(1)
         gather_words("down", 1)
         cast_w4(0)
-        stage_e(1, 0)
 
         stage_d(0, 0)
         weave(0, 0)
+        stage_e(*LAST, 0)
         for t in range(PACK):
             stage_d(0, 1, (t,))
-            stage_e(*LAST, (t,))
-        weave(0, 1)
-        for t in range(PACK):
             stage_last_d(t)
-            stage_d(1, 0, (t,))
+        weave(0, 1)
+        stage_d(1, 0)
         cast_w4(1)
         weave(1, 0)
 

@@ -63,7 +63,11 @@ def tile_list_codon_context_rate_kernel(
         def placed(shape, dtype, name, at):
             return shared.tile(shape, dtype, name=name, offset=at, align_bytes=64)
 
-        def bank(n):
+        taken = []
+
+        def next_bank():
+            n = len(taken) % 8
+            taken.append(n)
             return psum.tile([P, BANK], F32, name="bank%d" % n, tag="bank%d" % n)
 
         tab_plane = held([P, T], U8, "tab_plane")
@@ -172,15 +176,9 @@ def tile_list_codon_context_rate_kernel(
 
         def cast_w4(b):
             dst = w4_bf[:, b * N * PACK : (b + 1) * N * PACK]
-            if b == 0:
-                nc.gpsimd.tensor_copy(
-                    out=dst.rearrange("p (n i) -> p n i", i=PACK), in_=w4_raw[b][:].rearrange("p i n -> p n i")
-                )
-            else:
-                nc.scalar.copy(
-                    out=dst.rearrange("p (c n i) -> p c i n", i=PACK, n=4),
-                    in_=w4_raw[b][:].rearrange("p i (c n) -> p c i n", n=4),
-                )
+            nc.gpsimd.tensor_copy(
+                out=dst.rearrange("p (n i) -> p n i", i=PACK), in_=w4_raw[b][:].rearrange("p i n -> p n i")
+            )
 
         def quant_w4():
             nc.vector.quantize_mx(out=w4_codes[:].bitcast(FP8X4), scales=w4_plane[:], in_=w4_bf[:])
@@ -191,35 +189,51 @@ def tile_list_codon_context_rate_kernel(
         h_plane = {}
         h_bf = {}
 
-        def stage_e(half, b, group, slices=range(PACK)):
+        def pass_w2(acc, half, b, t, first):
+            nc.tensor.matmul_mx(
+                out=acc[:],
+                lhsT=w2_codes[b][:, t * P : (t + 1) * P].bitcast(FP8X4),
+                lhsT_scale=w2_plane[b][:, t * P : (t + 1) * P],
+                rhs=picked["words", "up", half].bitcast(FP8X4),
+                rhs_scale=picked["plane", "up", half],
+                start=first,
+                stop=not first,
+            )
+
+        def pass_w1(acc, half, b, t, first):
+            c0 = t * M + b * P
+            nc.tensor.matmul_mx(
+                out=acc[:],
+                lhsT=w1_dealt[:, 2 * c0 : 2 * (c0 + P)].bitcast(FP4X4),
+                lhsT_scale=w_plane[:, c0 : c0 + P],
+                rhs=picked["words", "own", half].bitcast(FP8X4),
+                rhs_scale=picked["plane", "own", half],
+                start=first,
+                stop=not first,
+            )
+
+        opened = {}
+
+        def open_e(half, b, opening, slices=range(PACK)):
+            for t in slices:
+                opened[half, b, t] = next_bank()
+                opening(opened[half, b, t], half, b, t, True)
+
+        def close_e(half, b, closing, slices=range(PACK)):
             if (half, b) not in rate:
                 rate[half, b] = held([P, PACK, BANK], F32, "rate%d%d" % (half, b))
-            dst = rate[half, b]
             for t in slices:
-                c0 = t * M + b * P
-                acc = bank(PACK * group + t)
-                nc.tensor.matmul_mx(
-                    out=acc[:],
-                    lhsT=w2_codes[b][:, t * P : (t + 1) * P].bitcast(FP8X4),
-                    lhsT_scale=w2_plane[b][:, t * P : (t + 1) * P],
-                    rhs=picked["words", "up", half].bitcast(FP8X4),
-                    rhs_scale=picked["plane", "up", half],
-                    start=True,
-                    stop=False,
-                )
-                nc.tensor.matmul_mx(
-                    out=acc[:],
-                    lhsT=w1_dealt[:, 2 * c0 : 2 * (c0 + P)].bitcast(FP4X4),
-                    lhsT_scale=w_plane[:, c0 : c0 + P],
-                    rhs=picked["words", "own", half].bitcast(FP8X4),
-                    rhs_scale=picked["plane", "own", half],
-                    start=False,
-                    stop=True,
-                )
-                nc.scalar.activation(dst[:, t, :], acc[:], ACT.Exp, bias=b1_sb[:, b, 2 * t : 2 * t + 1])
+                acc = opened[half, b, t]
+                closing(acc, half, b, t, False)
+                nc.scalar.activation(rate[half, b][:, t, :], acc[:], ACT.Exp, bias=b1_sb[:, b, 2 * t : 2 * t + 1])
+
+        def stage_e(half, b, slices=range(PACK)):
+            for t in slices:
+                open_e(half, b, pass_w2, (t,))
+                close_e(half, b, pass_w1, (t,))
 
         def product_d(half, b, t):
-            acc = bank(PACK * (0 if (half, b) == LAST else 1) + t)
+            acc = next_bank()
             cols = slice(t * M + b * P, t * M + (b + 1) * P)
             nc.tensor.matmul_mx(
                 out=acc[:],
@@ -258,19 +272,18 @@ def tile_list_codon_context_rate_kernel(
             )
             h_bf[(*LAST, j0)] = dst
 
-        def weave(half, b):
-            dst = held([P, BANK * PACK], BF16, "h_bf%d%d_0" % (half, b))
-            src = h_slices[half, b][:]
-            if half == 0:
-                nc.gpsimd.tensor_copy(
-                    out=dst[:].rearrange("p (c t) -> p c t", t=PACK), in_=src.rearrange("p t c -> p c t")
-                )
+        def weave(half, b, engine, j0=0, j1=BANK):
+            if (half, b, 0) not in h_bf:
+                h_bf[half, b, 0] = held([P, BANK * PACK], BF16, "h_bf%d%d_0" % (half, b))
+            dst = h_bf[half, b, 0][:, j0 * PACK : j1 * PACK]
+            src = h_slices[half, b][:, :, j0:j1]
+            if engine == "gpsimd":
+                nc.gpsimd.tensor_copy(out=dst.rearrange("p (c t) -> p c t", t=PACK), in_=src.rearrange("p t c -> p c t"))
             else:
                 nc.scalar.copy(
-                    out=dst[:].rearrange("p (c i t) -> p c t i", i=4, t=PACK),
+                    out=dst.rearrange("p (c i t) -> p c t i", i=4, t=PACK),
                     in_=src.rearrange("p t (c i) -> p c t i", i=4),
                 )
-            h_bf[half, b, 0] = dst
 
         def quant_h(half, b, j0, j1):
             codes = held([P, j1 - j0], U32, "h_codes%d%d_%d" % (half, b, j0))
@@ -282,10 +295,10 @@ def tile_list_codon_context_rate_kernel(
                     h_codes[half, b, a0, a1] = codes[:, a0 - j0 : a1 - j0]
                     h_plane[half, b, a0, a1] = plane[:, a0 - j0 : a1 - j0]
 
-        def stage_y(half, j0, j1, first_bank, shared_out=False):
+        def stage_y(half, j0, j1, shared_out=False):
             width = j1 - j0
             for c in range(N // P):
-                acc = bank(first_bank + c)
+                acc = next_bank()
                 for b in range(PASSES):
                     cols = slice(b * N + c * P, b * N + (c + 1) * P)
                     nc.tensor.matmul_mx(
@@ -312,37 +325,43 @@ def tile_list_codon_context_rate_kernel(
         cast_w2(1)
         quant_w2(0)
         gather_words("up", 0)
+        open_e(0, 0, pass_w2)
         gather_words("own", 0)
         deal_w1()
         deal_plane()
-        stage_e(0, 0, 0)
+        close_e(0, 0, pass_w1)
         gather_words("up", 1)
+        open_e(1, 0, pass_w2)
         gather_words("own", 1)
-        stage_e(1, 0, 1)
+        close_e(1, 0, pass_w1)
         quant_w2(1)
-        stage_e(0, 1, 0)
+        stage_e(0, 1)
         gather_late_plane(0)
         gather_words("down", 0)
         deal_w3()
         gather_late_plane(1)
         gather_words("down", 1)
         cast_w4(0)
-
-        stage_d(0, 0)
-        weave(0, 0)
-        stage_e(*LAST, 0)
-        for t in range(PACK):
-            stage_d(0, 1, (t,))
-            stage_last_d(t)
-        weave(0, 1)
-        stage_d(1, 0)
         cast_w4(1)
-        weave(1, 0)
+
+        stage_e(*LAST, (0, 1))
+        stage_d(0, 0, (0, 1))
+        for t in (2, 3):
+            stage_e(*LAST, (t,))
+            stage_d(0, 0, (t,))
+        weave(0, 0, "gpsimd")
+        stage_d(0, 1)
+        weave(0, 1, "gpsimd", 0, BANK // 2)
+        stage_d(1, 0)
+        for t in range(PACK):
+            stage_last_d(t)
+        weave(0, 1, "scalar", BANK // 2, BANK)
+        weave(1, 0, "scalar")
 
         quant_h(0, 0, 0, BANK)
         quant_w4()
         quant_h(0, 1, 0, BANK)
-        stage_y(0, 0, BANK, 0)
+        stage_y(0, 0, BANK)
         multiply_last(*TAIL[0])
         multiply_last(*TAIL[1])
         quant_h(1, 0, 0, BANK)
@@ -351,4 +370,4 @@ def tile_list_codon_context_rate_kernel(
         quant_h(*LAST, *TAIL[1])
         quant_h(*LAST, *TAIL[2])
         for n, piece in enumerate(TAIL):
-            stage_y(1, *piece, 2 + 2 * n, shared_out=(n == len(TAIL) - 1))
+            stage_y(1, *piece, shared_out=(n == len(TAIL) - 1))

@@ -34,8 +34,8 @@ RAW_AT = ROW_AT + WORDS - BANK
 BF1_AT = 18 * WORDS
 
 
-def load_scale_rows(nc, plane, rows, first, which=range(4)):
-    for r in which:
+def load_scale_rows(nc, plane, rows, first):
+    for r in range(4):
         nc.sync.dma_start(
             out=plane[first + r : P : 32, :].bitcast(I32),
             in_=rows[r:16:4, :].bitcast(I32),
@@ -93,12 +93,11 @@ def tile_list_codon_context_rate_kernel(
         nc.sync.dma_start(out=w2_raw[0][:], in_=w2_rows[:, :, 0:BANK])
         nc.sync.dma_start(out=tab[:], in_=tab_words[0].rearrange("p t i -> p (t i)").bitcast(I32))
         load_scale_rows(nc, w_plane_raw, w1_scales[0], 0)
-        nc.sync.dma_start(out=w1_raw.bitcast(I32), in_=w1_words[0].bitcast(I32))
-        load_scale_rows(nc, w_plane_raw, w3_scales[0], W3_ROW, (0,))
         nc.sync.dma_start(out=w2_raw[1][:], in_=w2_rows[:, :, BANK : 2 * BANK])
-        load_scale_rows(nc, w_plane_raw, w3_scales[0], W3_ROW, (1, 2, 3))
-        nc.sync.dma_start(out=w3_raw[:], in_=w3_words[0].rearrange("p c i -> p (c i)").bitcast(I32))
+        nc.sync.dma_start(out=w1_raw.bitcast(I32), in_=w1_words[0].bitcast(I32))
+        load_scale_rows(nc, w_plane_raw, w3_scales[0], W3_ROW)
         load_bias(nc, b1_sb, b1)
+        nc.sync.dma_start(out=w3_raw[:], in_=w3_words[0].rearrange("p c i -> p (c i)").bitcast(I32))
         load_bias(nc, b3_sb, b3)
         w4_rows = w4.rearrange("(b g t v) n -> b v g t n", b=PASSES, t=PACK, v=2)
         for b in range(PASSES):

@@ -350,11 +350,10 @@ def tile_list_codon_context_rate_kernel(
             stage_d(0, 0, (t,))
         weave(0, 0, "gpsimd")
         stage_d(0, 1)
-        weave(0, 1, "gpsimd", 0, BANK // 2)
         stage_d(1, 0)
         for t in range(PACK):
             stage_last_d(t)
-        weave(0, 1, "scalar", BANK // 2, BANK)
+        weave(0, 1, "scalar")
         weave(1, 0, "scalar")
 
         quant_h(0, 0, 0, BANK)

@@ -135,7 +135,7 @@ def tile_list_codon_context_rate_kernel(
             picked["words", name, half] = dst[:]
 
         w_plane = held([P, H], U8, "w_plane")
-        w3_dealt = placed([P, H], I32, "w3_dealt", W3_AT)
+        w3_dealt = [placed([P, BANK], I32, "w3_dealt%d" % b, at) for b, at in enumerate((W3_AT, TAB_AT + 2 * WORDS))]
         w1_dealt = held([P, 2 * H], U8, "w1_dealt")
 
         def deal_plane():
@@ -144,10 +144,11 @@ def tile_list_codon_context_rate_kernel(
                 in_=w_plane_raw.bitcast(U16).rearrange("p (c i t) -> p c t i", t=PACK, i=8),
             )
 
-        def deal_w3():
-            nc.vector.tensor_copy(
-                out=w3_dealt[:].rearrange("p (t c i v) -> p c t i v", t=PACK, i=2, v=2),
-                in_=w3_raw[:].rearrange("p (c i t v) -> p c t i v", t=PACK, i=2, v=2),
+        def deal_w3(b):
+            engine = nc.gpsimd if b else nc.vector
+            engine.tensor_copy(
+                out=w3_dealt[b][:].rearrange("p (t c i v) -> p c t i v", t=PACK, i=2, v=2),
+                in_=w3_raw[:, b * BANK : (b + 1) * BANK].rearrange("p (c i t v) -> p c t i v", t=PACK, i=2, v=2),
             )
 
         def deal_w1():
@@ -236,7 +237,7 @@ def tile_list_codon_context_rate_kernel(
             cols = slice(t * M + b * P, t * M + (b + 1) * P)
             nc.tensor.matmul_mx(
                 out=acc[:],
-                lhsT=w3_dealt[:, cols].bitcast(FP8X4),
+                lhsT=w3_dealt[b][:, t * P : (t + 1) * P].bitcast(FP8X4),
                 lhsT_scale=w_plane[W3_ROW:P, cols],
                 rhs=picked["words", "down", half].bitcast(FP8X4),
                 rhs_scale=picked["plane", "down", half],
@@ -262,7 +263,8 @@ def tile_list_codon_context_rate_kernel(
             nc.scalar.activation(last_down[:, t, :], acc[:], ACT.Identity, bias=b3_sb[:, LAST[1], 2 * t : 2 * t + 1])
 
         def multiply_last(j0, j1):
-            dst = held([P, (j1 - j0) * PACK], BF16, "h_bf11_%d" % j0)
+            at = W3_AT + 3 * BANK if j0 == 0 else BF1_AT + 2 * PACK * j0
+            dst = placed([P, (j1 - j0) * PACK], BF16, "h_bf11_%d" % j0, at)
             nc.vector.tensor_tensor(
                 out=dst[:].rearrange("p (c i t) -> p c t i", i=2, t=PACK),
                 in0=rate[LAST][:, :, j0:j1].rearrange("p t (c i) -> p c t i", i=2),
@@ -337,9 +339,10 @@ def tile_list_codon_context_rate_kernel(
         stage_e(0, 1)
         gather_late_plane(0)
         gather_words("down", 0)
-        deal_w3()
+        deal_w3(0)
         gather_late_plane(1)
         gather_words("down", 1)
+        deal_w3(1)
         cast_w4(0)
         cast_w4(1)
 
@@ -350,10 +353,11 @@ def tile_list_codon_context_rate_kernel(
             stage_d(0, 0, (t,))
         weave(0, 0, "gpsimd")
         stage_d(0, 1)
-        stage_d(1, 0)
         for t in range(PACK):
             stage_last_d(t)
-        weave(0, 1, "scalar")
+        weave(0, 1, "gpsimd", 0, BANK // 4)
+        weave(0, 1, "scalar", BANK // 4, BANK)
+        stage_d(1, 0)
         weave(1, 0, "scalar")
 
         quant_h(0, 0, 0, BANK)

@@ -123,7 +123,8 @@ def tile_list_codon_context_rate_kernel(
                 picked["plane", name, half] = dst[:, half * BANK : (half + 1) * BANK]
 
         def gather_late_plane(half):
-            dst = placed([P, BANK], U8, "plane_down%d" % half, ROW_AT + WORDS + half * BANK)
+            label = "plane_down%d" % half
+            dst = placed([P, BANK], U8, label, ROW_AT + WORDS) if half else held([P, BANK], U8, label)
             entries = lists["down"][:, half * BANK // 16 : (half + 1) * BANK // 16]
             nc.vector.tensor_copy(dst[:], tab_plane[:].indirect(entries))
             picked["plane", "down", half] = dst[:]
@@ -322,6 +323,7 @@ def tile_list_codon_context_rate_kernel(
 
         for name in ("up", "own"):
             gather_plane(name)
+        gather_late_plane(0)
         cast_w2(0)
         cast_w2(1)
         quant_w2(0)
@@ -337,7 +339,6 @@ def tile_list_codon_context_rate_kernel(
         close_e(1, 0, pass_w1)
         quant_w2(1)
         stage_e(0, 1)
-        gather_late_plane(0)
         gather_words("down", 0)
         deal_w3(0)
         gather_late_plane(1)

@@ -80,24 +80,37 @@ def tile_list_codon_context_rate_kernel(
         lists = {name: keep.tile([P, S // 16], U16, name="list_" + name) for name in ("down", "up", "own")}
         w2_rows = w2.rearrange("(p i) c -> p i c", i=PACK)
         tab = placed([P, T], I32, "tab", TAB_AT)
-        w3_raw = held([P, H], I32, "w3_raw")
+        w3_raw = [held([P, BANK], I32, "w3_raw%d" % b) for b in range(PASSES)]
         b1_sb = held([P, PASSES, 2 * PACK], F32, "b1_sb")
         b3_sb = held([P, PASSES, 2 * PACK], F32, "b3_sb")
         b4_sb = held([P, N // P], F32, "b4_sb")
-        w2_raw = [placed([P, PACK, BANK], F32, "w2_raw%d" % b, W2_AT[b]) for b in range(PASSES)]
+        w2_raw = {
+            (b, u): placed([P, PACK, BANK // 2], F32, "w2_raw%d%d" % (b, u), W2_AT[b] + 2 * u * WORDS)
+            for b in range(PASSES)
+            for u in range(2)
+        }
+
+        def load_w2(b, pieces=range(2)):
+            for u in pieces:
+                c0 = b * BANK + u * BANK // 2
+                nc.sync.dma_start(out=w2_raw[b, u][:], in_=w2_rows[:, :, c0 : c0 + BANK // 2])
+
         w4_raw = [held([P, PACK, N], F32, "w4_raw%d" % b) for b in range(PASSES)]
 
         for name, src in (("up", offs2), ("own", offs), ("down", offs3)):
             nc.sync.dma_start(lists[name][:], src)
         load_scale_rows(nc, tab_plane, tab_scales[0], 0)
-        nc.sync.dma_start(out=w2_raw[0][:], in_=w2_rows[:, :, 0:BANK])
+        load_w2(0)
         nc.sync.dma_start(out=tab[:], in_=tab_words[0].rearrange("p t i -> p (t i)").bitcast(I32))
         load_scale_rows(nc, w_plane_raw, w1_scales[0], 0)
-        nc.sync.dma_start(out=w2_raw[1][:], in_=w2_rows[:, :, BANK : 2 * BANK])
+        load_w2(1, (0,))
         nc.sync.dma_start(out=w1_raw.bitcast(I32), in_=w1_words[0].bitcast(I32))
         load_scale_rows(nc, w_plane_raw, w3_scales[0], W3_ROW)
+        load_w2(1, (1,))
+        w3_cols = w3_words[0].rearrange("p c i -> p (c i)").bitcast(I32)
+        nc.sync.dma_start(out=w3_raw[0][:], in_=w3_cols[:, 0:BANK])
         load_bias(nc, b1_sb, b1)
-        nc.sync.dma_start(out=w3_raw[:], in_=w3_words[0].rearrange("p c i -> p (c i)").bitcast(I32))
+        nc.sync.dma_start(out=w3_raw[1][:], in_=w3_cols[:, BANK : 2 * BANK])
         load_bias(nc, b3_sb, b3)
         w4_rows = w4.rearrange("(b g t v) n -> b v g t n", b=PASSES, t=PACK, v=2)
         for b in range(PASSES):
@@ -107,12 +120,12 @@ def tile_list_codon_context_rate_kernel(
             nc.sync.dma_start(out=b4_sb[:], in_=b4.rearrange("(c p) -> p c", p=P))
 
         words_at = {
-            ("up", 0): W2_AT[0],
-            ("own", 0): W2_AT[0] + WORDS,
+            ("up", 0): W2_AT[0] + 2 * WORDS,
+            ("own", 0): W2_AT[0] + 3 * WORDS,
             ("up", 1): ROW_AT,
-            ("own", 1): ROW_AT + WORDS + 3 * BANK,
-            ("down", 0): BF1_AT,
-            ("down", 1): BF1_AT + WORDS,
+            ("own", 1): ROW_AT + WORDS,
+            ("down", 0): W2_AT[1] + 2 * WORDS - BANK,
+            ("down", 1): W2_AT[1] + 3 * WORDS,
         }
         picked = {}
 
@@ -124,7 +137,7 @@ def tile_list_codon_context_rate_kernel(
 
         def gather_late_plane(half):
             label = "plane_down%d" % half
-            dst = placed([P, BANK], U8, label, ROW_AT + WORDS) if half else held([P, BANK], U8, label)
+            dst = placed([P, BANK], U8, label, W2_AT[1] + 3 * WORDS - BANK) if half else held([P, BANK], U8, label)
             entries = lists["down"][:, half * BANK // 16 : (half + 1) * BANK // 16]
             nc.vector.tensor_copy(dst[:], tab_plane[:].indirect(entries))
             picked["plane", "down", half] = dst[:]
@@ -149,7 +162,7 @@ def tile_list_codon_context_rate_kernel(
             engine = nc.gpsimd if b else nc.vector
             engine.tensor_copy(
                 out=w3_dealt[b][:].rearrange("p (t c i v) -> p c t i v", t=PACK, i=2, v=2),
-                in_=w3_raw[:, b * BANK : (b + 1) * BANK].rearrange("p (c i t v) -> p c t i v", t=PACK, i=2, v=2),
+                in_=w3_raw[b][:].rearrange("p (c i t v) -> p c t i v", t=PACK, i=2, v=2),
             )
 
         def deal_w1():
@@ -158,17 +171,18 @@ def tile_list_codon_context_rate_kernel(
                 in_=w1_raw.bitcast(I32).rearrange("p (c i t) -> p c t i", t=PACK, i=4),
             )
 
-        w2_bf = [held([P, BANK * PACK], BF16, "w2_bf0"), placed([P, BANK * PACK], BF16, "w2_bf1", BF1_AT)]
+        w2_bf = [held([P, BANK * PACK], BF16, "w2_bf0"), held([P, BANK * PACK], BF16, "w2_bf1")]
         w2_codes = [held([P, BANK], U32, "w2_codes%d" % b) for b in range(PASSES)]
-        w2_plane = [held([P, BANK], U8, "w2_plane0"), placed([P, BANK], U8, "w2_plane1", ROW_AT + WORDS + 2 * BANK)]
+        w2_plane = {}
 
         def cast_w2(b):
-            nc.scalar.copy(
-                out=w2_bf[b][:].rearrange("p (t g v i) -> p g t i v", t=PACK, v=2, i=PACK),
-                in_=w2_raw[b][:].rearrange("p i (g t v) -> p g t i v", t=PACK, v=2),
-            )
+            dst = w2_bf[b][:].rearrange("p (t u g v i) -> p u g t i v", t=PACK, u=2, v=2, i=PACK)
+            for u in range(2):
+                nc.scalar.copy(out=dst[:, u], in_=w2_raw[b, u][:].rearrange("p i (g t v) -> p g t i v", t=PACK, v=2))
 
         def quant_w2(b):
+            label = "w2_plane%d" % b
+            w2_plane[b] = held([P, BANK], U8, label)
             nc.vector.quantize_mx(out=w2_codes[b][:].bitcast(FP8X4), scales=w2_plane[b][:], in_=w2_bf[b][:])
 
         w4_bf = placed([P, PASSES * N * PACK], BF16, "w4_bf", TAB_AT)
@@ -264,7 +278,7 @@ def tile_list_codon_context_rate_kernel(
             nc.scalar.activation(last_down[:, t, :], acc[:], ACT.Identity, bias=b3_sb[:, LAST[1], 2 * t : 2 * t + 1])
 
         def multiply_last(j0, j1):
-            at = W3_AT + 3 * BANK if j0 == 0 else BF1_AT + 2 * PACK * j0
+            at = W3_AT + 3 * BANK if j0 == 0 else W2_AT[1] + 2 * WORDS + 2 * PACK * j0
             dst = placed([P, (j1 - j0) * PACK], BF16, "h_bf11_%d" % j0, at)
             nc.vector.tensor_tensor(
                 out=dst[:].rearrange("p (c i t) -> p c t i", i=2, t=PACK),

@@ -28,7 +28,7 @@ W3_ROW = 4
 WORDS = 4 * BANK
 W2_AT = (0, 4 * WORDS)
 TAB_AT = 8 * WORDS
-W3_AT = 12 * WORDS
+W3_AT = 18 * WORDS
 ROW_AT = 14 * WORDS
 RAW_AT = ROW_AT + WORDS - BANK
 BF1_AT = 18 * WORDS
@@ -100,11 +100,12 @@ def tile_list_codon_context_rate_kernel(
         for name, src in (("up", offs2), ("own", offs), ("down", offs3)):
             nc.sync.dma_start(lists[name][:], src)
         load_scale_rows(nc, tab_plane, tab_scales[0], 0)
-        load_w2(0)
+        load_w2(0, (0,))
         nc.sync.dma_start(out=tab[:], in_=tab_words[0].rearrange("p t i -> p (t i)").bitcast(I32))
+        load_w2(0, (1,))
         load_scale_rows(nc, w_plane_raw, w1_scales[0], 0)
-        load_w2(1, (0,))
         nc.sync.dma_start(out=w1_raw.bitcast(I32), in_=w1_words[0].bitcast(I32))
+        load_w2(1, (0,))
         load_scale_rows(nc, w_plane_raw, w3_scales[0], W3_ROW)
         load_w2(1, (1,))
         w3_cols = w3_words[0].rearrange("p c i -> p (c i)").bitcast(I32)
@@ -120,27 +121,20 @@ def tile_list_codon_context_rate_kernel(
             nc.sync.dma_start(out=b4_sb[:], in_=b4.rearrange("(c p) -> p c", p=P))
 
         words_at = {
-            ("up", 0): W2_AT[0] + 2 * WORDS,
-            ("own", 0): W2_AT[0] + 3 * WORDS,
+            ("up", 0): W2_AT[0],
+            ("own", 0): W2_AT[0] + WORDS,
             ("up", 1): ROW_AT,
             ("own", 1): ROW_AT + WORDS,
-            ("down", 0): W2_AT[1] + 2 * WORDS - BANK,
+            ("down", 0): W2_AT[1] + 2 * WORDS - 2 * BANK,
             ("down", 1): W2_AT[1] + 3 * WORDS,
         }
         picked = {}
 
-        def gather_plane(name):
-            dst = held([P, S], U8, "plane_%s0" % name)
+        def gather_plane(name, at=None):
+            dst = held([P, S], U8, "plane_" + name) if at is None else placed([P, S], U8, "plane_" + name, at)
             nc.vector.tensor_copy(dst[:], tab_plane[:].indirect(lists[name][:]))
             for half in range(S // BANK):
                 picked["plane", name, half] = dst[:, half * BANK : (half + 1) * BANK]
-
-        def gather_late_plane(half):
-            label = "plane_down%d" % half
-            dst = placed([P, BANK], U8, label, W2_AT[1] + 3 * WORDS - BANK) if half else held([P, BANK], U8, label)
-            entries = lists["down"][:, half * BANK // 16 : (half + 1) * BANK // 16]
-            nc.vector.tensor_copy(dst[:], tab_plane[:].indirect(entries))
-            picked["plane", "down", half] = dst[:]
 
         def gather_words(name, half):
             dst = placed([P, BANK], U32, "words_%s%d" % (name, half), words_at[name, half])
@@ -149,7 +143,7 @@ def tile_list_codon_context_rate_kernel(
             picked["words", name, half] = dst[:]
 
         w_plane = held([P, H], U8, "w_plane")
-        w3_dealt = [placed([P, BANK], I32, "w3_dealt%d" % b, at) for b, at in enumerate((W3_AT, TAB_AT + 2 * WORDS))]
+        w3_dealt = [placed([P, BANK], I32, "w3_dealt%d" % b, at) for b, at in enumerate((W3_AT, W3_AT + WORDS))]
         w1_dealt = held([P, 2 * H], U8, "w1_dealt")
 
         def deal_plane():
@@ -159,7 +153,7 @@ def tile_list_codon_context_rate_kernel(
             )
 
         def deal_w3(b):
-            engine = nc.gpsimd if b else nc.vector
+            engine = nc.gpsimd
             engine.tensor_copy(
                 out=w3_dealt[b][:].rearrange("p (t c i v) -> p c t i v", t=PACK, i=2, v=2),
                 in_=w3_raw[b][:].rearrange("p (c i t v) -> p c t i v", t=PACK, i=2, v=2),
@@ -171,7 +165,7 @@ def tile_list_codon_context_rate_kernel(
                 in_=w1_raw.bitcast(I32).rearrange("p (c i t) -> p c t i", t=PACK, i=4),
             )
 
-        w2_bf = [held([P, BANK * PACK], BF16, "w2_bf0"), held([P, BANK * PACK], BF16, "w2_bf1")]
+        w2_bf = [held([P, BANK * PACK], BF16, "w2_bf0"), placed([P, BANK * PACK], BF16, "w2_bf1", BF1_AT)]
         w2_codes = [held([P, BANK], U32, "w2_codes%d" % b) for b in range(PASSES)]
         w2_plane = {}
 
@@ -337,13 +331,12 @@ def tile_list_codon_context_rate_kernel(
 
         for name in ("up", "own"):
             gather_plane(name)
-        gather_late_plane(0)
         cast_w2(0)
         cast_w2(1)
-        quant_w2(0)
         gather_words("up", 0)
-        open_e(0, 0, pass_w2)
         gather_words("own", 0)
+        quant_w2(0)
+        open_e(0, 0, pass_w2)
         deal_w1()
         deal_plane()
         close_e(0, 0, pass_w1)
@@ -353,9 +346,9 @@ def tile_list_codon_context_rate_kernel(
         close_e(1, 0, pass_w1)
         quant_w2(1)
         stage_e(0, 1)
-        gather_words("down", 0)
         deal_w3(0)
-        gather_late_plane(1)
+        gather_words("down", 0)
+        gather_plane("down", W2_AT[1] + 3 * WORDS - 2 * BANK)
         gather_words("down", 1)
         deal_w3(1)
         cast_w4(0)
@@ -381,8 +374,8 @@ def tile_list_codon_context_rate_kernel(
         stage_y(0, 0, BANK)
         multiply_last(*TAIL[0])
         multiply_last(*TAIL[1])
-        quant_h(1, 0, 0, BANK)
         quant_h(*LAST, *TAIL[0])
+        quant_h(1, 0, 0, BANK)
         multiply_last(*TAIL[2])
         quant_h(*LAST, *TAIL[1])
         quant_h(*LAST, *TAIL[2])

@@ -18,20 +18,23 @@ ALU = mybir.AluOpType
 
 P = 128
 PACK = 4
+PAIR = 2
 BANK = 512
+BANKS = 8
 PASSES = H // (P * PACK)
 M = H // PACK
+PIECE = BANK // 2
 LAST = (1, 1)
 TAIL = ((0, 256), (256, 384), (384, 512))
+GPSIMD_SITES = 256
 W3_ROW = 4
 
 WORDS = 4 * BANK
 W2_AT = (0, 4 * WORDS)
-TAB_AT = 8 * WORDS
-W3_AT = 18 * WORDS
-ROW_AT = 14 * WORDS
-RAW_AT = ROW_AT + WORDS - BANK
-BF1_AT = 18 * WORDS
+LAST_PIECE_AT = W2_AT[1] + 2 * WORDS
+ROW_AT = 8 * WORDS
+RAW_AT = ROW_AT + WORDS - BANK // 2
+W3_AT = 12 * WORDS
 
 
 def load_scale_rows(nc, plane, rows, first):
@@ -43,9 +46,10 @@ def load_scale_rows(nc, plane, rows, first):
 
 
 def load_bias(nc, dst, bias):
-    runs = bias.rearrange("(b g e) -> g b e", b=PASSES, e=2 * PACK)
-    for v in range(2):
-        nc.sync.dma_start(out=dst[v:P:2, :, 0 : 2 * PACK - 1], in_=runs[:, :, v : v + 2 * PACK - 1])
+    runs = bias.rearrange("(b g e) -> g b e", b=PASSES, e=PAIR * PACK)
+    width = PAIR * PACK - 1
+    for v in range(PAIR):
+        nc.sync.dma_start(out=dst[v:P:PAIR, :, 0:width], in_=runs[:, :, v : v + width])
 
 
 def tile_list_codon_context_rate_kernel(
@@ -66,7 +70,7 @@ def tile_list_codon_context_rate_kernel(
         taken = []
 
         def next_bank():
-            n = len(taken) % 8
+            n = len(taken) % BANKS
             taken.append(n)
             return psum.tile([P, BANK], F32, name="bank%d" % n, tag="bank%d" % n)
 
@@ -79,54 +83,53 @@ def tile_list_codon_context_rate_kernel(
 
         lists = {name: keep.tile([P, S // 16], U16, name="list_" + name) for name in ("down", "up", "own")}
         w2_rows = w2.rearrange("(p i) c -> p i c", i=PACK)
-        tab = placed([P, T], I32, "tab", TAB_AT)
+        tab = held([P, T], I32, "tab")
         w3_raw = [held([P, BANK], I32, "w3_raw%d" % b) for b in range(PASSES)]
-        b1_sb = held([P, PASSES, 2 * PACK], F32, "b1_sb")
-        b3_sb = held([P, PASSES, 2 * PACK], F32, "b3_sb")
+        b1_sb = held([P, PASSES, PAIR * PACK], F32, "b1_sb")
+        b3_sb = held([P, PASSES, PAIR * PACK], F32, "b3_sb")
         b4_sb = held([P, N // P], F32, "b4_sb")
         w2_raw = {
-            (b, u): placed([P, PACK, BANK // 2], F32, "w2_raw%d%d" % (b, u), W2_AT[b] + 2 * u * WORDS)
+            (b, u): placed([P, PACK, PIECE], F32, "w2_raw%d%d" % (b, u), W2_AT[b] + 2 * u * WORDS)
             for b in range(PASSES)
             for u in range(2)
         }
 
-        def load_w2(b, pieces=range(2)):
-            for u in pieces:
-                c0 = b * BANK + u * BANK // 2
-                nc.sync.dma_start(out=w2_raw[b, u][:], in_=w2_rows[:, :, c0 : c0 + BANK // 2])
+        def load_w2(b, u):
+            c0 = b * BANK + u * PIECE
+            nc.sync.dma_start(out=w2_raw[b, u][:], in_=w2_rows[:, :, c0 : c0 + PIECE])
 
         w4_raw = [held([P, PACK, N], F32, "w4_raw%d" % b) for b in range(PASSES)]
 
-        for name, src in (("up", offs2), ("own", offs), ("down", offs3)):
+        for name, src in (("own", offs), ("up", offs2), ("down", offs3)):
             nc.sync.dma_start(lists[name][:], src)
         load_scale_rows(nc, tab_plane, tab_scales[0], 0)
-        load_w2(0, (0,))
+        load_w2(0, 0)
         nc.sync.dma_start(out=tab[:], in_=tab_words[0].rearrange("p t i -> p (t i)").bitcast(I32))
-        load_w2(0, (1,))
         load_scale_rows(nc, w_plane_raw, w1_scales[0], 0)
         nc.sync.dma_start(out=w1_raw.bitcast(I32), in_=w1_words[0].bitcast(I32))
-        load_w2(1, (0,))
+        load_w2(0, 1)
         load_scale_rows(nc, w_plane_raw, w3_scales[0], W3_ROW)
-        load_w2(1, (1,))
+        load_w2(1, 0)
+        load_w2(1, 1)
         w3_cols = w3_words[0].rearrange("p c i -> p (c i)").bitcast(I32)
         nc.sync.dma_start(out=w3_raw[0][:], in_=w3_cols[:, 0:BANK])
         load_bias(nc, b1_sb, b1)
         nc.sync.dma_start(out=w3_raw[1][:], in_=w3_cols[:, BANK : 2 * BANK])
         load_bias(nc, b3_sb, b3)
-        w4_rows = w4.rearrange("(b g t v) n -> b v g t n", b=PASSES, t=PACK, v=2)
+        w4_rows = w4.rearrange("(b g t v) n -> b v g t n", b=PASSES, t=PACK, v=PAIR)
         for b in range(PASSES):
-            for v in range(2):
-                nc.sync.dma_start(out=w4_raw[b][v:P:2], in_=w4_rows[b, v])
+            for v in range(PAIR):
+                nc.sync.dma_start(out=w4_raw[b][v:P:PAIR], in_=w4_rows[b, v])
         with nc.allow_non_contiguous_dma(reason="one bias value a partition"):
             nc.sync.dma_start(out=b4_sb[:], in_=b4.rearrange("(c p) -> p c", p=P))
 
         words_at = {
-            ("up", 0): W2_AT[0],
-            ("own", 0): W2_AT[0] + WORDS,
-            ("up", 1): ROW_AT,
-            ("own", 1): ROW_AT + WORDS,
-            ("down", 0): W2_AT[1] + 2 * WORDS - 2 * BANK,
-            ("down", 1): W2_AT[1] + 3 * WORDS,
+            ("own", 0): W2_AT[0],
+            ("up", 0): ROW_AT,
+            ("own", 1): ROW_AT + WORDS + BANK,
+            ("up", 1): ROW_AT + 2 * WORDS + BANK,
+            ("down", 0): LAST_PIECE_AT - S,
+            ("down", 1): LAST_PIECE_AT + WORDS,
         }
         picked = {}
 
@@ -143,7 +146,7 @@ def tile_list_codon_context_rate_kernel(
             picked["words", name, half] = dst[:]
 
         w_plane = held([P, H], U8, "w_plane")
-        w3_dealt = [placed([P, BANK], I32, "w3_dealt%d" % b, at) for b, at in enumerate((W3_AT, W3_AT + WORDS))]
+        w3_dealt = [placed([P, BANK], I32, "w3_dealt%d" % b, W3_AT + b * WORDS) for b in range(PASSES)]
         w1_dealt = held([P, 2 * H], U8, "w1_dealt")
 
         def deal_plane():
@@ -153,10 +156,9 @@ def tile_list_codon_context_rate_kernel(
             )
 
         def deal_w3(b):
-            engine = nc.gpsimd
-            engine.tensor_copy(
-                out=w3_dealt[b][:].rearrange("p (t c i v) -> p c t i v", t=PACK, i=2, v=2),
-                in_=w3_raw[b][:].rearrange("p (c i t v) -> p c t i v", t=PACK, i=2, v=2),
+            nc.gpsimd.tensor_copy(
+                out=w3_dealt[b][:].rearrange("p (t c i v) -> p c t i v", t=PACK, i=2, v=PAIR),
+                in_=w3_raw[b][:].rearrange("p (c i t v) -> p c t i v", t=PACK, i=2, v=PAIR),
             )
 
         def deal_w1():
@@ -165,28 +167,28 @@ def tile_list_codon_context_rate_kernel(
                 in_=w1_raw.bitcast(I32).rearrange("p (c i t) -> p c t i", t=PACK, i=4),
             )
 
-        w2_bf = [held([P, BANK * PACK], BF16, "w2_bf0"), placed([P, BANK * PACK], BF16, "w2_bf1", BF1_AT)]
+        w2_bf = [held([P, BANK * PACK], BF16, "w2_bf0"), placed([P, BANK * PACK], BF16, "w2_bf1", W3_AT)]
         w2_codes = [held([P, BANK], U32, "w2_codes%d" % b) for b in range(PASSES)]
         w2_plane = {}
 
         def cast_w2(b):
-            dst = w2_bf[b][:].rearrange("p (t u g v i) -> p u g t i v", t=PACK, u=2, v=2, i=PACK)
+            dst = w2_bf[b][:].rearrange("p (t u g v i) -> p u g t i v", t=PACK, u=2, v=PAIR, i=PACK)
             for u in range(2):
-                nc.scalar.copy(out=dst[:, u], in_=w2_raw[b, u][:].rearrange("p i (g t v) -> p g t i v", t=PACK, v=2))
+                nc.scalar.copy(out=dst[:, u], in_=w2_raw[b, u][:].rearrange("p i (g t v) -> p g t i v", t=PACK, v=PAIR))
 
         def quant_w2(b):
             label = "w2_plane%d" % b
-            w2_plane[b] = held([P, BANK], U8, label)
+            w2_plane[b] = held([P, BANK], U8, label) if b else placed([P, BANK], U8, label, ROW_AT + WORDS)
             nc.vector.quantize_mx(out=w2_codes[b][:].bitcast(FP8X4), scales=w2_plane[b][:], in_=w2_bf[b][:])
 
-        w4_bf = placed([P, PASSES * N * PACK], BF16, "w4_bf", TAB_AT)
+        w4_bf = held([P, PASSES * N * PACK], BF16, "w4_bf")
         w4_codes = held([P, PASSES * N], U32, "w4_codes")
         w4_plane = placed([P, PASSES * N], U8, "w4_plane", W3_AT + PASSES * BANK)
 
         def cast_w4(b):
             dst = w4_bf[:, b * N * PACK : (b + 1) * N * PACK]
             nc.gpsimd.tensor_copy(
-                out=dst.rearrange("p (n i) -> p n i", i=PACK), in_=w4_raw[b][:].rearrange("p i n -> p n i")
+                out=dst.rearrange("p (n t) -> p n t", t=PACK), in_=w4_raw[b][:].rearrange("p t n -> p n t")
             )
 
         def quant_w4():
@@ -234,7 +236,7 @@ def tile_list_codon_context_rate_kernel(
             for t in slices:
                 acc = opened[half, b, t]
                 closing(acc, half, b, t, False)
-                nc.scalar.activation(rate[half, b][:, t, :], acc[:], ACT.Exp, bias=b1_sb[:, b, 2 * t : 2 * t + 1])
+                nc.scalar.activation(rate[half, b][:, t, :], acc[:], ACT.Exp, bias=b1_sb[:, b, PAIR * t : PAIR * t + 1])
 
         def stage_e(half, b, slices=range(PACK)):
             for t in slices:
@@ -262,17 +264,17 @@ def tile_list_codon_context_rate_kernel(
             for t in slices:
                 acc = product_d(half, b, t)
                 nc.vector.scalar_tensor_tensor(
-                    dst[:, t, :], acc[:], b3_sb[:, b, 2 * t : 2 * t + 1], rate[half, b][:, t, :], ALU.add, ALU.mult
+                    dst[:, t, :], acc[:], b3_sb[:, b, PAIR * t : PAIR * t + 1], rate[half, b][:, t, :], ALU.add, ALU.mult
                 )
 
         last_down = held([P, PACK, BANK], F32, "last_down")
 
         def stage_last_d(t):
             acc = product_d(*LAST, t)
-            nc.scalar.activation(last_down[:, t, :], acc[:], ACT.Identity, bias=b3_sb[:, LAST[1], 2 * t : 2 * t + 1])
+            nc.scalar.activation(last_down[:, t, :], acc[:], ACT.Identity, bias=b3_sb[:, LAST[1], PAIR * t : PAIR * t + 1])
 
         def multiply_last(j0, j1):
-            at = W3_AT + 3 * BANK if j0 == 0 else W2_AT[1] + 2 * WORDS + 2 * PACK * j0
+            at = W3_AT + 3 * BANK if j0 == 0 else LAST_PIECE_AT + 2 * PACK * j0
             dst = placed([P, (j1 - j0) * PACK], BF16, "h_bf11_%d" % j0, at)
             nc.vector.tensor_tensor(
                 out=dst[:].rearrange("p (c i t) -> p c t i", i=2, t=PACK),
@@ -282,24 +284,28 @@ def tile_list_codon_context_rate_kernel(
             )
             h_bf[(*LAST, j0)] = dst
 
-        def weave(half, b, engine, j0=0, j1=BANK):
+        def weave_views(half, b, j0, j1):
             if (half, b, 0) not in h_bf:
                 h_bf[half, b, 0] = held([P, BANK * PACK], BF16, "h_bf%d%d_0" % (half, b))
-            dst = h_bf[half, b, 0][:, j0 * PACK : j1 * PACK]
-            src = h_slices[half, b][:, :, j0:j1]
-            if engine == "gpsimd":
-                nc.gpsimd.tensor_copy(out=dst.rearrange("p (c t) -> p c t", t=PACK), in_=src.rearrange("p t c -> p c t"))
-            else:
-                nc.scalar.copy(
-                    out=dst.rearrange("p (c i t) -> p c t i", i=4, t=PACK),
-                    in_=src.rearrange("p t (c i) -> p c t i", i=4),
-                )
+            return h_bf[half, b, 0][:, j0 * PACK : j1 * PACK], h_slices[half, b][:, :, j0:j1]
+
+        def weave_gpsimd(half, b, j0, j1):
+            dst, src = weave_views(half, b, j0, j1)
+            nc.gpsimd.tensor_copy(out=dst.rearrange("p (c t) -> p c t", t=PACK), in_=src.rearrange("p t c -> p c t"))
+
+        def weave_scalar(half, b, j0, j1):
+            dst, src = weave_views(half, b, j0, j1)
+            nc.scalar.copy(
+                out=dst.rearrange("p (c i t) -> p c t i", i=4, t=PACK),
+                in_=src.rearrange("p t (c i) -> p c t i", i=4),
+            )
 
         def quant_h(half, b, j0, j1):
+            src = h_bf[half, b, j0][:] if (half, b) == LAST else h_bf[half, b, 0][:, j0 * PACK : j1 * PACK]
             codes = held([P, j1 - j0], U32, "h_codes%d%d_%d" % (half, b, j0))
             label = "h_plane%d%d_%d" % (half, b, j0)
             plane = placed([P, BANK], U8, label, W3_AT + b * BANK) if half == 0 else held([P, j1 - j0], U8, label)
-            nc.vector.quantize_mx(out=codes[:].bitcast(FP8X4), scales=plane[:], in_=h_bf[half, b, j0][:])
+            nc.vector.quantize_mx(out=codes[:].bitcast(FP8X4), scales=plane[:], in_=src)
             for a0, a1 in ((0, BANK),) + TAIL:
                 if j0 <= a0 and a1 <= j1:
                     h_codes[half, b, a0, a1] = codes[:, a0 - j0 : a1 - j0]
@@ -329,26 +335,26 @@ def tile_list_codon_context_rate_kernel(
                     queue = nc.scalar if shared_out else nc.sync
                 queue.dma_start(out=out[c * P : (c + 1) * P, half * BANK + j0 : half * BANK + j1], in_=res[:])
 
-        for name in ("up", "own"):
+        for name in ("own", "up"):
             gather_plane(name)
         cast_w2(0)
         cast_w2(1)
-        gather_words("up", 0)
         gather_words("own", 0)
-        quant_w2(0)
-        open_e(0, 0, pass_w2)
         deal_w1()
         deal_plane()
-        close_e(0, 0, pass_w1)
-        gather_words("up", 1)
-        open_e(1, 0, pass_w2)
+        open_e(0, 0, pass_w1)
+        gather_words("up", 0)
+        quant_w2(0)
+        close_e(0, 0, pass_w2)
         gather_words("own", 1)
-        close_e(1, 0, pass_w1)
+        open_e(1, 0, pass_w1)
+        gather_words("up", 1)
+        close_e(1, 0, pass_w2)
         quant_w2(1)
         stage_e(0, 1)
         deal_w3(0)
         gather_words("down", 0)
-        gather_plane("down", W2_AT[1] + 3 * WORDS - 2 * BANK)
+        gather_plane("down", LAST_PIECE_AT + WORDS - S)
         gather_words("down", 1)
         deal_w3(1)
         cast_w4(0)
@@ -359,14 +365,16 @@ def tile_list_codon_context_rate_kernel(
         for t in (2, 3):
             stage_e(*LAST, (t,))
             stage_d(0, 0, (t,))
-        weave(0, 0, "gpsimd")
+        weave_gpsimd(0, 0, 0, BANK)
         stage_d(0, 1)
         for t in range(PACK):
             stage_last_d(t)
-        weave(0, 1, "gpsimd", 0, BANK // 4)
-        weave(0, 1, "scalar", BANK // 4, BANK)
+        weave_gpsimd(0, 1, 0, GPSIMD_SITES)
+        weave_scalar(0, 1, GPSIMD_SITES, BANK)
         stage_d(1, 0)
-        weave(1, 0, "scalar")
+        cut = TAIL[0][1]
+        weave_scalar(1, 0, 0, cut)
+        weave_scalar(1, 0, cut, BANK)
 
         quant_h(0, 0, 0, BANK)
         quant_w4()
@@ -375,9 +383,10 @@ def tile_list_codon_context_rate_kernel(
         multiply_last(*TAIL[0])
         multiply_last(*TAIL[1])
         quant_h(*LAST, *TAIL[0])
-        quant_h(1, 0, 0, BANK)
+        quant_h(1, 0, 0, cut)
         multiply_last(*TAIL[2])
         quant_h(*LAST, *TAIL[1])
+        quant_h(1, 0, cut, BANK)
         quant_h(*LAST, *TAIL[2])
-        for n, piece in enumerate(TAIL):
-            stage_y(1, *piece, shared_out=(n == len(TAIL) - 1))
+        for piece in TAIL:
+            stage_y(1, *piece, shared_out=(piece == TAIL[-1]))

@@ -27,20 +27,20 @@ PIECE = BANK // 2
 LAST = (1, 1)
 TAIL = ((0, 256), (256, 384), (384, 512))
 GPSIMD_SITES = 256
-W3_ROW = 4
 
 WORDS = 4 * BANK
 W2_AT = (0, 4 * WORDS)
 LAST_PIECE_AT = W2_AT[1] + 2 * WORDS
-ROW_AT = 8 * WORDS
-RAW_AT = ROW_AT + WORDS - BANK // 2
+W3_PLANE_AT = 8 * WORDS
+ROW_AT = W3_PLANE_AT + H
+W2_BF_AT = ROW_AT - 64
 W3_AT = 12 * WORDS
 
 
-def load_scale_rows(nc, plane, rows, first):
+def load_scale_rows(nc, plane, rows):
     for r in range(4):
         nc.sync.dma_start(
-            out=plane[first + r : P : 32, :].bitcast(I32),
+            out=plane[r:P:32, :].bitcast(I32),
             in_=rows[r:16:4, :].bitcast(I32),
         )
 
@@ -76,10 +76,10 @@ def tile_list_codon_context_rate_kernel(
 
         tab_plane = held([P, T], U8, "tab_plane")
         nc.gpsimd.memset(tab_plane[:].bitcast(I32), 0)
-        raw = placed([P, 3 * H], U8, "raw", RAW_AT)
-        w1_raw = raw[:, 0 : 2 * H]
-        w_plane_raw = raw[:, 2 * H : 3 * H]
-        nc.vector.memset(w_plane_raw.bitcast(I32), 0)
+        w1_raw = held([P, 2 * H], U8, "w1_raw")
+        plane_raw = {name: held([P, H], U8, name + "_plane_raw")[:] for name in ("w1", "w3")}
+        for raw in plane_raw.values():
+            nc.vector.memset(raw.bitcast(I32), 0)
 
         lists = {name: keep.tile([P, S // 16], U16, name="list_" + name) for name in ("down", "up", "own")}
         w2_rows = w2.rearrange("(p i) c -> p i c", i=PACK)
@@ -102,14 +102,14 @@ def tile_list_codon_context_rate_kernel(
 
         for name, src in (("own", offs), ("up", offs2), ("down", offs3)):
             nc.sync.dma_start(lists[name][:], src)
-        load_scale_rows(nc, tab_plane, tab_scales[0], 0)
+        load_scale_rows(nc, tab_plane, tab_scales[0])
         load_w2(0, 0)
         nc.sync.dma_start(out=tab[:], in_=tab_words[0].rearrange("p t i -> p (t i)").bitcast(I32))
-        load_scale_rows(nc, w_plane_raw, w1_scales[0], 0)
-        nc.sync.dma_start(out=w1_raw.bitcast(I32), in_=w1_words[0].bitcast(I32))
+        load_scale_rows(nc, plane_raw["w1"], w1_scales[0])
+        nc.sync.dma_start(out=w1_raw[:].bitcast(I32), in_=w1_words[0].bitcast(I32))
         load_w2(0, 1)
-        load_scale_rows(nc, w_plane_raw, w3_scales[0], W3_ROW)
         load_w2(1, 0)
+        load_scale_rows(nc, plane_raw["w3"], w3_scales[0])
         load_w2(1, 1)
         w3_cols = w3_words[0].rearrange("p c i -> p (c i)").bitcast(I32)
         nc.sync.dma_start(out=w3_raw[0][:], in_=w3_cols[:, 0:BANK])
@@ -124,35 +124,38 @@ def tile_list_codon_context_rate_kernel(
             nc.sync.dma_start(out=b4_sb[:], in_=b4.rearrange("(c p) -> p c", p=P))
 
         words_at = {
-            ("own", 0): W2_AT[0],
-            ("up", 0): ROW_AT,
-            ("own", 1): ROW_AT + WORDS + BANK,
-            ("up", 1): ROW_AT + 2 * WORDS + BANK,
-            ("down", 0): LAST_PIECE_AT - S,
+            ("own", 1): ROW_AT,
+            ("up", 1): ROW_AT + WORDS + BANK,
+            ("down", 0): LAST_PIECE_AT - BANK,
             ("down", 1): LAST_PIECE_AT + WORDS,
         }
         picked = {}
 
-        def gather_plane(name, at=None):
-            dst = held([P, S], U8, "plane_" + name) if at is None else placed([P, S], U8, "plane_" + name, at)
-            nc.vector.tensor_copy(dst[:], tab_plane[:].indirect(lists[name][:]))
-            for half in range(S // BANK):
-                picked["plane", name, half] = dst[:, half * BANK : (half + 1) * BANK]
+        def gather_plane(name, halves, at=None):
+            label = "plane_%s%d" % (name, halves[0])
+            width = len(halves) * BANK
+            dst = held([P, width], U8, label) if at is None else placed([P, width], U8, label, at)
+            entries = lists[name][:, halves[0] * BANK // 16 : (halves[-1] + 1) * BANK // 16]
+            nc.vector.tensor_copy(dst[:], tab_plane[:].indirect(entries))
+            for i, half in enumerate(halves):
+                picked["plane", name, half] = dst[:, i * BANK : (i + 1) * BANK]
 
         def gather_words(name, half):
-            dst = placed([P, BANK], U32, "words_%s%d" % (name, half), words_at[name, half])
+            label = "words_%s%d" % (name, half)
+            at = words_at.get((name, half))
+            dst = held([P, BANK], U32, label) if at is None else placed([P, BANK], U32, label, at)
             entries = lists[name][:, half * BANK // 16 : (half + 1) * BANK // 16]
             nc.vector.tensor_copy(dst[:], tab[:].bitcast(U32).indirect(entries))
             picked["words", name, half] = dst[:]
 
-        w_plane = held([P, H], U8, "w_plane")
+        w_plane = {"w1": held([P, H], U8, "w1_plane"), "w3": placed([P, H], U8, "w3_plane", W3_PLANE_AT)}
         w3_dealt = [placed([P, BANK], I32, "w3_dealt%d" % b, W3_AT + b * WORDS) for b in range(PASSES)]
         w1_dealt = held([P, 2 * H], U8, "w1_dealt")
 
-        def deal_plane():
-            nc.vector.tensor_copy(
-                out=w_plane[:].bitcast(U16).rearrange("p (t c i) -> p c t i", t=PACK, i=8),
-                in_=w_plane_raw.bitcast(U16).rearrange("p (c i t) -> p c t i", t=PACK, i=8),
+        def deal_plane(name):
+            nc.gpsimd.tensor_copy(
+                out=w_plane[name][:].rearrange("p (t g v) -> p t g v", t=PACK, v=PAIR),
+                in_=plane_raw[name].rearrange("p (g t v) -> p t g v", t=PACK, v=PAIR),
             )
 
         def deal_w3(b):
@@ -162,12 +165,12 @@ def tile_list_codon_context_rate_kernel(
             )
 
         def deal_w1():
-            nc.vector.tensor_copy(
+            nc.gpsimd.tensor_copy(
                 out=w1_dealt[:].bitcast(I32).rearrange("p (t c i) -> p c t i", t=PACK, i=4),
-                in_=w1_raw.bitcast(I32).rearrange("p (c i t) -> p c t i", t=PACK, i=4),
+                in_=w1_raw[:].bitcast(I32).rearrange("p (c i t) -> p c t i", t=PACK, i=4),
             )
 
-        w2_bf = [held([P, BANK * PACK], BF16, "w2_bf0"), placed([P, BANK * PACK], BF16, "w2_bf1", W3_AT)]
+        w2_bf = [placed([P, BANK * PACK], BF16, "w2_bf0", W2_BF_AT), placed([P, BANK * PACK], BF16, "w2_bf1", W3_AT)]
         w2_codes = [held([P, BANK], U32, "w2_codes%d" % b) for b in range(PASSES)]
         w2_plane = {}
 
@@ -178,7 +181,7 @@ def tile_list_codon_context_rate_kernel(
 
         def quant_w2(b):
             label = "w2_plane%d" % b
-            w2_plane[b] = held([P, BANK], U8, label) if b else placed([P, BANK], U8, label, ROW_AT + WORDS)
+            w2_plane[b] = held([P, BANK], U8, label)
             nc.vector.quantize_mx(out=w2_codes[b][:].bitcast(FP8X4), scales=w2_plane[b][:], in_=w2_bf[b][:])
 
         w4_bf = held([P, PASSES * N * PACK], BF16, "w4_bf")
@@ -216,7 +219,7 @@ def tile_list_codon_context_rate_kernel(
             nc.tensor.matmul_mx(
                 out=acc[:],
                 lhsT=w1_dealt[:, 2 * c0 : 2 * (c0 + P)].bitcast(FP4X4),
-                lhsT_scale=w_plane[:, c0 : c0 + P],
+                lhsT_scale=w_plane["w1"][:, c0 : c0 + P],
                 rhs=picked["words", "own", half].bitcast(FP8X4),
                 rhs_scale=picked["plane", "own", half],
                 start=first,
@@ -249,7 +252,7 @@ def tile_list_codon_context_rate_kernel(
             nc.tensor.matmul_mx(
                 out=acc[:],
                 lhsT=w3_dealt[b][:, t * P : (t + 1) * P].bitcast(FP8X4),
-                lhsT_scale=w_plane[W3_ROW:P, cols],
+                lhsT_scale=w_plane["w3"][:, cols],
                 rhs=picked["words", "down", half].bitcast(FP8X4),
                 rhs_scale=picked["plane", "down", half],
                 start=True,
@@ -336,25 +339,27 @@ def tile_list_codon_context_rate_kernel(
                 queue.dma_start(out=out[c * P : (c + 1) * P, half * BANK + j0 : half * BANK + j1], in_=res[:])
 
         for name in ("own", "up"):
-            gather_plane(name)
+            gather_plane(name, (0, 1))
         cast_w2(0)
         cast_w2(1)
         gather_words("own", 0)
+        deal_plane("w1")
         deal_w1()
-        deal_plane()
         open_e(0, 0, pass_w1)
         gather_words("up", 0)
         quant_w2(0)
+        deal_plane("w3")
         close_e(0, 0, pass_w2)
         gather_words("own", 1)
         open_e(1, 0, pass_w1)
         gather_words("up", 1)
+        gather_plane("down", (0,), ROW_AT + WORDS)
         close_e(1, 0, pass_w2)
         quant_w2(1)
         stage_e(0, 1)
         deal_w3(0)
         gather_words("down", 0)
-        gather_plane("down", LAST_PIECE_AT + WORDS - S)
+        gather_plane("down", (1,), LAST_PIECE_AT + WORDS - BANK)
         gather_words("down", 1)
         deal_w3(1)
         cast_w4(0)

@@ -34,6 +34,7 @@ LAST_PIECE_AT = W2_AT[1] + 2 * WORDS
 W3_PLANE_AT = 8 * WORDS
 ROW_AT = W3_PLANE_AT + H
 W2_BF_AT = ROW_AT - 64
+RAW_AT = 14 * WORDS
 W3_AT = 12 * WORDS
 
 
@@ -77,7 +78,7 @@ def tile_list_codon_context_rate_kernel(
         tab_plane = held([P, T], U8, "tab_plane")
         nc.gpsimd.memset(tab_plane[:].bitcast(I32), 0)
         w1_raw = held([P, 2 * H], U8, "w1_raw")
-        plane_raw = {name: held([P, H], U8, name + "_plane_raw")[:] for name in ("w1", "w3")}
+        plane_raw = {"w1": placed([P, H], U8, "w1_plane_raw", RAW_AT)[:], "w3": held([P, H], U8, "w3_plane_raw")[:]}
         for raw in plane_raw.values():
             nc.vector.memset(raw.bitcast(I32), 0)
 
@@ -125,7 +126,7 @@ def tile_list_codon_context_rate_kernel(
 
         words_at = {
             ("own", 1): ROW_AT,
-            ("up", 1): ROW_AT + WORDS + BANK,
+            ("up", 1): ROW_AT + WORDS,
             ("down", 0): LAST_PIECE_AT - BANK,
             ("down", 1): LAST_PIECE_AT + WORDS,
         }
@@ -347,13 +348,13 @@ def tile_list_codon_context_rate_kernel(
         deal_w1()
         open_e(0, 0, pass_w1)
         gather_words("up", 0)
+        gather_plane("down", (0,), RAW_AT)
         quant_w2(0)
         deal_plane("w3")
         close_e(0, 0, pass_w2)
         gather_words("own", 1)
         open_e(1, 0, pass_w1)
         gather_words("up", 1)
-        gather_plane("down", (0,), ROW_AT + WORDS)
         close_e(1, 0, pass_w2)
         quant_w2(1)
         stage_e(0, 1)

@@ -30,12 +30,12 @@ GPSIMD_SITES = 256
 
 WORDS = 4 * BANK
 W2_AT = (0, 4 * WORDS)
-LAST_PIECE_AT = W2_AT[1] + 2 * WORDS
-W3_PLANE_AT = 8 * WORDS
-ROW_AT = W3_PLANE_AT + H
-W2_BF_AT = ROW_AT - 64
-RAW_AT = 14 * WORDS
-W3_AT = 12 * WORDS
+W2_BF_AT = (8 * WORDS, 11 * WORDS)
+ROW_AT = W2_BF_AT[1] + 64
+W3_AT = ROW_AT + H
+W1_RAW_AT = 14 * WORDS
+W3_RAW_AT = 15 * WORDS
+W4_AT = 17 * WORDS
 
 
 def load_scale_rows(nc, plane, rows):
@@ -68,17 +68,19 @@ def tile_list_codon_context_rate_kernel(
         def placed(shape, dtype, name, at):
             return shared.tile(shape, dtype, name=name, offset=at, align_bytes=64)
 
-        taken = []
+        X, Y = list(range(PACK)), list(range(PACK, BANKS))
+        taken = X + Y + X + Y + [n for pair in zip(X, Y) for n in pair] * 2 + X + Y
 
         def next_bank():
-            n = len(taken) % BANKS
-            taken.append(n)
+            n = taken.pop(0)
             return psum.tile([P, BANK], F32, name="bank%d" % n, tag="bank%d" % n)
 
         tab_plane = held([P, T], U8, "tab_plane")
         nc.gpsimd.memset(tab_plane[:].bitcast(I32), 0)
         w1_raw = held([P, 2 * H], U8, "w1_raw")
-        plane_raw = {"w1": placed([P, H], U8, "w1_plane_raw", RAW_AT)[:], "w3": held([P, H], U8, "w3_plane_raw")[:]}
+        plane_raw = {
+            name: placed([P, H], U8, name + "_plane_raw", at)[:] for name, at in (("w1", W1_RAW_AT), ("w3", W3_RAW_AT))
+        }
         for raw in plane_raw.values():
             nc.vector.memset(raw.bitcast(I32), 0)
 
@@ -99,7 +101,7 @@ def tile_list_codon_context_rate_kernel(
             c0 = b * BANK + u * PIECE
             nc.sync.dma_start(out=w2_raw[b, u][:], in_=w2_rows[:, :, c0 : c0 + PIECE])
 
-        w4_raw = [held([P, PACK, N], F32, "w4_raw%d" % b) for b in range(PASSES)]
+        w4_raw = [held([P, PACK, N], F32, "w4_raw0"), placed([P, PACK, N], F32, "w4_raw1", W4_AT)]
 
         for name, src in (("own", offs), ("up", offs2), ("down", offs3)):
             nc.sync.dma_start(lists[name][:], src)
@@ -116,19 +118,20 @@ def tile_list_codon_context_rate_kernel(
         nc.sync.dma_start(out=w3_raw[0][:], in_=w3_cols[:, 0:BANK])
         load_bias(nc, b1_sb, b1)
         nc.sync.dma_start(out=w3_raw[1][:], in_=w3_cols[:, BANK : 2 * BANK])
-        load_bias(nc, b3_sb, b3)
         w4_rows = w4.rearrange("(b g t v) n -> b v g t n", b=PASSES, t=PACK, v=PAIR)
         for b in range(PASSES):
             for v in range(PAIR):
                 nc.sync.dma_start(out=w4_raw[b][v:P:PAIR], in_=w4_rows[b, v])
+            if b == 0:
+                load_bias(nc, b3_sb, b3)
         with nc.allow_non_contiguous_dma(reason="one bias value a partition"):
             nc.sync.dma_start(out=b4_sb[:], in_=b4.rearrange("(c p) -> p c", p=P))
 
         words_at = {
-            ("own", 1): ROW_AT,
-            ("up", 1): ROW_AT + WORDS,
-            ("down", 0): LAST_PIECE_AT - BANK,
-            ("down", 1): LAST_PIECE_AT + WORDS,
+            ("own", 1): W2_BF_AT[0],
+            ("up", 1): ROW_AT - WORDS,
+            ("down", 0): W3_AT + WORDS,
+            ("down", 1): W3_RAW_AT + BANK,
         }
         picked = {}
 
@@ -149,8 +152,8 @@ def tile_list_codon_context_rate_kernel(
             nc.vector.tensor_copy(dst[:], tab[:].bitcast(U32).indirect(entries))
             picked["words", name, half] = dst[:]
 
-        w_plane = {"w1": held([P, H], U8, "w1_plane"), "w3": placed([P, H], U8, "w3_plane", W3_PLANE_AT)}
-        w3_dealt = [placed([P, BANK], I32, "w3_dealt%d" % b, W3_AT + b * WORDS) for b in range(PASSES)]
+        w_plane = {"w1": held([P, H], U8, "w1_plane"), "w3": placed([P, H], U8, "w3_plane", ROW_AT)}
+        w3_dealt = [placed([P, BANK], I32, "w3_dealt0", W3_AT), held([P, BANK], I32, "w3_dealt1")]
         w1_dealt = held([P, 2 * H], U8, "w1_dealt")
 
         def deal_plane(name):
@@ -171,7 +174,7 @@ def tile_list_codon_context_rate_kernel(
                 in_=w1_raw[:].bitcast(I32).rearrange("p (c i t) -> p c t i", t=PACK, i=4),
             )
 
-        w2_bf = [placed([P, BANK * PACK], BF16, "w2_bf0", W2_BF_AT), placed([P, BANK * PACK], BF16, "w2_bf1", W3_AT)]
+        w2_bf = [placed([P, BANK * PACK], BF16, "w2_bf%d" % b, W2_BF_AT[b]) for b in range(PASSES)]
         w2_codes = [held([P, BANK], U32, "w2_codes%d" % b) for b in range(PASSES)]
         w2_plane = {}
 
@@ -278,7 +281,7 @@ def tile_list_codon_context_rate_kernel(
             nc.scalar.activation(last_down[:, t, :], acc[:], ACT.Identity, bias=b3_sb[:, LAST[1], PAIR * t : PAIR * t + 1])
 
         def multiply_last(j0, j1):
-            at = W3_AT + 3 * BANK if j0 == 0 else LAST_PIECE_AT + 2 * PACK * j0
+            at = W3_AT + 3 * BANK if j0 == 0 else W3_RAW_AT + BANK + 2 * PACK * (j0 - TAIL[0][1])
             dst = placed([P, (j1 - j0) * PACK], BF16, "h_bf11_%d" % j0, at)
             nc.vector.tensor_tensor(
                 out=dst[:].rearrange("p (c i t) -> p c t i", i=2, t=PACK),
@@ -290,7 +293,9 @@ def tile_list_codon_context_rate_kernel(
 
         def weave_views(half, b, j0, j1):
             if (half, b, 0) not in h_bf:
-                h_bf[half, b, 0] = held([P, BANK * PACK], BF16, "h_bf%d%d_0" % (half, b))
+                label = "h_bf%d%d_0" % (half, b)
+                shape = [P, BANK * PACK]
+                h_bf[half, b, 0] = held(shape, BF16, label) if half or b else placed(shape, BF16, label, W4_AT)
             return h_bf[half, b, 0][:, j0 * PACK : j1 * PACK], h_slices[half, b][:, :, j0:j1]
 
         def weave_gpsimd(half, b, j0, j1):
@@ -339,45 +344,45 @@ def tile_list_codon_context_rate_kernel(
                     queue = nc.scalar if shared_out else nc.sync
                 queue.dma_start(out=out[c * P : (c + 1) * P, half * BANK + j0 : half * BANK + j1], in_=res[:])
 
-        for name in ("own", "up"):
-            gather_plane(name, (0, 1))
+        gather_plane("own", (0, 1))
+        gather_plane("up", (0,))
         cast_w2(0)
         cast_w2(1)
         gather_words("own", 0)
         deal_plane("w1")
         deal_w1()
         open_e(0, 0, pass_w1)
+        open_e(0, 1, pass_w1)
         gather_words("up", 0)
-        gather_plane("down", (0,), RAW_AT)
+        gather_plane("up", (1,), W1_RAW_AT)
+        gather_plane("down", (0,), W1_RAW_AT + BANK)
         quant_w2(0)
-        deal_plane("w3")
         close_e(0, 0, pass_w2)
         gather_words("own", 1)
-        open_e(1, 0, pass_w1)
-        gather_words("up", 1)
-        close_e(1, 0, pass_w2)
         quant_w2(1)
-        stage_e(0, 1)
+        close_e(0, 1, pass_w2)
+        gather_words("up", 1)
+        deal_plane("w3")
         deal_w3(0)
         gather_words("down", 0)
-        gather_plane("down", (1,), LAST_PIECE_AT + WORDS - BANK)
+        open_e(1, 0, pass_w1)
+        close_e(1, 0, pass_w2)
+        gather_plane("down", (1,), W3_RAW_AT)
         gather_words("down", 1)
         deal_w3(1)
         cast_w4(0)
         cast_w4(1)
 
-        stage_e(*LAST, (0, 1))
-        stage_d(0, 0, (0, 1))
-        for t in (2, 3):
-            stage_e(*LAST, (t,))
-            stage_d(0, 0, (t,))
+        stage_d(0, 0)
         weave_gpsimd(0, 0, 0, BANK)
-        stage_d(0, 1)
+        for t in range(PACK):
+            stage_e(*LAST, (t,))
+            stage_d(0, 1, (t,))
+        weave_gpsimd(0, 1, 0, GPSIMD_SITES)
         for t in range(PACK):
             stage_last_d(t)
-        weave_gpsimd(0, 1, 0, GPSIMD_SITES)
+            stage_d(1, 0, (t,))
         weave_scalar(0, 1, GPSIMD_SITES, BANK)
-        stage_d(1, 0)
         cut = TAIL[0][1]
         weave_scalar(1, 0, 0, cut)
         weave_scalar(1, 0, cut, BANK)

@@ -23,7 +23,7 @@ BANK = 512
 BANKS = 8
 PASSES = H // (P * PACK)
 M = H // PACK
-PIECE = BANK // 2
+PIECES = ((0, 256), (256, 384), (384, 512))
 LAST = (1, 1)
 TAIL = ((0, 256), (256, 384), (384, 512))
 GPSIMD_SITES = 256
@@ -69,7 +69,7 @@ def tile_list_codon_context_rate_kernel(
             return shared.tile(shape, dtype, name=name, offset=at, align_bytes=64)
 
         X, Y = list(range(PACK)), list(range(PACK, BANKS))
-        taken = X + Y + X + Y + [n for pair in zip(X, Y) for n in pair] * 2 + X + Y
+        taken = X + Y + X + Y + [n for pair in zip(X, Y) for n in pair] + Y + Y + X + Y
 
         def next_bank():
             n = taken.pop(0)
@@ -92,14 +92,14 @@ def tile_list_codon_context_rate_kernel(
         b3_sb = held([P, PASSES, PAIR * PACK], F32, "b3_sb")
         b4_sb = held([P, N // P], F32, "b4_sb")
         w2_raw = {
-            (b, u): placed([P, PACK, PIECE], F32, "w2_raw%d%d" % (b, u), W2_AT[b] + 2 * u * WORDS)
+            (b, u): placed([P, PACK, c1 - c0], F32, "w2_raw%d%d" % (b, u), W2_AT[b] + 4 * PACK * c0)
             for b in range(PASSES)
-            for u in range(2)
+            for u, (c0, c1) in enumerate(PIECES)
         }
 
         def load_w2(b, u):
-            c0 = b * BANK + u * PIECE
-            nc.sync.dma_start(out=w2_raw[b, u][:], in_=w2_rows[:, :, c0 : c0 + PIECE])
+            c0, c1 = PIECES[u]
+            nc.sync.dma_start(out=w2_raw[b, u][:], in_=w2_rows[:, :, b * BANK + c0 : b * BANK + c1])
 
         w4_raw = [held([P, PACK, N], F32, "w4_raw0"), placed([P, PACK, N], F32, "w4_raw1", W4_AT)]
 
@@ -111,9 +111,11 @@ def tile_list_codon_context_rate_kernel(
         load_scale_rows(nc, plane_raw["w1"], w1_scales[0])
         nc.sync.dma_start(out=w1_raw[:].bitcast(I32), in_=w1_words[0].bitcast(I32))
         load_w2(0, 1)
+        load_w2(0, 2)
         load_w2(1, 0)
         load_scale_rows(nc, plane_raw["w3"], w3_scales[0])
         load_w2(1, 1)
+        load_w2(1, 2)
         w3_cols = w3_words[0].rearrange("p c i -> p (c i)").bitcast(I32)
         nc.sync.dma_start(out=w3_raw[0][:], in_=w3_cols[:, 0:BANK])
         load_bias(nc, b1_sb, b1)
@@ -179,9 +181,10 @@ def tile_list_codon_context_rate_kernel(
         w2_plane = {}
 
         def cast_w2(b):
-            dst = w2_bf[b][:].rearrange("p (t u g v i) -> p u g t i v", t=PACK, u=2, v=PAIR, i=PACK)
-            for u in range(2):
-                nc.scalar.copy(out=dst[:, u], in_=w2_raw[b, u][:].rearrange("p i (g t v) -> p g t i v", t=PACK, v=PAIR))
+            dst = w2_bf[b][:].rearrange("p (t g v i) -> p g t i v", t=PACK, v=PAIR, i=PACK)
+            for u, (c0, c1) in enumerate(PIECES):
+                src = w2_raw[b, u][:].rearrange("p i (g t v) -> p g t i v", t=PACK, v=PAIR)
+                nc.scalar.copy(out=dst[:, c0 // (PAIR * PACK) : c1 // (PAIR * PACK)], in_=src)
 
         def quant_w2(b):
             label = "w2_plane%d" % b
@@ -322,6 +325,10 @@ def tile_list_codon_context_rate_kernel(
 
         def stage_y(half, j0, j1, shared_out=False):
             width = j1 - j0
+            rows = out.rearrange("(c p) j -> p c j", p=P)[:, :, half * BANK + j0 : half * BANK + j1]
+            joined = width < BANK and not shared_out
+            if joined:
+                both = held([P, N // P, width], F32, "res%d_%d" % (half, j0))
             for c in range(N // P):
                 acc = next_bank()
                 for b in range(PASSES):
@@ -335,14 +342,17 @@ def tile_list_codon_context_rate_kernel(
                         start=(b == 0),
                         stop=(b == PASSES - 1),
                     )
-                res = held([P, width], F32, "res%d%d_%d" % (half, c, j0))
+                res = both[:, c, :] if joined else held([P, width], F32, "res%d%d_%d" % (half, c, j0))[:]
                 if shared_out and c == 1:
-                    nc.vector.tensor_scalar(res[:], acc[:, 0:width], b4_sb[:, c : c + 1], None, ALU.add)
+                    nc.vector.tensor_scalar(res, acc[:, 0:width], b4_sb[:, c : c + 1], None, ALU.add)
                     queue = nc.sync
                 else:
-                    nc.scalar.activation(res[:], acc[:, 0:width], ACT.Identity, bias=b4_sb[:, c : c + 1])
+                    nc.scalar.activation(res, acc[:, 0:width], ACT.Identity, bias=b4_sb[:, c : c + 1])
                     queue = nc.scalar if shared_out else nc.sync
-                queue.dma_start(out=out[c * P : (c + 1) * P, half * BANK + j0 : half * BANK + j1], in_=res[:])
+                if not joined:
+                    queue.dma_start(out=rows[:, c, :], in_=res)
+            if joined:
+                nc.sync.dma_start(out=rows, in_=both[:])
 
         gather_plane("own", (0, 1))
         gather_plane("up", (0,))
@@ -379,10 +389,10 @@ def tile_list_codon_context_rate_kernel(
             stage_e(*LAST, (t,))
             stage_d(0, 1, (t,))
         weave_gpsimd(0, 1, 0, GPSIMD_SITES)
+        weave_scalar(0, 1, GPSIMD_SITES, BANK)
+        stage_d(1, 0)
         for t in range(PACK):
             stage_last_d(t)
-            stage_d(1, 0, (t,))
-        weave_scalar(0, 1, GPSIMD_SITES, BANK)
         cut = TAIL[0][1]
         weave_scalar(1, 0, 0, cut)
         weave_scalar(1, 0, cut, BANK)

@@ -160,8 +160,8 @@ def tile_list_codon_context_rate_kernel(
 
         def deal_plane(name):
             nc.gpsimd.tensor_copy(
-                out=w_plane[name][:].rearrange("p (t g v) -> p t g v", t=PACK, v=PAIR),
-                in_=plane_raw[name].rearrange("p (g t v) -> p t g v", t=PACK, v=PAIR),
+                out=w_plane[name][:].rearrange("p (t g v) -> p t v g", t=PACK, v=PAIR),
+                in_=plane_raw[name].rearrange("p (g t v) -> p t v g", t=PACK, v=PAIR),
             )
 
         def deal_w3(b):
@@ -362,7 +362,7 @@ def tile_list_codon_context_rate_kernel(
         deal_plane("w1")
         deal_w1()
         open_e(0, 0, pass_w1)
-        open_e(0, 1, pass_w1)
+        open_e(0, 1, pass_w1, (0, 1))
         gather_words("up", 0)
         gather_plane("up", (1,), W1_RAW_AT)
         gather_plane("down", (0,), W1_RAW_AT + BANK)
@@ -370,7 +370,8 @@ def tile_list_codon_context_rate_kernel(
         close_e(0, 0, pass_w2)
         gather_words("own", 1)
         quant_w2(1)
-        close_e(0, 1, pass_w2)
+        close_e(0, 1, pass_w2, (0, 1))
+        stage_e(0, 1, (2, 3))
         gather_words("up", 1)
         deal_plane("w3")
         deal_w3(0)

@@ -35,6 +35,7 @@ ROW_AT = W2_BF_AT[1] + 64
 W3_AT = ROW_AT + H
 W1_RAW_AT = 14 * WORDS
 W3_RAW_AT = 15 * WORDS
+TAB_AT = 19 * WORDS
 W4_AT = 17 * WORDS
 
 
@@ -69,7 +70,7 @@ def tile_list_codon_context_rate_kernel(
             return shared.tile(shape, dtype, name=name, offset=at, align_bytes=64)
 
         X, Y = list(range(PACK)), list(range(PACK, BANKS))
-        taken = X + Y + X + Y + [n for pair in zip(X, Y) for n in pair] + Y + Y + X + Y
+        taken = X + Y + X + Y + [n for pair in zip(X, Y) for n in pair] + Y + Y[:2] + X + Y[2:] + X[:2] + Y[:2]
 
         def next_bank():
             n = taken.pop(0)
@@ -86,7 +87,7 @@ def tile_list_codon_context_rate_kernel(
 
         lists = {name: keep.tile([P, S // 16], U16, name="list_" + name) for name in ("down", "up", "own")}
         w2_rows = w2.rearrange("(p i) c -> p i c", i=PACK)
-        tab = held([P, T], I32, "tab")
+        tab = placed([P, T], I32, "tab", TAB_AT)
         w3_raw = [held([P, BANK], I32, "w3_raw%d" % b) for b in range(PASSES)]
         b1_sb = held([P, PASSES, PAIR * PACK], F32, "b1_sb")
         b3_sb = held([P, PASSES, PAIR * PACK], F32, "b3_sb")
@@ -191,18 +192,19 @@ def tile_list_codon_context_rate_kernel(
             w2_plane[b] = held([P, BANK], U8, label)
             nc.vector.quantize_mx(out=w2_codes[b][:].bitcast(FP8X4), scales=w2_plane[b][:], in_=w2_bf[b][:])
 
-        w4_bf = held([P, PASSES * N * PACK], BF16, "w4_bf")
+        w4_bf = [held([P, N * PACK], BF16, "w4_bf0"), placed([P, N * PACK], BF16, "w4_bf1", TAB_AT)]
         w4_codes = held([P, PASSES * N], U32, "w4_codes")
         w4_plane = placed([P, PASSES * N], U8, "w4_plane", W3_AT + PASSES * BANK)
 
         def cast_w4(b):
-            dst = w4_bf[:, b * N * PACK : (b + 1) * N * PACK]
             nc.gpsimd.tensor_copy(
-                out=dst.rearrange("p (n t) -> p n t", t=PACK), in_=w4_raw[b][:].rearrange("p t n -> p n t")
+                out=w4_bf[b][:].rearrange("p (n t) -> p n t", t=PACK), in_=w4_raw[b][:].rearrange("p t n -> p n t")
             )
 
         def quant_w4():
-            nc.vector.quantize_mx(out=w4_codes[:].bitcast(FP8X4), scales=w4_plane[:], in_=w4_bf[:])
+            for b in range(PASSES):
+                cols = slice(b * N, (b + 1) * N)
+                nc.vector.quantize_mx(out=w4_codes[:, cols].bitcast(FP8X4), scales=w4_plane[:, cols], in_=w4_bf[b][:])
 
         rate = {}
         h_slices = {}
@@ -305,9 +307,9 @@ def tile_list_codon_context_rate_kernel(
             dst, src = weave_views(half, b, j0, j1)
             nc.gpsimd.tensor_copy(out=dst.rearrange("p (c t) -> p c t", t=PACK), in_=src.rearrange("p t c -> p c t"))
 
-        def weave_scalar(half, b, j0, j1):
+        def weave_lines(copy, half, b, j0, j1):
             dst, src = weave_views(half, b, j0, j1)
-            nc.scalar.copy(
+            copy(
                 out=dst.rearrange("p (c i t) -> p c t i", i=4, t=PACK),
                 in_=src.rearrange("p t (c i) -> p c t i", i=4),
             )
@@ -390,13 +392,14 @@ def tile_list_codon_context_rate_kernel(
             stage_e(*LAST, (t,))
             stage_d(0, 1, (t,))
         weave_gpsimd(0, 1, 0, GPSIMD_SITES)
-        weave_scalar(0, 1, GPSIMD_SITES, BANK)
+        weave_lines(nc.scalar.copy, 0, 1, GPSIMD_SITES, BANK)
         stage_d(1, 0)
         for t in range(PACK):
             stage_last_d(t)
         cut = TAIL[0][1]
-        weave_scalar(1, 0, 0, cut)
-        weave_scalar(1, 0, cut, BANK)
+        weave_lines(nc.scalar.copy, 1, 0, 0, cut)
+        weave_lines(nc.scalar.copy, 1, 0, *TAIL[1])
+        weave_lines(nc.vector.tensor_copy, 1, 0, *TAIL[2])
 
         quant_h(0, 0, 0, BANK)
         quant_w4()

@@ -20,13 +20,14 @@ P = 128
 PACK = 4
 PAIR = 2
 BANK = 512
-BANKS = 8
+FRONT, BACK = (0, 1, 2, 3), (4, 5, 6, 7)
 PASSES = H // (P * PACK)
 M = H // PACK
 PIECES = ((0, 256), (256, 384), (384, 512))
 LAST = (1, 1)
 TAIL = ((0, 256), (256, 384), (384, 512))
 GPSIMD_SITES = 256
+VECTOR_SITES = 64
 
 WORDS = 4 * BANK
 W2_AT = (0, 4 * WORDS)
@@ -35,8 +36,8 @@ ROW_AT = W2_BF_AT[1] + 64
 W3_AT = ROW_AT + H
 W1_RAW_AT = 14 * WORDS
 W3_RAW_AT = 15 * WORDS
-TAB_AT = 19 * WORDS
 W4_AT = 17 * WORDS
+TAB_AT = 19 * WORDS
 
 
 def load_scale_rows(nc, plane, rows):
@@ -69,11 +70,7 @@ def tile_list_codon_context_rate_kernel(
         def placed(shape, dtype, name, at):
             return shared.tile(shape, dtype, name=name, offset=at, align_bytes=64)
 
-        X, Y = list(range(PACK)), list(range(PACK, BANKS))
-        taken = X + Y + X + Y + [n for pair in zip(X, Y) for n in pair] + Y + Y[:2] + X + Y[2:] + X[:2] + Y[:2]
-
-        def next_bank():
-            n = taken.pop(0)
+        def bank(n):
             return psum.tile([P, BANK], F32, name="bank%d" % n, tag="bank%d" % n)
 
         tab_plane = held([P, T], U8, "tab_plane")
@@ -188,8 +185,7 @@ def tile_list_codon_context_rate_kernel(
                 nc.scalar.copy(out=dst[:, c0 // (PAIR * PACK) : c1 // (PAIR * PACK)], in_=src)
 
         def quant_w2(b):
-            label = "w2_plane%d" % b
-            w2_plane[b] = held([P, BANK], U8, label)
+            w2_plane[b] = held([P, BANK], U8, "w2_plane%d" % b)
             nc.vector.quantize_mx(out=w2_codes[b][:].bitcast(FP8X4), scales=w2_plane[b][:], in_=w2_bf[b][:])
 
         w4_bf = [held([P, N * PACK], BF16, "w4_bf0"), placed([P, N * PACK], BF16, "w4_bf1", TAB_AT)]
@@ -237,9 +233,9 @@ def tile_list_codon_context_rate_kernel(
 
         opened = {}
 
-        def open_e(half, b, opening, slices=range(PACK)):
+        def open_e(half, b, banks, opening, slices=range(PACK)):
             for t in slices:
-                opened[half, b, t] = next_bank()
+                opened[half, b, t] = bank(banks[t])
                 opening(opened[half, b, t], half, b, t, True)
 
         def close_e(half, b, closing, slices=range(PACK)):
@@ -250,13 +246,13 @@ def tile_list_codon_context_rate_kernel(
                 closing(acc, half, b, t, False)
                 nc.scalar.activation(rate[half, b][:, t, :], acc[:], ACT.Exp, bias=b1_sb[:, b, PAIR * t : PAIR * t + 1])
 
-        def stage_e(half, b, slices=range(PACK)):
+        def stage_e(half, b, banks, slices):
             for t in slices:
-                open_e(half, b, pass_w2, (t,))
+                open_e(half, b, banks, pass_w2, (t,))
                 close_e(half, b, pass_w1, (t,))
 
-        def product_d(half, b, t):
-            acc = next_bank()
+        def product_d(half, b, banks, t):
+            acc = bank(banks[t])
             cols = slice(t * M + b * P, t * M + (b + 1) * P)
             nc.tensor.matmul_mx(
                 out=acc[:],
@@ -269,20 +265,20 @@ def tile_list_codon_context_rate_kernel(
             )
             return acc
 
-        def stage_d(half, b, slices=range(PACK)):
+        def stage_d(half, b, banks, slices=range(PACK)):
             if (half, b) not in h_slices:
                 h_slices[half, b] = held([P, PACK, BANK], BF16, "h_slices%d%d" % (half, b))
             dst = h_slices[half, b]
             for t in slices:
-                acc = product_d(half, b, t)
+                acc = product_d(half, b, banks, t)
                 nc.vector.scalar_tensor_tensor(
                     dst[:, t, :], acc[:], b3_sb[:, b, PAIR * t : PAIR * t + 1], rate[half, b][:, t, :], ALU.add, ALU.mult
                 )
 
         last_down = held([P, PACK, BANK], F32, "last_down")
 
-        def stage_last_d(t):
-            acc = product_d(*LAST, t)
+        def stage_last_d(banks, t):
+            acc = product_d(*LAST, banks, t)
             nc.scalar.activation(last_down[:, t, :], acc[:], ACT.Identity, bias=b3_sb[:, LAST[1], PAIR * t : PAIR * t + 1])
 
         def multiply_last(j0, j1):
@@ -325,14 +321,14 @@ def tile_list_codon_context_rate_kernel(
                     h_codes[half, b, a0, a1] = codes[:, a0 - j0 : a1 - j0]
                     h_plane[half, b, a0, a1] = plane[:, a0 - j0 : a1 - j0]
 
-        def stage_y(half, j0, j1, shared_out=False):
+        def stage_y(half, j0, j1, banks, shared_out=False, last=False):
             width = j1 - j0
             rows = out.rearrange("(c p) j -> p c j", p=P)[:, :, half * BANK + j0 : half * BANK + j1]
-            joined = width < BANK and not shared_out
+            joined = width < BANK and not last
             if joined:
                 both = held([P, N // P, width], F32, "res%d_%d" % (half, j0))
             for c in range(N // P):
-                acc = next_bank()
+                acc = bank(banks[c])
                 for b in range(PASSES):
                     cols = slice(b * N + c * P, b * N + (c + 1) * P)
                     nc.tensor.matmul_mx(
@@ -350,7 +346,7 @@ def tile_list_codon_context_rate_kernel(
                     queue = nc.sync
                 else:
                     nc.scalar.activation(res, acc[:, 0:width], ACT.Identity, bias=b4_sb[:, c : c + 1])
-                    queue = nc.scalar if shared_out else nc.sync
+                    queue = nc.scalar if last else nc.sync
                 if not joined:
                     queue.dma_start(out=rows[:, c, :], in_=res)
             if joined:
@@ -363,8 +359,8 @@ def tile_list_codon_context_rate_kernel(
         gather_words("own", 0)
         deal_plane("w1")
         deal_w1()
-        open_e(0, 0, pass_w1)
-        open_e(0, 1, pass_w1, (0, 1))
+        open_e(0, 0, FRONT, pass_w1)
+        open_e(0, 1, BACK, pass_w1, (0, 1))
         gather_words("up", 0)
         gather_plane("up", (1,), W1_RAW_AT)
         gather_plane("down", (0,), W1_RAW_AT + BANK)
@@ -373,12 +369,12 @@ def tile_list_codon_context_rate_kernel(
         gather_words("own", 1)
         quant_w2(1)
         close_e(0, 1, pass_w2, (0, 1))
-        stage_e(0, 1, (2, 3))
+        stage_e(0, 1, BACK, (2, 3))
         gather_words("up", 1)
         deal_plane("w3")
         deal_w3(0)
         gather_words("down", 0)
-        open_e(1, 0, pass_w1)
+        open_e(1, 0, FRONT, pass_w1)
         close_e(1, 0, pass_w2)
         gather_plane("down", (1,), W3_RAW_AT)
         gather_words("down", 1)
@@ -386,25 +382,25 @@ def tile_list_codon_context_rate_kernel(
         cast_w4(0)
         cast_w4(1)
 
-        stage_d(0, 0)
+        stage_d(0, 0, BACK)
         weave_gpsimd(0, 0, 0, BANK)
         for t in range(PACK):
-            stage_e(*LAST, (t,))
-            stage_d(0, 1, (t,))
+            stage_e(*LAST, FRONT, (t,))
+            stage_d(0, 1, BACK, (t,))
         weave_gpsimd(0, 1, 0, GPSIMD_SITES)
         weave_lines(nc.scalar.copy, 0, 1, GPSIMD_SITES, BANK)
-        stage_d(1, 0)
+        stage_d(1, 0, BACK)
         for t in range(PACK):
-            stage_last_d(t)
+            stage_last_d(BACK[:2] + FRONT[:2], t)
         cut = TAIL[0][1]
         weave_lines(nc.scalar.copy, 1, 0, 0, cut)
-        weave_lines(nc.scalar.copy, 1, 0, *TAIL[1])
-        weave_lines(nc.vector.tensor_copy, 1, 0, *TAIL[2])
+        weave_lines(nc.scalar.copy, 1, 0, cut, BANK - VECTOR_SITES)
+        weave_lines(nc.vector.tensor_copy, 1, 0, BANK - VECTOR_SITES, BANK)
 
         quant_h(0, 0, 0, BANK)
         quant_w4()
         quant_h(0, 1, 0, BANK)
-        stage_y(0, 0, BANK)
+        stage_y(0, 0, BANK, FRONT[2:])
         multiply_last(*TAIL[0])
         multiply_last(*TAIL[1])
         quant_h(*LAST, *TAIL[0])
@@ -413,5 +409,5 @@ def tile_list_codon_context_rate_kernel(
         quant_h(*LAST, *TAIL[1])
         quant_h(1, 0, cut, BANK)
         quant_h(*LAST, *TAIL[2])
-        for piece in TAIL:
-            stage_y(1, *piece, shared_out=(piece == TAIL[-1]))
+        for piece, banks in zip(TAIL, (BACK[2:], FRONT[:2], BACK[:2])):
+            stage_y(1, *piece, banks, shared_out=(piece != TAIL[0]), last=(piece == TAIL[-1]))

@@ -20,24 +20,23 @@ P = 128
 PACK = 4
 PAIR = 2
 BANK = 512
-FRONT, BACK = (0, 1, 2, 3), (4, 5, 6, 7)
+VECTOR_BANKS, SCALAR_BANKS = (4, 5, 0, 1), (6, 7, 2, 3)
 PASSES = H // (P * PACK)
 M = H // PACK
 PIECES = ((0, 256), (256, 384), (384, 512))
-LAST = (1, 1)
-TAIL = ((0, 256), (256, 384), (384, 512))
+TAIL = ((0, 256), (256, 512))
 GPSIMD_SITES = 256
-VECTOR_SITES = 64
 
 WORDS = 4 * BANK
-W2_AT = (0, 4 * WORDS)
-W2_BF_AT = (8 * WORDS, 11 * WORDS)
-ROW_AT = W2_BF_AT[1] + 64
-W3_AT = ROW_AT + H
-W1_RAW_AT = 14 * WORDS
-W3_RAW_AT = 15 * WORDS
-W4_AT = 17 * WORDS
-TAB_AT = 19 * WORDS
+W1_RAW_AT = 0
+W3_RAW_AT = 2 * WORDS
+W2_BF_AT = (4 * WORDS, 6 * WORDS)
+W4_RAW_AT = (10 * WORDS, 12 * WORDS)
+DOWN_AT = 14 * WORDS
+SLICES_AT = 18 * WORDS
+EARLY_AT = 22 * WORDS
+UP_AT = 25 * WORDS
+W3_DEALT_AT = 20 * WORDS
 
 
 def load_scale_rows(nc, plane, rows):
@@ -64,108 +63,86 @@ def tile_list_codon_context_rate_kernel(
         shared = ctx.enter_context(tc.tile_pool(name="shared", bufs=1))
         psum = ctx.enter_context(tc.psum_pool(name="psum", bufs=1))
 
-        def held(shape, dtype, name):
-            return keep.tile(shape, dtype, name=name, align_bytes=64)
-
-        def placed(shape, dtype, name, at):
+        def tile(shape, dtype, name, at=None):
+            if at is None:
+                return keep.tile(shape, dtype, name=name, align_bytes=64)
             return shared.tile(shape, dtype, name=name, offset=at, align_bytes=64)
 
         def bank(n):
             return psum.tile([P, BANK], F32, name="bank%d" % n, tag="bank%d" % n)
 
-        tab_plane = held([P, T], U8, "tab_plane")
+        tab_plane = tile([P, T], U8, "tab_plane")
         nc.gpsimd.memset(tab_plane[:].bitcast(I32), 0)
-        w1_raw = held([P, 2 * H], U8, "w1_raw")
-        plane_raw = {
-            name: placed([P, H], U8, name + "_plane_raw", at)[:] for name, at in (("w1", W1_RAW_AT), ("w3", W3_RAW_AT))
-        }
+        plane_raw = {"w1": tile([P, H], U8, "w1_plane_raw", W1_RAW_AT), "w3": tile([P, H], U8, "w3_plane_raw")}
         for raw in plane_raw.values():
-            nc.vector.memset(raw.bitcast(I32), 0)
+            nc.vector.memset(raw[:].bitcast(I32), 0)
 
-        lists = {name: keep.tile([P, S // 16], U16, name="list_" + name) for name in ("down", "up", "own")}
-        w2_rows = w2.rearrange("(p i) c -> p i c", i=PACK)
-        tab = placed([P, T], I32, "tab", TAB_AT)
-        w3_raw = [held([P, BANK], I32, "w3_raw%d" % b) for b in range(PASSES)]
-        b1_sb = held([P, PASSES, PAIR * PACK], F32, "b1_sb")
-        b3_sb = held([P, PASSES, PAIR * PACK], F32, "b3_sb")
-        b4_sb = held([P, N // P], F32, "b4_sb")
+        lists = {name: keep.tile([P, S // 16], U16, name="list_" + name) for name in ("own", "up", "down")}
+        tab = tile([P, T], I32, "tab")
+        w1_raw = tile([P, 2 * H], U8, "w1_raw")
+        w3_raw = tile([P, H], I32, "w3_raw", W3_RAW_AT)
         w2_raw = {
-            (b, u): placed([P, PACK, c1 - c0], F32, "w2_raw%d%d" % (b, u), W2_AT[b] + 4 * PACK * c0)
+            (b, u): tile([P, PACK, c1 - c0], F32, "w2_raw%d%d" % (b, u))
             for b in range(PASSES)
             for u, (c0, c1) in enumerate(PIECES)
         }
+        w4_raw = [tile([P, PACK, N], F32, "w4_raw%d" % b, W4_RAW_AT[b]) for b in range(PASSES)]
+        b1_sb = tile([P, PASSES, PAIR * PACK], F32, "b1_sb")
+        b3_sb = tile([P, PASSES, PAIR * PACK], F32, "b3_sb")
+        b4_sb = tile([P, N // P], F32, "b4_sb")
+
+        w2_rows = w2.rearrange("(p i) c -> p i c", i=PACK)
+        w4_rows = w4.rearrange("(b g t v) n -> b v g t n", b=PASSES, t=PACK, v=PAIR)
 
         def load_w2(b, u):
             c0, c1 = PIECES[u]
             nc.sync.dma_start(out=w2_raw[b, u][:], in_=w2_rows[:, :, b * BANK + c0 : b * BANK + c1])
 
-        w4_raw = [held([P, PACK, N], F32, "w4_raw0"), placed([P, PACK, N], F32, "w4_raw1", W4_AT)]
-
         for name, src in (("own", offs), ("up", offs2), ("down", offs3)):
             nc.sync.dma_start(lists[name][:], src)
         load_scale_rows(nc, tab_plane, tab_scales[0])
-        load_w2(0, 0)
         nc.sync.dma_start(out=tab[:], in_=tab_words[0].rearrange("p t i -> p (t i)").bitcast(I32))
         load_scale_rows(nc, plane_raw["w1"], w1_scales[0])
+        load_w2(0, 0)
         nc.sync.dma_start(out=w1_raw[:].bitcast(I32), in_=w1_words[0].bitcast(I32))
         load_w2(0, 1)
         load_w2(0, 2)
-        load_w2(1, 0)
         load_scale_rows(nc, plane_raw["w3"], w3_scales[0])
-        load_w2(1, 1)
-        load_w2(1, 2)
-        w3_cols = w3_words[0].rearrange("p c i -> p (c i)").bitcast(I32)
-        nc.sync.dma_start(out=w3_raw[0][:], in_=w3_cols[:, 0:BANK])
+        nc.sync.dma_start(out=w3_raw[:], in_=w3_words[0].rearrange("p c i -> p (c i)").bitcast(I32))
+        for u in range(len(PIECES)):
+            load_w2(1, u)
         load_bias(nc, b1_sb, b1)
-        nc.sync.dma_start(out=w3_raw[1][:], in_=w3_cols[:, BANK : 2 * BANK])
-        w4_rows = w4.rearrange("(b g t v) n -> b v g t n", b=PASSES, t=PACK, v=PAIR)
+        load_bias(nc, b3_sb, b3)
         for b in range(PASSES):
             for v in range(PAIR):
                 nc.sync.dma_start(out=w4_raw[b][v:P:PAIR], in_=w4_rows[b, v])
-            if b == 0:
-                load_bias(nc, b3_sb, b3)
         with nc.allow_non_contiguous_dma(reason="one bias value a partition"):
             nc.sync.dma_start(out=b4_sb[:], in_=b4.rearrange("(c p) -> p c", p=P))
 
-        words_at = {
-            ("own", 1): W2_BF_AT[0],
-            ("up", 1): ROW_AT - WORDS,
-            ("down", 0): W3_AT + WORDS,
-            ("down", 1): W3_RAW_AT + BANK,
-        }
         picked = {}
 
+        def entries(name, halves):
+            return lists[name][:, halves[0] * BANK // 16 : (halves[-1] + 1) * BANK // 16]
+
         def gather_plane(name, halves, at=None):
-            label = "plane_%s%d" % (name, halves[0])
-            width = len(halves) * BANK
-            dst = held([P, width], U8, label) if at is None else placed([P, width], U8, label, at)
-            entries = lists[name][:, halves[0] * BANK // 16 : (halves[-1] + 1) * BANK // 16]
-            nc.vector.tensor_copy(dst[:], tab_plane[:].indirect(entries))
+            dst = tile([P, len(halves) * BANK], U8, "plane_%s%d" % (name, halves[0]), at)
+            nc.vector.tensor_copy(dst[:], tab_plane[:].indirect(entries(name, halves)))
             for i, half in enumerate(halves):
                 picked["plane", name, half] = dst[:, i * BANK : (i + 1) * BANK]
 
-        def gather_words(name, half):
-            label = "words_%s%d" % (name, half)
-            at = words_at.get((name, half))
-            dst = held([P, BANK], U32, label) if at is None else placed([P, BANK], U32, label, at)
-            entries = lists[name][:, half * BANK // 16 : (half + 1) * BANK // 16]
-            nc.vector.tensor_copy(dst[:], tab[:].bitcast(U32).indirect(entries))
+        def gather_words(name, half, at=None):
+            dst = tile([P, BANK], U32, "words_%s%d" % (name, half), at)
+            nc.vector.tensor_copy(dst[:], tab[:].bitcast(U32).indirect(entries(name, (half,))))
             picked["words", name, half] = dst[:]
 
-        w_plane = {"w1": held([P, H], U8, "w1_plane"), "w3": placed([P, H], U8, "w3_plane", ROW_AT)}
-        w3_dealt = [placed([P, BANK], I32, "w3_dealt0", W3_AT), held([P, BANK], I32, "w3_dealt1")]
-        w1_dealt = held([P, 2 * H], U8, "w1_dealt")
+        w_plane = {name: tile([P, H], U8, name + "_plane") for name in plane_raw}
+        w1_dealt = tile([P, 2 * H], U8, "w1_dealt")
+        w3_dealt = [tile([P, BANK], I32, "w3_dealt0"), tile([P, BANK], I32, "w3_dealt1", W3_DEALT_AT)]
 
         def deal_plane(name):
             nc.gpsimd.tensor_copy(
                 out=w_plane[name][:].rearrange("p (t g v) -> p t v g", t=PACK, v=PAIR),
-                in_=plane_raw[name].rearrange("p (g t v) -> p t v g", t=PACK, v=PAIR),
-            )
-
-        def deal_w3(b):
-            nc.gpsimd.tensor_copy(
-                out=w3_dealt[b][:].rearrange("p (t c i v) -> p c t i v", t=PACK, i=2, v=PAIR),
-                in_=w3_raw[b][:].rearrange("p (c i t v) -> p c t i v", t=PACK, i=2, v=PAIR),
+                in_=plane_raw[name][:].rearrange("p (g t v) -> p t v g", t=PACK, v=PAIR),
             )
 
         def deal_w1():
@@ -174,8 +151,14 @@ def tile_list_codon_context_rate_kernel(
                 in_=w1_raw[:].bitcast(I32).rearrange("p (c i t) -> p c t i", t=PACK, i=4),
             )
 
-        w2_bf = [placed([P, BANK * PACK], BF16, "w2_bf%d" % b, W2_BF_AT[b]) for b in range(PASSES)]
-        w2_codes = [held([P, BANK], U32, "w2_codes%d" % b) for b in range(PASSES)]
+        def deal_w3(b):
+            nc.gpsimd.tensor_copy(
+                out=w3_dealt[b][:].rearrange("p (t c i v) -> p c t i v", t=PACK, i=2, v=PAIR),
+                in_=w3_raw[:, b * BANK : (b + 1) * BANK].rearrange("p (c i t v) -> p c t i v", t=PACK, i=2, v=PAIR),
+            )
+
+        w2_bf = [tile([P, BANK * PACK], BF16, "w2_bf%d" % b, W2_BF_AT[b]) for b in range(PASSES)]
+        w2_codes = [tile([P, BANK], U32, "w2_codes%d" % b) for b in range(PASSES)]
         w2_plane = {}
 
         def cast_w2(b):
@@ -184,40 +167,24 @@ def tile_list_codon_context_rate_kernel(
                 src = w2_raw[b, u][:].rearrange("p i (g t v) -> p g t i v", t=PACK, v=PAIR)
                 nc.scalar.copy(out=dst[:, c0 // (PAIR * PACK) : c1 // (PAIR * PACK)], in_=src)
 
-        def quant_w2(b):
-            w2_plane[b] = held([P, BANK], U8, "w2_plane%d" % b)
+        def quant_w2(b, at=None):
+            w2_plane[b] = tile([P, BANK], U8, "w2_plane%d" % b, at)
             nc.vector.quantize_mx(out=w2_codes[b][:].bitcast(FP8X4), scales=w2_plane[b][:], in_=w2_bf[b][:])
 
-        w4_bf = [held([P, N * PACK], BF16, "w4_bf0"), placed([P, N * PACK], BF16, "w4_bf1", TAB_AT)]
-        w4_codes = held([P, PASSES * N], U32, "w4_codes")
-        w4_plane = placed([P, PASSES * N], U8, "w4_plane", W3_AT + PASSES * BANK)
+        w4_bf = {}
+        w4_codes = tile([P, PASSES * N], U32, "w4_codes")
+        w4_plane = {}
 
         def cast_w4(b):
+            w4_bf[b] = tile([P, N * PACK], BF16, "w4_bf%d" % b, W2_BF_AT[1] - WORDS + 64 if b == 0 else EARLY_AT)
             nc.gpsimd.tensor_copy(
                 out=w4_bf[b][:].rearrange("p (n t) -> p n t", t=PACK), in_=w4_raw[b][:].rearrange("p t n -> p n t")
             )
 
-        def quant_w4():
-            for b in range(PASSES):
-                cols = slice(b * N, (b + 1) * N)
-                nc.vector.quantize_mx(out=w4_codes[:, cols].bitcast(FP8X4), scales=w4_plane[:, cols], in_=w4_bf[b][:])
-
-        rate = {}
-        h_slices = {}
-        h_codes = {}
-        h_plane = {}
-        h_bf = {}
-
-        def pass_w2(acc, half, b, t, first):
-            nc.tensor.matmul_mx(
-                out=acc[:],
-                lhsT=w2_codes[b][:, t * P : (t + 1) * P].bitcast(FP8X4),
-                lhsT_scale=w2_plane[b][:, t * P : (t + 1) * P],
-                rhs=picked["words", "up", half].bitcast(FP8X4),
-                rhs_scale=picked["plane", "up", half],
-                start=first,
-                stop=not first,
-            )
+        def quant_w4(b, at):
+            w4_plane[b] = tile([P, N], U8, "w4_plane%d" % b, at)
+            codes = w4_codes[:, b * N : (b + 1) * N]
+            nc.vector.quantize_mx(out=codes.bitcast(FP8X4), scales=w4_plane[b][:], in_=w4_bf[b][:])
 
         def pass_w1(acc, half, b, t, first):
             c0 = t * M + b * P
@@ -231,7 +198,22 @@ def tile_list_codon_context_rate_kernel(
                 stop=not first,
             )
 
+        def pass_w2(acc, half, b, t, first):
+            nc.tensor.matmul_mx(
+                out=acc[:],
+                lhsT=w2_codes[b][:, t * P : (t + 1) * P].bitcast(FP8X4),
+                lhsT_scale=w2_plane[b][:, t * P : (t + 1) * P],
+                rhs=picked["words", "up", half].bitcast(FP8X4),
+                rhs_scale=picked["plane", "up", half],
+                start=first,
+                stop=not first,
+            )
+
         opened = {}
+        rate = {(half, b): tile([P, PACK, BANK], F32, "rate%d%d" % (half, b)) for half in range(2) for b in range(PASSES)}
+
+        def bias(sb, b, t):
+            return sb[:, b, PAIR * t : PAIR * t + 1]
 
         def open_e(half, b, banks, opening, slices=range(PACK)):
             for t in slices:
@@ -239,25 +221,23 @@ def tile_list_codon_context_rate_kernel(
                 opening(opened[half, b, t], half, b, t, True)
 
         def close_e(half, b, closing, slices=range(PACK)):
-            if (half, b) not in rate:
-                rate[half, b] = held([P, PACK, BANK], F32, "rate%d%d" % (half, b))
             for t in slices:
                 acc = opened[half, b, t]
                 closing(acc, half, b, t, False)
-                nc.scalar.activation(rate[half, b][:, t, :], acc[:], ACT.Exp, bias=b1_sb[:, b, PAIR * t : PAIR * t + 1])
+                nc.scalar.activation(rate[half, b][:, t, :], acc[:], ACT.Exp, bias=bias(b1_sb, b, t))
 
-        def stage_e(half, b, banks, slices):
+        def stage_e(half, b, banks, slices=range(PACK)):
             for t in slices:
                 open_e(half, b, banks, pass_w2, (t,))
                 close_e(half, b, pass_w1, (t,))
 
-        def product_d(half, b, banks, t):
-            acc = bank(banks[t])
-            cols = slice(t * M + b * P, t * M + (b + 1) * P)
+        def product_d(half, b, n, t):
+            acc = bank(n)
+            c0 = t * M + b * P
             nc.tensor.matmul_mx(
                 out=acc[:],
                 lhsT=w3_dealt[b][:, t * P : (t + 1) * P].bitcast(FP8X4),
-                lhsT_scale=w_plane["w3"][:, cols],
+                lhsT_scale=w_plane["w3"][:, c0 : c0 + P],
                 rhs=picked["words", "down", half].bitcast(FP8X4),
                 rhs_scale=picked["plane", "down", half],
                 start=True,
@@ -265,82 +245,84 @@ def tile_list_codon_context_rate_kernel(
             )
             return acc
 
-        def stage_d(half, b, banks, slices=range(PACK)):
-            if (half, b) not in h_slices:
-                h_slices[half, b] = held([P, PACK, BANK], BF16, "h_slices%d%d" % (half, b))
-            dst = h_slices[half, b]
-            for t in slices:
-                acc = product_d(half, b, banks, t)
-                nc.vector.scalar_tensor_tensor(
-                    dst[:, t, :], acc[:], b3_sb[:, b, PAIR * t : PAIR * t + 1], rate[half, b][:, t, :], ALU.add, ALU.mult
+        woven = {}
+
+        def first_unit(banks):
+            down = tile([P, PACK, BANK], F32, "down00", DOWN_AT)
+            for t in range(PACK):
+                acc = product_d(0, 0, banks[t], t)
+                nc.scalar.activation(down[:, t, :], acc[:], ACT.Identity, bias=bias(b3_sb, 0, t))
+            return down
+
+        def multiply_first(down):
+            woven[0, 0] = tile([P, BANK * PACK], BF16, "woven00", W4_RAW_AT[1])
+            dst = woven[0, 0][:].rearrange("p (c t) -> p c t", t=PACK)
+            for t in range(0, PACK, 2):
+                nc.gpsimd.tensor_tensor(
+                    out=dst[:, :, t : t + 2],
+                    in0=rate[0, 0][:, t : t + 2, :].rearrange("p t c -> p c t"),
+                    in1=down[:, t : t + 2, :].rearrange("p t c -> p c t"),
+                    op=ALU.mult,
                 )
 
-        last_down = held([P, PACK, BANK], F32, "last_down")
-
-        def stage_last_d(banks, t):
-            acc = product_d(*LAST, banks, t)
-            nc.scalar.activation(last_down[:, t, :], acc[:], ACT.Identity, bias=b3_sb[:, LAST[1], PAIR * t : PAIR * t + 1])
-
-        def multiply_last(j0, j1):
-            at = W3_AT + 3 * BANK if j0 == 0 else W3_RAW_AT + BANK + 2 * PACK * (j0 - TAIL[0][1])
-            dst = placed([P, (j1 - j0) * PACK], BF16, "h_bf11_%d" % j0, at)
-            nc.vector.tensor_tensor(
-                out=dst[:].rearrange("p (c i t) -> p c t i", i=2, t=PACK),
-                in0=rate[LAST][:, :, j0:j1].rearrange("p t (c i) -> p c t i", i=2),
-                in1=last_down[:, :, j0:j1].rearrange("p t (c i) -> p c t i", i=2),
-                op=ALU.mult,
+        def multiply(dst, acc, half, b, t, j0, j1):
+            nc.vector.scalar_tensor_tensor(
+                dst[:, t, :], acc[:, j0:j1], bias(b3_sb, b, t), rate[half, b][:, t, j0:j1], ALU.add, ALU.mult
             )
-            h_bf[(*LAST, j0)] = dst
 
-        def weave_views(half, b, j0, j1):
-            if (half, b, 0) not in h_bf:
-                label = "h_bf%d%d_0" % (half, b)
-                shape = [P, BANK * PACK]
-                h_bf[half, b, 0] = held(shape, BF16, label) if half or b else placed(shape, BF16, label, W4_AT)
-            return h_bf[half, b, 0][:, j0 * PACK : j1 * PACK], h_slices[half, b][:, :, j0:j1]
+        def stage_d(half, b, banks, at=None):
+            dst = tile([P, PACK, BANK], BF16, "slices%d%d" % (half, b), at)
+            for t in range(PACK):
+                multiply(dst, product_d(half, b, banks[t], t), half, b, t, 0, BANK)
+            return dst
 
-        def weave_gpsimd(half, b, j0, j1):
-            dst, src = weave_views(half, b, j0, j1)
+        def weave_gpsimd(dst, src):
             nc.gpsimd.tensor_copy(out=dst.rearrange("p (c t) -> p c t", t=PACK), in_=src.rearrange("p t c -> p c t"))
 
-        def weave_lines(copy, half, b, j0, j1):
-            dst, src = weave_views(half, b, j0, j1)
+        def weave_lines(copy, dst, src):
             copy(
                 out=dst.rearrange("p (c i t) -> p c t i", i=4, t=PACK),
                 in_=src.rearrange("p t (c i) -> p c t i", i=4),
             )
 
-        def quant_h(half, b, j0, j1):
-            src = h_bf[half, b, j0][:] if (half, b) == LAST else h_bf[half, b, 0][:, j0 * PACK : j1 * PACK]
-            codes = held([P, j1 - j0], U32, "h_codes%d%d_%d" % (half, b, j0))
-            label = "h_plane%d%d_%d" % (half, b, j0)
-            plane = placed([P, BANK], U8, label, W3_AT + b * BANK) if half == 0 else held([P, j1 - j0], U8, label)
+        h_codes = {}
+        h_plane = {}
+
+        def quant_h(half, b, j0, j1, src, at=None):
+            codes = tile([P, j1 - j0], U32, "h_codes%d%d_%d" % (half, b, j0))
+            plane = tile([P, j1 - j0], U8, "h_plane%d%d_%d" % (half, b, j0), at)
             nc.vector.quantize_mx(out=codes[:].bitcast(FP8X4), scales=plane[:], in_=src)
             for a0, a1 in ((0, BANK),) + TAIL:
                 if j0 <= a0 and a1 <= j1:
                     h_codes[half, b, a0, a1] = codes[:, a0 - j0 : a1 - j0]
                     h_plane[half, b, a0, a1] = plane[:, a0 - j0 : a1 - j0]
 
-        def stage_y(half, j0, j1, banks, shared_out=False, last=False):
+        def pass_y(acc, half, b, c, j0, j1):
+            nc.tensor.matmul_mx(
+                out=acc[:, 0 : j1 - j0],
+                lhsT=w4_codes[:, b * N + c * P : b * N + (c + 1) * P].bitcast(FP8X4),
+                lhsT_scale=w4_plane[b][:, c * P : (c + 1) * P],
+                rhs=h_codes[half, b, j0, j1].bitcast(FP8X4),
+                rhs_scale=h_plane[half, b, j0, j1],
+                start=(b == 0),
+                stop=(b == PASSES - 1),
+            )
+
+        def open_y(half, j0, j1, banks):
+            sums = [bank(n) for n in banks]
+            for c, acc in enumerate(sums):
+                pass_y(acc, half, 0, c, j0, j1)
+            return sums
+
+        def close_y(sums, half, j0, j1, shared_out=False, last=False):
             width = j1 - j0
             rows = out.rearrange("(c p) j -> p c j", p=P)[:, :, half * BANK + j0 : half * BANK + j1]
             joined = width < BANK and not last
             if joined:
-                both = held([P, N // P, width], F32, "res%d_%d" % (half, j0))
-            for c in range(N // P):
-                acc = bank(banks[c])
-                for b in range(PASSES):
-                    cols = slice(b * N + c * P, b * N + (c + 1) * P)
-                    nc.tensor.matmul_mx(
-                        out=acc[:, 0:width],
-                        lhsT=w4_codes[:, cols].bitcast(FP8X4),
-                        lhsT_scale=w4_plane[:, cols],
-                        rhs=h_codes[half, b, j0, j1].bitcast(FP8X4),
-                        rhs_scale=h_plane[half, b, j0, j1],
-                        start=(b == 0),
-                        stop=(b == PASSES - 1),
-                    )
-                res = both[:, c, :] if joined else held([P, width], F32, "res%d%d_%d" % (half, c, j0))[:]
+                both = tile([P, N // P, width], F32, "res%d_%d" % (half, j0))
+            for c, acc in enumerate(sums):
+                pass_y(acc, half, 1, c, j0, j1)
+                res = both[:, c, :] if joined else tile([P, width], F32, "res%d%d_%d" % (half, c, j0))[:]
                 if shared_out and c == 1:
                     nc.vector.tensor_scalar(res, acc[:, 0:width], b4_sb[:, c : c + 1], None, ALU.add)
                     queue = nc.sync
@@ -357,57 +339,75 @@ def tile_list_codon_context_rate_kernel(
         cast_w2(0)
         cast_w2(1)
         gather_words("own", 0)
+        gather_words("up", 0, UP_AT)
         deal_plane("w1")
         deal_w1()
-        open_e(0, 0, FRONT, pass_w1)
-        open_e(0, 1, BACK, pass_w1, (0, 1))
-        gather_words("up", 0)
-        gather_plane("up", (1,), W1_RAW_AT)
-        gather_plane("down", (0,), W1_RAW_AT + BANK)
+        open_e(0, 0, (0, 1, 2, 3), pass_w1)
+        open_e(0, 1, VECTOR_BANKS, pass_w1, (0, 1))
+        gather_plane("down", (0,), W1_RAW_AT)
+        gather_plane("up", (1,), W1_RAW_AT + BANK)
         quant_w2(0)
         close_e(0, 0, pass_w2)
-        gather_words("own", 1)
-        quant_w2(1)
-        close_e(0, 1, pass_w2, (0, 1))
-        stage_e(0, 1, BACK, (2, 3))
-        gather_words("up", 1)
         deal_plane("w3")
         deal_w3(0)
-        gather_words("down", 0)
-        open_e(1, 0, FRONT, pass_w1)
-        close_e(1, 0, pass_w2)
-        gather_plane("down", (1,), W3_RAW_AT)
-        gather_words("down", 1)
         deal_w3(1)
+        gather_words("down", 0, W3_RAW_AT)
+        down = first_unit(SCALAR_BANKS)
+        quant_w2(1)
+        close_e(0, 1, pass_w2, (0, 1))
+        stage_e(0, 1, VECTOR_BANKS, (2, 3))
+        row = W2_BF_AT[1] + 2 * WORDS - 128
+        gather_words("own", 1, row - WORDS + 64)
+        gather_words("up", 1, row + 64)
+        gather_plane("down", (1,), UP_AT)
+        gather_words("down", 1, UP_AT + BANK)
         cast_w4(0)
         cast_w4(1)
+        multiply_first(down)
 
-        stage_d(0, 0, BACK)
-        weave_gpsimd(0, 0, 0, BANK)
-        for t in range(PACK):
-            stage_e(*LAST, FRONT, (t,))
-            stage_d(0, 1, BACK, (t,))
-        weave_gpsimd(0, 1, 0, GPSIMD_SITES)
-        weave_lines(nc.scalar.copy, 0, 1, GPSIMD_SITES, BANK)
-        stage_d(1, 0, BACK)
-        for t in range(PACK):
-            stage_last_d(BACK[:2] + FRONT[:2], t)
-        cut = TAIL[0][1]
-        weave_lines(nc.scalar.copy, 1, 0, 0, cut)
-        weave_lines(nc.scalar.copy, 1, 0, cut, BANK - VECTOR_SITES)
-        weave_lines(nc.vector.tensor_copy, 1, 0, BANK - VECTOR_SITES, BANK)
+        e_banks, d_banks = SCALAR_BANKS[:2] + VECTOR_BANKS[:2], SCALAR_BANKS[2:] + VECTOR_BANKS[2:]
+        slices01 = tile([P, PACK, BANK], BF16, "slices01", SLICES_AT)
+        for pair in ((0, 1), (2, 3)):
+            stage_e(1, 0, e_banks, pair)
+            for t in pair:
+                multiply(slices01, product_d(0, 1, d_banks[t], t), 0, 1, t, 0, BANK)
+        first, second = TAIL
+        woven01 = [tile([P, N * PACK], BF16, "woven01_0", DOWN_AT + WORDS)]
+        weave_gpsimd(woven01[0][:], slices01[:, :, first[0] : first[1]])
+        slices10 = stage_d(1, 0, d_banks)
+        quant_h(0, 0, 0, BANK, woven[0, 0][:])
+        quant_w4(0, DOWN_AT)
+        quant_w4(1, DOWN_AT + N)
+        woven01.append(tile([P, N * PACK], BF16, "woven01_1", EARLY_AT))
+        weave_gpsimd(woven01[1][:], slices01[:, :, second[0] : second[1]])
+        stage_e(1, 1, e_banks)
+        opened_y = open_y(0, 0, BANK, e_banks[:2])
+        last_sums = [product_d(1, 1, d_banks[t], t) for t in range(PACK)]
 
-        quant_h(0, 0, 0, BANK)
-        quant_w4()
-        quant_h(0, 1, 0, BANK)
-        stage_y(0, 0, BANK, FRONT[2:])
-        multiply_last(*TAIL[0])
-        multiply_last(*TAIL[1])
-        quant_h(*LAST, *TAIL[0])
-        quant_h(1, 0, 0, cut)
-        multiply_last(*TAIL[2])
-        quant_h(*LAST, *TAIL[1])
-        quant_h(1, 0, cut, BANK)
-        quant_h(*LAST, *TAIL[2])
-        for piece, banks in zip(TAIL, (BACK[2:], FRONT[:2], BACK[:2])):
-            stage_y(1, *piece, banks, shared_out=(piece != TAIL[0]), last=(piece == TAIL[-1]))
+        def multiply_last(j0, j1, at=None):
+            dst = tile([P, PACK, j1 - j0], BF16, "slices11_%d" % j0, at)
+            for t in range(PACK):
+                multiply(dst, last_sums[t], 1, 1, t, j0, j1)
+            return dst
+
+        def piece_tile(b, j0, j1, at=None):
+            woven[1, b, j0] = tile([P, (j1 - j0) * PACK], BF16, "woven1%d_%d" % (b, j0), at)
+            return woven[1, b, j0][:]
+
+        for j0, j1 in TAIL:
+            weave_lines(nc.scalar.copy, piece_tile(0, j0, j1), slices10[:, :, j0:j1])
+        weave_lines(nc.scalar.copy, piece_tile(1, *first), multiply_last(*first, W4_RAW_AT[1])[:])
+        codes = tile([P, BANK], U32, "h_codes01")
+        plane = tile([P, BANK], U8, "h_plane01", SLICES_AT + WORDS)
+        for src, (j0, j1) in zip(woven01, TAIL):
+            nc.vector.quantize_mx(out=codes[:, j0:j1].bitcast(FP8X4), scales=plane[:, j0:j1], in_=src[:])
+        h_codes[0, 1, 0, BANK], h_plane[0, 1, 0, BANK] = codes[:], plane[:]
+        close_y(opened_y, 0, 0, BANK)
+        last = multiply_last(*second, SLICES_AT)
+        quant_h(1, 0, *first, woven[1, 0, first[0]][:], EARLY_AT)
+        quant_h(1, 0, *second, woven[1, 0, second[0]][:], EARLY_AT + N)
+        weave_lines(nc.vector.tensor_copy, piece_tile(1, *second, EARLY_AT + 3 * N), last[:])
+        quant_h(1, 1, *first, woven[1, 1, first[0]][:], EARLY_AT + 2 * N)
+        close_y(open_y(1, *first, e_banks[2:]), 1, *first, shared_out=True)
+        quant_h(1, 1, *second, woven[1, 1, second[0]][:])
+        close_y(open_y(1, *second, d_banks[:2]), 1, *second, shared_out=True, last=True)

@@ -20,23 +20,20 @@ P = 128
 PACK = 4
 PAIR = 2
 BANK = 512
-VECTOR_BANKS, SCALAR_BANKS = (4, 5, 0, 1), (6, 7, 2, 3)
+FRONT, BACK = (0, 1, 2, 3), (4, 5, 6, 7)
 PASSES = H // (P * PACK)
 M = H // PACK
 PIECES = ((0, 256), (256, 384), (384, 512))
-TAIL = ((0, 256), (256, 512))
-GPSIMD_SITES = 256
+TAIL = ((0, 256), (256, 384), (384, 512))
+GPSIMD_SITES = 384
 
 WORDS = 4 * BANK
 W1_RAW_AT = 0
-W3_RAW_AT = 2 * WORDS
-W2_BF_AT = (4 * WORDS, 6 * WORDS)
-W4_RAW_AT = (10 * WORDS, 12 * WORDS)
-DOWN_AT = 14 * WORDS
-SLICES_AT = 18 * WORDS
-EARLY_AT = 22 * WORDS
-UP_AT = 25 * WORDS
-W3_DEALT_AT = 20 * WORDS
+W2_PIECE_AT = 2 * WORDS
+W2_BF_AT = 5 * WORDS
+W3_DEALT_AT = W2_BF_AT - WORDS + 64
+W4_RAW_AT = (None, 8 * WORDS)
+RATE_AT = 12 * WORDS
 
 
 def load_scale_rows(nc, plane, rows):
@@ -80,9 +77,9 @@ def tile_list_codon_context_rate_kernel(
         lists = {name: keep.tile([P, S // 16], U16, name="list_" + name) for name in ("own", "up", "down")}
         tab = tile([P, T], I32, "tab")
         w1_raw = tile([P, 2 * H], U8, "w1_raw")
-        w3_raw = tile([P, H], I32, "w3_raw", W3_RAW_AT)
+        w3_raw = [tile([P, BANK], I32, "w3_raw%d" % b) for b in range(PASSES)]
         w2_raw = {
-            (b, u): tile([P, PACK, c1 - c0], F32, "w2_raw%d%d" % (b, u))
+            (b, u): tile([P, PACK, c1 - c0], F32, "w2_raw%d%d" % (b, u), W2_PIECE_AT if (b, u) == (1, 0) else None)
             for b in range(PASSES)
             for u, (c0, c1) in enumerate(PIECES)
         }
@@ -98,7 +95,7 @@ def tile_list_codon_context_rate_kernel(
             c0, c1 = PIECES[u]
             nc.sync.dma_start(out=w2_raw[b, u][:], in_=w2_rows[:, :, b * BANK + c0 : b * BANK + c1])
 
-        for name, src in (("own", offs), ("up", offs2), ("down", offs3)):
+        for name, src in (("own", offs), ("up", offs2)):
             nc.sync.dma_start(lists[name][:], src)
         load_scale_rows(nc, tab_plane, tab_scales[0])
         nc.sync.dma_start(out=tab[:], in_=tab_words[0].rearrange("p t i -> p (t i)").bitcast(I32))
@@ -108,14 +105,17 @@ def tile_list_codon_context_rate_kernel(
         load_w2(0, 1)
         load_w2(0, 2)
         load_scale_rows(nc, plane_raw["w3"], w3_scales[0])
-        nc.sync.dma_start(out=w3_raw[:], in_=w3_words[0].rearrange("p c i -> p (c i)").bitcast(I32))
         for u in range(len(PIECES)):
             load_w2(1, u)
+        w3_cols = w3_words[0].rearrange("p c i -> p (c i)").bitcast(I32)
+        nc.sync.dma_start(out=w3_raw[0][:], in_=w3_cols[:, 0:BANK])
+        nc.sync.dma_start(lists["down"][:], offs3)
         load_bias(nc, b1_sb, b1)
-        load_bias(nc, b3_sb, b3)
+        nc.sync.dma_start(out=w3_raw[1][:], in_=w3_cols[:, BANK : 2 * BANK])
         for b in range(PASSES):
             for v in range(PAIR):
                 nc.sync.dma_start(out=w4_raw[b][v:P:PAIR], in_=w4_rows[b, v])
+        load_bias(nc, b3_sb, b3)
         with nc.allow_non_contiguous_dma(reason="one bias value a partition"):
             nc.sync.dma_start(out=b4_sb[:], in_=b4.rearrange("(c p) -> p c", p=P))
 
@@ -137,7 +137,7 @@ def tile_list_codon_context_rate_kernel(
 
         w_plane = {name: tile([P, H], U8, name + "_plane") for name in plane_raw}
         w1_dealt = tile([P, 2 * H], U8, "w1_dealt")
-        w3_dealt = [tile([P, BANK], I32, "w3_dealt0"), tile([P, BANK], I32, "w3_dealt1", W3_DEALT_AT)]
+        w3_dealt = [tile([P, BANK], I32, "w3_dealt0", W3_DEALT_AT), tile([P, BANK], I32, "w3_dealt1", W2_BF_AT + 64)]
 
         def deal_plane(name):
             nc.gpsimd.tensor_copy(
@@ -154,10 +154,10 @@ def tile_list_codon_context_rate_kernel(
         def deal_w3(b):
             nc.gpsimd.tensor_copy(
                 out=w3_dealt[b][:].rearrange("p (t c i v) -> p c t i v", t=PACK, i=2, v=PAIR),
-                in_=w3_raw[:, b * BANK : (b + 1) * BANK].rearrange("p (c i t v) -> p c t i v", t=PACK, i=2, v=PAIR),
+                in_=w3_raw[b][:].rearrange("p (c i t v) -> p c t i v", t=PACK, i=2, v=PAIR),
             )
 
-        w2_bf = [tile([P, BANK * PACK], BF16, "w2_bf%d" % b, W2_BF_AT[b]) for b in range(PASSES)]
+        w2_bf = [tile([P, BANK * PACK], BF16, "w2_bf%d" % b, W2_BF_AT if b else None) for b in range(PASSES)]
         w2_codes = [tile([P, BANK], U32, "w2_codes%d" % b) for b in range(PASSES)]
         w2_plane = {}
 
@@ -171,20 +171,22 @@ def tile_list_codon_context_rate_kernel(
             w2_plane[b] = tile([P, BANK], U8, "w2_plane%d" % b, at)
             nc.vector.quantize_mx(out=w2_codes[b][:].bitcast(FP8X4), scales=w2_plane[b][:], in_=w2_bf[b][:])
 
-        w4_bf = {}
+        w4_bf = tile([P, PASSES, N * PACK], BF16, "w4_bf")
         w4_codes = tile([P, PASSES * N], U32, "w4_codes")
         w4_plane = {}
 
         def cast_w4(b):
-            w4_bf[b] = tile([P, N * PACK], BF16, "w4_bf%d" % b, W2_BF_AT[1] - WORDS + 64 if b == 0 else EARLY_AT)
             nc.gpsimd.tensor_copy(
-                out=w4_bf[b][:].rearrange("p (n t) -> p n t", t=PACK), in_=w4_raw[b][:].rearrange("p t n -> p n t")
+                out=w4_bf[:, b, :].rearrange("p (n t) -> p n t", t=PACK), in_=w4_raw[b][:].rearrange("p t n -> p n t")
             )
 
-        def quant_w4(b, at):
-            w4_plane[b] = tile([P, N], U8, "w4_plane%d" % b, at)
-            codes = w4_codes[:, b * N : (b + 1) * N]
-            nc.vector.quantize_mx(out=codes.bitcast(FP8X4), scales=w4_plane[b][:], in_=w4_bf[b][:])
+        def quant_w4(at):
+            plane = tile([P, PASSES * N], U8, "w4_plane", at)
+            for b in range(PASSES):
+                w4_plane[b] = plane[:, b * N : (b + 1) * N]
+            nc.vector.quantize_mx(
+                out=w4_codes[:].bitcast(FP8X4), scales=plane[:], in_=w4_bf[:].rearrange("p b c -> p (b c)")
+            )
 
         def pass_w1(acc, half, b, t, first):
             c0 = t * M + b * P
@@ -210,7 +212,7 @@ def tile_list_codon_context_rate_kernel(
             )
 
         opened = {}
-        rate = {(half, b): tile([P, PACK, BANK], F32, "rate%d%d" % (half, b)) for half in range(2) for b in range(PASSES)}
+        rate = {(half, b): tile([P, PACK, BANK], F32, "rate%d%d" % (half, b), None if half or b else RATE_AT) for half in range(2) for b in range(PASSES)}
 
         def bias(sb, b, t):
             return sb[:, b, PAIR * t : PAIR * t + 1]
@@ -247,24 +249,6 @@ def tile_list_codon_context_rate_kernel(
 
         woven = {}
 
-        def first_unit(banks):
-            down = tile([P, PACK, BANK], F32, "down00", DOWN_AT)
-            for t in range(PACK):
-                acc = product_d(0, 0, banks[t], t)
-                nc.scalar.activation(down[:, t, :], acc[:], ACT.Identity, bias=bias(b3_sb, 0, t))
-            return down
-
-        def multiply_first(down):
-            woven[0, 0] = tile([P, BANK * PACK], BF16, "woven00", W4_RAW_AT[1])
-            dst = woven[0, 0][:].rearrange("p (c t) -> p c t", t=PACK)
-            for t in range(0, PACK, 2):
-                nc.gpsimd.tensor_tensor(
-                    out=dst[:, :, t : t + 2],
-                    in0=rate[0, 0][:, t : t + 2, :].rearrange("p t c -> p c t"),
-                    in1=down[:, t : t + 2, :].rearrange("p t c -> p c t"),
-                    op=ALU.mult,
-                )
-
         def multiply(dst, acc, half, b, t, j0, j1):
             nc.vector.scalar_tensor_tensor(
                 dst[:, t, :], acc[:, j0:j1], bias(b3_sb, b, t), rate[half, b][:, t, j0:j1], ALU.add, ALU.mult
@@ -288,14 +272,19 @@ def tile_list_codon_context_rate_kernel(
         h_codes = {}
         h_plane = {}
 
-        def quant_h(half, b, j0, j1, src, at=None):
-            codes = tile([P, j1 - j0], U32, "h_codes%d%d_%d" % (half, b, j0))
-            plane = tile([P, j1 - j0], U8, "h_plane%d%d_%d" % (half, b, j0), at)
+        def quant_h(src, half, part, at=None):
+            width = sum(j1 - j0 for b, j0, j1 in part)
+            label = "%d_%d_%d" % (half, *part[0][:2])
+            codes = tile([P, width], U32, "h_codes" + label)
+            plane = tile([P, width], U8, "h_plane" + label, at)
             nc.vector.quantize_mx(out=codes[:].bitcast(FP8X4), scales=plane[:], in_=src)
-            for a0, a1 in ((0, BANK),) + TAIL:
-                if j0 <= a0 and a1 <= j1:
-                    h_codes[half, b, a0, a1] = codes[:, a0 - j0 : a1 - j0]
-                    h_plane[half, b, a0, a1] = plane[:, a0 - j0 : a1 - j0]
+            start = 0
+            for b, j0, j1 in part:
+                for a0, a1 in ((0, BANK),) + TAIL:
+                    if j0 <= a0 and a1 <= j1:
+                        h_codes[half, b, a0, a1] = codes[:, start + a0 - j0 : start + a1 - j0]
+                        h_plane[half, b, a0, a1] = plane[:, start + a0 - j0 : start + a1 - j0]
+                start += j1 - j0
 
         def pass_y(acc, half, b, c, j0, j1):
             nc.tensor.matmul_mx(
@@ -308,20 +297,19 @@ def tile_list_codon_context_rate_kernel(
                 stop=(b == PASSES - 1),
             )
 
-        def open_y(half, j0, j1, banks):
+        def stage_y(banks, half, j0, j1, shared_out=False, last=False):
             sums = [bank(n) for n in banks]
-            for c, acc in enumerate(sums):
-                pass_y(acc, half, 0, c, j0, j1)
-            return sums
-
-        def close_y(sums, half, j0, j1, shared_out=False, last=False):
+            if last:
+                for c, acc in enumerate(sums):
+                    pass_y(acc, half, 0, c, j0, j1)
             width = j1 - j0
             rows = out.rearrange("(c p) j -> p c j", p=P)[:, :, half * BANK + j0 : half * BANK + j1]
             joined = width < BANK and not last
             if joined:
                 both = tile([P, N // P, width], F32, "res%d_%d" % (half, j0))
             for c, acc in enumerate(sums):
-                pass_y(acc, half, 1, c, j0, j1)
+                for b in range(1 if last else 0, PASSES):
+                    pass_y(acc, half, b, c, j0, j1)
                 res = both[:, c, :] if joined else tile([P, width], F32, "res%d%d_%d" % (half, c, j0))[:]
                 if shared_out and c == 1:
                     nc.vector.tensor_scalar(res, acc[:, 0:width], b4_sb[:, c : c + 1], None, ALU.add)
@@ -334,80 +322,84 @@ def tile_list_codon_context_rate_kernel(
             if joined:
                 nc.sync.dma_start(out=rows, in_=both[:])
 
+        last_down = tile([P, PACK, BANK], F32, "last_down")
+
+        def stage_last_d(banks, t):
+            acc = product_d(1, 1, banks[t], t)
+            nc.scalar.activation(last_down[:, t, :], acc[:], ACT.Identity, bias=bias(b3_sb, 1, t))
+
+        def multiply_last(j0, j1, dst):
+            nc.vector.tensor_tensor(
+                out=dst.rearrange("p (c i t) -> p c t i", i=2, t=PACK),
+                in0=rate[1, 1][:, :, j0:j1].rearrange("p t (c i) -> p c t i", i=2),
+                in1=last_down[:, :, j0:j1].rearrange("p t (c i) -> p c t i", i=2),
+                op=ALU.mult,
+            )
+
         gather_plane("own", (0, 1))
         gather_plane("up", (0,))
         cast_w2(0)
         cast_w2(1)
         gather_words("own", 0)
-        gather_words("up", 0, UP_AT)
+        gather_words("up", 0)
         deal_plane("w1")
         deal_w1()
-        open_e(0, 0, (0, 1, 2, 3), pass_w1)
-        open_e(0, 1, VECTOR_BANKS, pass_w1, (0, 1))
-        gather_plane("down", (0,), W1_RAW_AT)
-        gather_plane("up", (1,), W1_RAW_AT + BANK)
+        deal_plane("w3")
+        open_e(0, 0, FRONT, pass_w1)
+        open_e(0, 1, BACK, pass_w1)
+        gather_plane("up", (1,), W1_RAW_AT)
+        gather_words("own", 1, W1_RAW_AT + BANK)
         quant_w2(0)
         close_e(0, 0, pass_w2)
-        deal_plane("w3")
+        gather_words("up", 1, W2_PIECE_AT)
+        quant_w2(1)
+        close_e(0, 1, pass_w2)
         deal_w3(0)
         deal_w3(1)
-        gather_words("down", 0, W3_RAW_AT)
-        down = first_unit(SCALAR_BANKS)
-        quant_w2(1)
-        close_e(0, 1, pass_w2, (0, 1))
-        stage_e(0, 1, VECTOR_BANKS, (2, 3))
-        row = W2_BF_AT[1] + 2 * WORDS - 128
-        gather_words("own", 1, row - WORDS + 64)
-        gather_words("up", 1, row + 64)
-        gather_plane("down", (1,), UP_AT)
-        gather_words("down", 1, UP_AT + BANK)
         cast_w4(0)
         cast_w4(1)
-        multiply_first(down)
+        gather_plane("down", (0,))
+        gather_words("down", 0)
+        gather_plane("down", (1,))
+        e_banks, d_banks = FRONT[:2] + BACK[2:], FRONT[2:] + BACK[:2]
+        stage_e(1, 0, e_banks, (0, 1))
+        slices00 = stage_d(0, 0, d_banks)
+        stage_e(1, 0, e_banks, (2, 3))
+        first_half = tile([P, PASSES, BANK * PACK], BF16, "woven0", W4_RAW_AT[1])
+        weave_gpsimd(first_half[:, 0, :], slices00[:])
+        gather_words("down", 1, RATE_AT)
+        stage_e(1, 1, d_banks)
+        slices01 = stage_d(0, 1, e_banks)
+        cut = GPSIMD_SITES
+        weave_gpsimd(first_half[:, 1, 0 : cut * PACK], slices01[:, :, 0:cut])
+        weave_lines(nc.scalar.copy, first_half[:, 1, cut * PACK :], slices01[:, :, cut:])
+        slices10 = tile([P, PACK, BANK], BF16, "slices10")
+        for t in range(PACK):
+            multiply(slices10, product_d(1, 0, d_banks[t], t), 1, 0, t, 0, BANK)
+            stage_last_d(e_banks, t)
 
-        e_banks, d_banks = SCALAR_BANKS[:2] + VECTOR_BANKS[:2], SCALAR_BANKS[2:] + VECTOR_BANKS[2:]
-        slices01 = tile([P, PACK, BANK], BF16, "slices01", SLICES_AT)
-        for pair in ((0, 1), (2, 3)):
-            stage_e(1, 0, e_banks, pair)
-            for t in pair:
-                multiply(slices01, product_d(0, 1, d_banks[t], t), 0, 1, t, 0, BANK)
-        first, second = TAIL
-        woven01 = [tile([P, N * PACK], BF16, "woven01_0", DOWN_AT + WORDS)]
-        weave_gpsimd(woven01[0][:], slices01[:, :, first[0] : first[1]])
-        slices10 = stage_d(1, 0, d_banks)
-        quant_h(0, 0, 0, BANK, woven[0, 0][:])
-        quant_w4(0, DOWN_AT)
-        quant_w4(1, DOWN_AT + N)
-        woven01.append(tile([P, N * PACK], BF16, "woven01_1", EARLY_AT))
-        weave_gpsimd(woven01[1][:], slices01[:, :, second[0] : second[1]])
-        stage_e(1, 1, e_banks)
-        opened_y = open_y(0, 0, BANK, e_banks[:2])
-        last_sums = [product_d(1, 1, d_banks[t], t) for t in range(PACK)]
+        cut = TAIL[0][1]
+        parts = (((0, 0, cut), (1, *TAIL[0])), ((0, cut, BANK), (1, *TAIL[1])), ((1, *TAIL[2]),))
+        inputs = {}
+        joined = []
+        for n, part in enumerate(parts):
+            width = sum(j1 - j0 for b, j0, j1 in part)
+            joined.append(tile([P, width * PACK], BF16, "woven1_%d" % n))
+            at = 0
+            for b, j0, j1 in part:
+                inputs[b, j0] = joined[n][:, at * PACK : (at + j1 - j0) * PACK]
+                at += j1 - j0
+        weave_lines(nc.scalar.copy, inputs[0, 0], slices10[:, :, 0:cut])
+        weave_lines(nc.scalar.copy, inputs[0, cut], slices10[:, :, cut:])
 
-        def multiply_last(j0, j1, at=None):
-            dst = tile([P, PACK, j1 - j0], BF16, "slices11_%d" % j0, at)
-            for t in range(PACK):
-                multiply(dst, last_sums[t], 1, 1, t, j0, j1)
-            return dst
-
-        def piece_tile(b, j0, j1, at=None):
-            woven[1, b, j0] = tile([P, (j1 - j0) * PACK], BF16, "woven1%d_%d" % (b, j0), at)
-            return woven[1, b, j0][:]
-
-        for j0, j1 in TAIL:
-            weave_lines(nc.scalar.copy, piece_tile(0, j0, j1), slices10[:, :, j0:j1])
-        weave_lines(nc.scalar.copy, piece_tile(1, *first), multiply_last(*first, W4_RAW_AT[1])[:])
-        codes = tile([P, BANK], U32, "h_codes01")
-        plane = tile([P, BANK], U8, "h_plane01", SLICES_AT + WORDS)
-        for src, (j0, j1) in zip(woven01, TAIL):
-            nc.vector.quantize_mx(out=codes[:, j0:j1].bitcast(FP8X4), scales=plane[:, j0:j1], in_=src[:])
-        h_codes[0, 1, 0, BANK], h_plane[0, 1, 0, BANK] = codes[:], plane[:]
-        close_y(opened_y, 0, 0, BANK)
-        last = multiply_last(*second, SLICES_AT)
-        quant_h(1, 0, *first, woven[1, 0, first[0]][:], EARLY_AT)
-        quant_h(1, 0, *second, woven[1, 0, second[0]][:], EARLY_AT + N)
-        weave_lines(nc.vector.tensor_copy, piece_tile(1, *second, EARLY_AT + 3 * N), last[:])
-        quant_h(1, 1, *first, woven[1, 1, first[0]][:], EARLY_AT + 2 * N)
-        close_y(open_y(1, *first, e_banks[2:]), 1, *first, shared_out=True)
-        quant_h(1, 1, *second, woven[1, 1, second[0]][:])
-        close_y(open_y(1, *second, d_banks[:2]), 1, *second, shared_out=True, last=True)
+        quant_w4(W3_DEALT_AT)
+        quant_h(first_half[:].rearrange("p b c -> p (b c)"), 0, ((0, 0, BANK), (1, 0, BANK)), W3_DEALT_AT + BANK)
+        stage_y(e_banks[:2], 0, 0, BANK)
+        multiply_last(*TAIL[0], inputs[1, TAIL[0][0]])
+        multiply_last(*TAIL[1], inputs[1, TAIL[1][0]])
+        quant_h(joined[0][:], 1, parts[0])
+        multiply_last(*TAIL[2], inputs[1, TAIL[2][0]])
+        quant_h(joined[1][:], 1, parts[1])
+        quant_h(joined[2][:], 1, parts[2])
+        for piece, banks in zip(TAIL, (e_banks[2:], d_banks[:2], d_banks[2:])):
+            stage_y(banks, 1, *piece, shared_out=(piece != TAIL[0]), last=(piece == TAIL[-1]))

@@ -23,12 +23,11 @@ BANK = 512
 FRONT, BACK = (0, 1, 2, 3), (4, 5, 6, 7)
 PASSES = H // (P * PACK)
 M = H // PACK
-PIECES = ((0, 256), (256, 384), (384, 512))
+PIECES = (((0, 256), (256, 512)), ((0, 256), (256, 384), (384, 512)))
 TAIL = ((0, 256), (256, 384), (384, 512))
-GPSIMD_SITES = 384
+GPSIMD_SITES = 256
 
 WORDS = 4 * BANK
-W1_RAW_AT = 0
 W2_PIECE_AT = 2 * WORDS
 W2_BF_AT = 5 * WORDS
 W3_DEALT_AT = W2_BF_AT - WORDS + 64
@@ -70,7 +69,7 @@ def tile_list_codon_context_rate_kernel(
 
         tab_plane = tile([P, T], U8, "tab_plane")
         nc.gpsimd.memset(tab_plane[:].bitcast(I32), 0)
-        plane_raw = {"w1": tile([P, H], U8, "w1_plane_raw", W1_RAW_AT), "w3": tile([P, H], U8, "w3_plane_raw")}
+        plane_raw = {"w1": tile([P, H], U8, "w1_plane_raw"), "w3": tile([P, H], U8, "w3_plane_raw")}
         for raw in plane_raw.values():
             nc.vector.memset(raw[:].bitcast(I32), 0)
 
@@ -81,7 +80,7 @@ def tile_list_codon_context_rate_kernel(
         w2_raw = {
             (b, u): tile([P, PACK, c1 - c0], F32, "w2_raw%d%d" % (b, u), W2_PIECE_AT if (b, u) == (1, 0) else None)
             for b in range(PASSES)
-            for u, (c0, c1) in enumerate(PIECES)
+            for u, (c0, c1) in enumerate(PIECES[b])
         }
         w4_raw = [tile([P, PACK, N], F32, "w4_raw%d" % b, W4_RAW_AT[b]) for b in range(PASSES)]
         b1_sb = tile([P, PASSES, PAIR * PACK], F32, "b1_sb")
@@ -92,7 +91,7 @@ def tile_list_codon_context_rate_kernel(
         w4_rows = w4.rearrange("(b g t v) n -> b v g t n", b=PASSES, t=PACK, v=PAIR)
 
         def load_w2(b, u):
-            c0, c1 = PIECES[u]
+            c0, c1 = PIECES[b][u]
             nc.sync.dma_start(out=w2_raw[b, u][:], in_=w2_rows[:, :, b * BANK + c0 : b * BANK + c1])
 
         for name, src in (("own", offs), ("up", offs2)):
@@ -103,9 +102,8 @@ def tile_list_codon_context_rate_kernel(
         load_w2(0, 0)
         nc.sync.dma_start(out=w1_raw[:].bitcast(I32), in_=w1_words[0].bitcast(I32))
         load_w2(0, 1)
-        load_w2(0, 2)
         load_scale_rows(nc, plane_raw["w3"], w3_scales[0])
-        for u in range(len(PIECES)):
+        for u in range(len(PIECES[1])):
             load_w2(1, u)
         w3_cols = w3_words[0].rearrange("p c i -> p (c i)").bitcast(I32)
         nc.sync.dma_start(out=w3_raw[0][:], in_=w3_cols[:, 0:BANK])
@@ -130,10 +128,11 @@ def tile_list_codon_context_rate_kernel(
             for i, half in enumerate(halves):
                 picked["plane", name, half] = dst[:, i * BANK : (i + 1) * BANK]
 
-        def gather_words(name, half, at=None):
-            dst = tile([P, BANK], U32, "words_%s%d" % (name, half), at)
-            nc.vector.tensor_copy(dst[:], tab[:].bitcast(U32).indirect(entries(name, (half,))))
-            picked["words", name, half] = dst[:]
+        def gather_words(name, halves, at=None):
+            dst = tile([P, len(halves) * BANK], U32, "words_%s%d" % (name, halves[0]), at)
+            nc.vector.tensor_copy(dst[:], tab[:].bitcast(U32).indirect(entries(name, halves)))
+            for i, half in enumerate(halves):
+                picked["words", name, half] = dst[:, i * BANK : (i + 1) * BANK]
 
         w_plane = {name: tile([P, H], U8, name + "_plane") for name in plane_raw}
         w1_dealt = tile([P, 2 * H], U8, "w1_dealt")
@@ -163,7 +162,7 @@ def tile_list_codon_context_rate_kernel(
 
         def cast_w2(b):
             dst = w2_bf[b][:].rearrange("p (t g v i) -> p g t i v", t=PACK, v=PAIR, i=PACK)
-            for u, (c0, c1) in enumerate(PIECES):
+            for u, (c0, c1) in enumerate(PIECES[b]):
                 src = w2_raw[b, u][:].rearrange("p i (g t v) -> p g t i v", t=PACK, v=PAIR)
                 nc.scalar.copy(out=dst[:, c0 // (PAIR * PACK) : c1 // (PAIR * PACK)], in_=src)
 
@@ -340,34 +339,32 @@ def tile_list_codon_context_rate_kernel(
         gather_plane("up", (0,))
         cast_w2(0)
         cast_w2(1)
-        gather_words("own", 0)
-        gather_words("up", 0)
+        gather_words("own", (0,))
+        gather_words("own", (1,))
+        gather_words("up", (0, 1))
         deal_plane("w1")
         deal_w1()
         deal_plane("w3")
         open_e(0, 0, FRONT, pass_w1)
-        open_e(0, 1, BACK, pass_w1)
-        gather_plane("up", (1,), W1_RAW_AT)
-        gather_words("own", 1, W1_RAW_AT + BANK)
+        open_e(1, 0, BACK, pass_w1)
         quant_w2(0)
         close_e(0, 0, pass_w2)
-        gather_words("up", 1, W2_PIECE_AT)
+        gather_plane("up", (1,), W2_PIECE_AT)
+        close_e(1, 0, pass_w2)
         quant_w2(1)
-        close_e(0, 1, pass_w2)
         deal_w3(0)
         deal_w3(1)
         cast_w4(0)
         cast_w4(1)
         gather_plane("down", (0,))
-        gather_words("down", 0)
+        gather_words("down", (0,))
         gather_plane("down", (1,))
-        e_banks, d_banks = FRONT[:2] + BACK[2:], FRONT[2:] + BACK[:2]
-        stage_e(1, 0, e_banks, (0, 1))
-        slices00 = stage_d(0, 0, d_banks)
-        stage_e(1, 0, e_banks, (2, 3))
+        stage_e(0, 1, FRONT)
+        slices00 = stage_d(0, 0, BACK)
+        e_banks, d_banks = FRONT[:1] + BACK[:1] + BACK[2:], FRONT[1:] + BACK[1:2]
         first_half = tile([P, PASSES, BANK * PACK], BF16, "woven0", W4_RAW_AT[1])
         weave_gpsimd(first_half[:, 0, :], slices00[:])
-        gather_words("down", 1, RATE_AT)
+        gather_words("down", (1,), RATE_AT)
         stage_e(1, 1, d_banks)
         slices01 = stage_d(0, 1, e_banks)
         cut = GPSIMD_SITES
@@ -375,8 +372,8 @@ def tile_list_codon_context_rate_kernel(
         weave_lines(nc.scalar.copy, first_half[:, 1, cut * PACK :], slices01[:, :, cut:])
         slices10 = tile([P, PACK, BANK], BF16, "slices10")
         for t in range(PACK):
-            multiply(slices10, product_d(1, 0, d_banks[t], t), 1, 0, t, 0, BANK)
             stage_last_d(e_banks, t)
+            multiply(slices10, product_d(1, 0, d_banks[t], t), 1, 0, t, 0, BANK)
 
         cut = TAIL[0][1]
         parts = (((0, 0, cut), (1, *TAIL[0])), ((0, cut, BANK), (1, *TAIL[1])), ((1, *TAIL[2]),))

@@ -99,8 +99,8 @@ def tile_list_codon_context_rate_kernel(
         load_scale_rows(nc, tab_plane, tab_scales[0])
         nc.sync.dma_start(out=tab[:], in_=tab_words[0].rearrange("p t i -> p (t i)").bitcast(I32))
         load_scale_rows(nc, plane_raw["w1"], w1_scales[0])
-        load_w2(0, 0)
         nc.sync.dma_start(out=w1_raw[:].bitcast(I32), in_=w1_words[0].bitcast(I32))
+        load_w2(0, 0)
         load_w2(0, 1)
         load_scale_rows(nc, plane_raw["w3"], w3_scales[0])
         for u in range(len(PIECES[1])):
@@ -359,9 +359,10 @@ def tile_list_codon_context_rate_kernel(
         gather_plane("down", (0,))
         gather_words("down", (0,))
         gather_plane("down", (1,))
-        stage_e(0, 1, FRONT)
-        slices00 = stage_d(0, 0, BACK)
-        e_banks, d_banks = FRONT[:1] + BACK[:1] + BACK[2:], FRONT[1:] + BACK[1:2]
+        e_first, d_first = FRONT[:3] + BACK[1:2], FRONT[3:] + BACK[:1] + BACK[2:]
+        stage_e(0, 1, e_first)
+        slices00 = stage_d(0, 0, d_first)
+        e_banks, d_banks = e_first[:1] + d_first[:1] + d_first[2:], e_first[1:] + d_first[1:2]
         first_half = tile([P, PASSES, BANK * PACK], BF16, "woven0", W4_RAW_AT[1])
         weave_gpsimd(first_half[:, 0, :], slices00[:])
         gather_words("down", (1,), RATE_AT)

@@ -303,7 +303,7 @@ def tile_list_codon_context_rate_kernel(
                     pass_y(acc, half, 0, c, j0, j1)
             width = j1 - j0
             rows = out.rearrange("(c p) j -> p c j", p=P)[:, :, half * BANK + j0 : half * BANK + j1]
-            joined = width < BANK and not last
+            joined = width < BANK
             if joined:
                 both = tile([P, N // P, width], F32, "res%d_%d" % (half, j0))
             for c, acc in enumerate(sums):

from contextlib import ExitStack

import concourse.mybir as mybir

K, T, S, H, N = 512, 2048, 1024, 1024, 256
FLOPS = 2 * (3 * K * H * S + H * N * S)

F32 = mybir.dt.float32
BF16 = mybir.dt.bfloat16
I32 = mybir.dt.int32
U32 = mybir.dt.uint32
U16 = mybir.dt.uint16
U8 = mybir.dt.uint8
FP8X4 = mybir.dt.float8_e4m3fn_x4
FP4X4 = mybir.dt.float4_e2m1fn_x4
ACT = mybir.ActivationFunctionType
ALU = mybir.AluOpType

P = 128
PACK = 4
PAIR = 2
BANK = 512
FRONT, BACK = (0, 1, 2, 3), (4, 5, 6, 7)
PASSES = H // (P * PACK)
M = H // PACK
PIECES = (((0, 256), (256, 512)), ((0, 256), (256, 384), (384, 512)))
TAIL = ((0, 256), (256, 384), (384, 512))
GPSIMD_SITES = 256

WORDS = 4 * BANK
W2_PIECE_AT = 2 * WORDS
W2_BF_AT = 5 * WORDS
W3_DEALT_AT = W2_BF_AT - WORDS + 64
W4_RAW_AT = (None, 8 * WORDS)
RATE_AT = 12 * WORDS


def load_scale_rows(nc, plane, rows):
    for r in range(4):
        nc.sync.dma_start(
            out=plane[r:P:32, :].bitcast(I32),
            in_=rows[r:16:4, :].bitcast(I32),
        )


def load_bias(nc, dst, bias):
    runs = bias.rearrange("(b g e) -> g b e", b=PASSES, e=PAIR * PACK)
    width = PAIR * PACK - 1
    for v in range(PAIR):
        nc.sync.dma_start(out=dst[v:P:PAIR, :, 0:width], in_=runs[:, :, v : v + width])


def tile_list_codon_context_rate_kernel(
    tc, tab_words, tab_scales, offs, offs2, offs3, w1_words, w1_scales, w2, w3_words, w3_scales, w4, b1, b3, b4, out
):
    nc = tc.nc
    with ExitStack() as ctx:
        keep = ctx.enter_context(tc.tile_pool(name="keep", bufs=1))
        shared = ctx.enter_context(tc.tile_pool(name="shared", bufs=1))
        psum = ctx.enter_context(tc.psum_pool(name="psum", bufs=1))

        def tile(shape, dtype, name, at=None):
            if at is None:
                return keep.tile(shape, dtype, name=name, align_bytes=64)
            return shared.tile(shape, dtype, name=name, offset=at, align_bytes=64)

        def bank(n):
            return psum.tile([P, BANK], F32, name="bank%d" % n, tag="bank%d" % n)

        tab_plane = tile([P, T], U8, "tab_plane")
        nc.gpsimd.memset(tab_plane[:].bitcast(I32), 0)
        plane_raw = {"w1": tile([P, H], U8, "w1_plane_raw"), "w3": tile([P, H], U8, "w3_plane_raw")}
        for raw in plane_raw.values():
            nc.vector.memset(raw[:].bitcast(I32), 0)

        lists = {name: keep.tile([P, S // 16], U16, name="list_" + name) for name in ("own", "up", "down")}
        tab = tile([P, T], I32, "tab")
        w1_raw = tile([P, 2 * H], U8, "w1_raw")
        w3_raw = [tile([P, BANK], I32, "w3_raw%d" % b) for b in range(PASSES)]
        w2_raw = {
            (b, u): tile([P, PACK, c1 - c0], F32, "w2_raw%d%d" % (b, u), W2_PIECE_AT if (b, u) == (1, 0) else None)
            for b in range(PASSES)
            for u, (c0, c1) in enumerate(PIECES[b])
        }
        w4_raw = [tile([P, PACK, N], F32, "w4_raw%d" % b, W4_RAW_AT[b]) for b in range(PASSES)]
        b1_sb = tile([P, PASSES, PAIR * PACK], F32, "b1_sb")
        b3_sb = tile([P, PASSES, PAIR * PACK], F32, "b3_sb")
        b4_sb = tile([P, N // P], F32, "b4_sb")

        w2_rows = w2.rearrange("(p i) c -> p i c", i=PACK)
        w4_rows = w4.rearrange("(b g t v) n -> b v g t n", b=PASSES, t=PACK, v=PAIR)

        def load_w2(b, u):
            c0, c1 = PIECES[b][u]
            nc.sync.dma_start(out=w2_raw[b, u][:], in_=w2_rows[:, :, b * BANK + c0 : b * BANK + c1])

        for name, src in (("own", offs), ("up", offs2)):
            nc.sync.dma_start(lists[name][:], src)
        load_scale_rows(nc, tab_plane, tab_scales[0])
        nc.sync.dma_start(out=tab[:], in_=tab_words[0].rearrange("p t i -> p (t i)").bitcast(I32))
        load_scale_rows(nc, plane_raw["w1"], w1_scales[0])
        nc.sync.dma_start(out=w1_raw[:].bitcast(I32), in_=w1_words[0].bitcast(I32))
        load_w2(0, 0)
        load_w2(0, 1)
        load_scale_rows(nc, plane_raw["w3"], w3_scales[0])
        for u in range(len(PIECES[1])):
            load_w2(1, u)
        w3_cols = w3_words[0].rearrange("p c i -> p (c i)").bitcast(I32)
        nc.sync.dma_start(out=w3_raw[0][:], in_=w3_cols[:, 0:BANK])
        nc.sync.dma_start(lists["down"][:], offs3)
        load_bias(nc, b1_sb, b1)
        nc.sync.dma_start(out=w3_raw[1][:], in_=w3_cols[:, BANK : 2 * BANK])
        for b in range(PASSES):
            for v in range(PAIR):
                nc.sync.dma_start(out=w4_raw[b][v:P:PAIR], in_=w4_rows[b, v])
        load_bias(nc, b3_sb, b3)
        with nc.allow_non_contiguous_dma(reason="one bias value a partition"):
            nc.sync.dma_start(out=b4_sb[:], in_=b4.rearrange("(c p) -> p c", p=P))

        picked = {}

        def entries(name, halves):
            return lists[name][:, halves[0] * BANK // 16 : (halves[-1] + 1) * BANK // 16]

        def gather_plane(name, halves, at=None):
            dst = tile([P, len(halves) * BANK], U8, "plane_%s%d" % (name, halves[0]), at)
            nc.vector.tensor_copy(dst[:], tab_plane[:].indirect(entries(name, halves)))
            for i, half in enumerate(halves):
                picked["plane", name, half] = dst[:, i * BANK : (i + 1) * BANK]

        def gather_words(name, halves, at=None):
            dst = tile([P, len(halves) * BANK], U32, "words_%s%d" % (name, halves[0]), at)
            nc.vector.tensor_copy(dst[:], tab[:].bitcast(U32).indirect(entries(name, halves)))
            for i, half in enumerate(halves):
                picked["words", name, half] = dst[:, i * BANK : (i + 1) * BANK]

        w_plane = {name: tile([P, H], U8, name + "_plane") for name in plane_raw}
        w1_dealt = tile([P, 2 * H], U8, "w1_dealt")
        w3_dealt = [tile([P, BANK], I32, "w3_dealt0", W3_DEALT_AT), tile([P, BANK], I32, "w3_dealt1", W2_BF_AT + 64)]

        def deal_plane(name):
            nc.gpsimd.tensor_copy(
                out=w_plane[name][:].rearrange("p (t g v) -> p t v g", t=PACK, v=PAIR),
                in_=plane_raw[name][:].rearrange("p (g t v) -> p t v g", t=PACK, v=PAIR),
            )

        def deal_w1():
            nc.gpsimd.tensor_copy(
                out=w1_dealt[:].bitcast(I32).rearrange("p (t c i) -> p c t i", t=PACK, i=4),
                in_=w1_raw[:].bitcast(I32).rearrange("p (c i t) -> p c t i", t=PACK, i=4),
            )

        def deal_w3(b):
            nc.gpsimd.tensor_copy(
                out=w3_dealt[b][:].rearrange("p (t c i v) -> p c t i v", t=PACK, i=2, v=PAIR),
                in_=w3_raw[b][:].rearrange("p (c i t v) -> p c t i v", t=PACK, i=2, v=PAIR),
            )

        w2_bf = [tile([P, BANK * PACK], BF16, "w2_bf%d" % b, W2_BF_AT if b else None) for b in range(PASSES)]
        w2_codes = [tile([P, BANK], U32, "w2_codes%d" % b) for b in range(PASSES)]
        w2_plane = {}

        def cast_w2(b):
            dst = w2_bf[b][:].rearrange("p (t g v i) -> p g t i v", t=PACK, v=PAIR, i=PACK)
            for u, (c0, c1) in enumerate(PIECES[b]):
                src = w2_raw[b, u][:].rearrange("p i (g t v) -> p g t i v", t=PACK, v=PAIR)
                nc.scalar.copy(out=dst[:, c0 // (PAIR * PACK) : c1 // (PAIR * PACK)], in_=src)

        def quant_w2(b, at=None):
            w2_plane[b] = tile([P, BANK], U8, "w2_plane%d" % b, at)
            nc.vector.quantize_mx(out=w2_codes[b][:].bitcast(FP8X4), scales=w2_plane[b][:], in_=w2_bf[b][:])

        w4_bf = tile([P, PASSES, N * PACK], BF16, "w4_bf")
        w4_codes = tile([P, PASSES * N], U32, "w4_codes")
        w4_plane = {}

        def cast_w4(b):
            nc.gpsimd.tensor_copy(
                out=w4_bf[:, b, :].rearrange("p (n t) -> p n t", t=PACK), in_=w4_raw[b][:].rearrange("p t n -> p n t")
            )

        def quant_w4(at):
            plane = tile([P, PASSES * N], U8, "w4_plane", at)
            for b in range(PASSES):
                w4_plane[b] = plane[:, b * N : (b + 1) * N]
            nc.vector.quantize_mx(
                out=w4_codes[:].bitcast(FP8X4), scales=plane[:], in_=w4_bf[:].rearrange("p b c -> p (b c)")
            )

        def pass_w1(acc, half, b, t, first):
            c0 = t * M + b * P
            nc.tensor.matmul_mx(
                out=acc[:],
                lhsT=w1_dealt[:, 2 * c0 : 2 * (c0 + P)].bitcast(FP4X4),
                lhsT_scale=w_plane["w1"][:, c0 : c0 + P],
                rhs=picked["words", "own", half].bitcast(FP8X4),
                rhs_scale=picked["plane", "own", half],
                start=first,
                stop=not first,
            )

        def pass_w2(acc, half, b, t, first):
            nc.tensor.matmul_mx(
                out=acc[:],
                lhsT=w2_codes[b][:, t * P : (t + 1) * P].bitcast(FP8X4),
                lhsT_scale=w2_plane[b][:, t * P : (t + 1) * P],
                rhs=picked["words", "up", half].bitcast(FP8X4),
                rhs_scale=picked["plane", "up", half],
                start=first,
                stop=not first,
            )

        opened = {}
        rate = {(half, b): tile([P, PACK, BANK], F32, "rate%d%d" % (half, b), None if half or b else RATE_AT) for half in range(2) for b in range(PASSES)}

        def bias(sb, b, t):
            return sb[:, b, PAIR * t : PAIR * t + 1]

        def open_e(half, b, banks, opening, slices=range(PACK)):
            for t in slices:
                opened[half, b, t] = bank(banks[t])
                opening(opened[half, b, t], half, b, t, True)

        def close_e(half, b, closing, slices=range(PACK)):
            for t in slices:
                acc = opened[half, b, t]
                closing(acc, half, b, t, False)
                nc.scalar.activation(rate[half, b][:, t, :], acc[:], ACT.Exp, bias=bias(b1_sb, b, t))

        def stage_e(half, b, banks, slices=range(PACK)):
            for t in slices:
                open_e(half, b, banks, pass_w2, (t,))
                close_e(half, b, pass_w1, (t,))

        def product_d(half, b, n, t):
            acc = bank(n)
            c0 = t * M + b * P
            nc.tensor.matmul_mx(
                out=acc[:],
                lhsT=w3_dealt[b][:, t * P : (t + 1) * P].bitcast(FP8X4),
                lhsT_scale=w_plane["w3"][:, c0 : c0 + P],
                rhs=picked["words", "down", half].bitcast(FP8X4),
                rhs_scale=picked["plane", "down", half],
                start=True,
                stop=True,
            )
            return acc

        woven = {}

        def multiply(dst, acc, half, b, t, j0, j1):
            nc.vector.scalar_tensor_tensor(
                dst[:, t, :], acc[:, j0:j1], bias(b3_sb, b, t), rate[half, b][:, t, j0:j1], ALU.add, ALU.mult
            )

        def stage_d(half, b, banks, at=None):
            dst = tile([P, PACK, BANK], BF16, "slices%d%d" % (half, b), at)
            for t in range(PACK):
                multiply(dst, product_d(half, b, banks[t], t), half, b, t, 0, BANK)
            return dst

        def weave_gpsimd(dst, src):
            nc.gpsimd.tensor_copy(out=dst.rearrange("p (c t) -> p c t", t=PACK), in_=src.rearrange("p t c -> p c t"))

        def weave_lines(copy, dst, src):
            copy(
                out=dst.rearrange("p (c i t) -> p c t i", i=4, t=PACK),
                in_=src.rearrange("p t (c i) -> p c t i", i=4),
            )

        h_codes = {}
        h_plane = {}

        def quant_h(src, half, part, at=None):
            width = sum(j1 - j0 for b, j0, j1 in part)
            label = "%d_%d_%d" % (half, *part[0][:2])
            codes = tile([P, width], U32, "h_codes" + label)
            plane = tile([P, width], U8, "h_plane" + label, at)
            nc.vector.quantize_mx(out=codes[:].bitcast(FP8X4), scales=plane[:], in_=src)
            start = 0
            for b, j0, j1 in part:
                for a0, a1 in ((0, BANK),) + TAIL:
                    if j0 <= a0 and a1 <= j1:
                        h_codes[half, b, a0, a1] = codes[:, start + a0 - j0 : start + a1 - j0]
                        h_plane[half, b, a0, a1] = plane[:, start + a0 - j0 : start + a1 - j0]
                start += j1 - j0

        def pass_y(acc, half, b, c, j0, j1):
            nc.tensor.matmul_mx(
                out=acc[:, 0 : j1 - j0],
                lhsT=w4_codes[:, b * N + c * P : b * N + (c + 1) * P].bitcast(FP8X4),
                lhsT_scale=w4_plane[b][:, c * P : (c + 1) * P],
                rhs=h_codes[half, b, j0, j1].bitcast(FP8X4),
                rhs_scale=h_plane[half, b, j0, j1],
                start=(b == 0),
                stop=(b == PASSES - 1),
            )

        def stage_y(banks, half, j0, j1, shared_out=False, last=False):
            sums = [bank(n) for n in banks]
            if last:
                for c, acc in enumerate(sums):
                    pass_y(acc, half, 0, c, j0, j1)
            width = j1 - j0
            rows = out.rearrange("(c p) j -> p c j", p=P)[:, :, half * BANK + j0 : half * BANK + j1]
            joined = width < BANK
            if joined:
                both = tile([P, N // P, width], F32, "res%d_%d" % (half, j0))
            for c, acc in enumerate(sums):
                for b in range(1 if last else 0, PASSES):
                    pass_y(acc, half, b, c, j0, j1)
                res = both[:, c, :] if joined else tile([P, width], F32, "res%d%d_%d" % (half, c, j0))[:]
                if shared_out and c == 1:
                    nc.vector.tensor_scalar(res, acc[:, 0:width], b4_sb[:, c : c + 1], None, ALU.add)
                    queue = nc.sync
                else:
                    nc.scalar.activation(res, acc[:, 0:width], ACT.Identity, bias=b4_sb[:, c : c + 1])
                    queue = nc.scalar if last else nc.sync
                if not joined:
                    queue.dma_start(out=rows[:, c, :], in_=res)
            if joined:
                nc.sync.dma_start(out=rows, in_=both[:])

        last_down = tile([P, PACK, BANK], F32, "last_down")

        def stage_last_d(banks, t):
            acc = product_d(1, 1, banks[t], t)
            nc.scalar.activation(last_down[:, t, :], acc[:], ACT.Identity, bias=bias(b3_sb, 1, t))

        def multiply_last(j0, j1, dst):
            nc.vector.tensor_tensor(
                out=dst.rearrange("p (c i t) -> p c t i", i=2, t=PACK),
                in0=rate[1, 1][:, :, j0:j1].rearrange("p t (c i) -> p c t i", i=2),
                in1=last_down[:, :, j0:j1].rearrange("p t (c i) -> p c t i", i=2),
                op=ALU.mult,
            )

        gather_plane("own", (0, 1))
        gather_plane("up", (0,))
        cast_w2(0)
        cast_w2(1)
        gather_words("own", (0,))
        gather_words("own", (1,))
        gather_words("up", (0, 1))
        deal_plane("w1")
        deal_w1()
        deal_plane("w3")
        open_e(0, 0, FRONT, pass_w1)
        open_e(1, 0, BACK, pass_w1)
        quant_w2(0)
        close_e(0, 0, pass_w2)
        gather_plane("up", (1,), W2_PIECE_AT)
        close_e(1, 0, pass_w2)
        quant_w2(1)
        deal_w3(0)
        deal_w3(1)
        cast_w4(0)
        cast_w4(1)
        gather_plane("down", (0,))
        gather_words("down", (0,))
        gather_plane("down", (1,))
        e_first, d_first = FRONT[:3] + BACK[1:2], FRONT[3:] + BACK[:1] + BACK[2:]
        stage_e(0, 1, e_first)
        slices00 = stage_d(0, 0, d_first)
        e_banks, d_banks = e_first[:1] + d_first[:1] + d_first[2:], e_first[1:] + d_first[1:2]
        first_half = tile([P, PASSES, BANK * PACK], BF16, "woven0", W4_RAW_AT[1])
        weave_gpsimd(first_half[:, 0, :], slices00[:])
        gather_words("down", (1,), RATE_AT)
        stage_e(1, 1, d_banks)
        slices01 = stage_d(0, 1, e_banks)
        cut = GPSIMD_SITES
        weave_gpsimd(first_half[:, 1, 0 : cut * PACK], slices01[:, :, 0:cut])
        weave_lines(nc.scalar.copy, first_half[:, 1, cut * PACK :], slices01[:, :, cut:])
        slices10 = tile([P, PACK, BANK], BF16, "slices10")
        for t in range(PACK):
            stage_last_d(e_banks, t)
            multiply(slices10, product_d(1, 0, d_banks[t], t), 1, 0, t, 0, BANK)

        cut = TAIL[0][1]
        parts = (((0, 0, cut), (1, *TAIL[0])), ((0, cut, BANK), (1, *TAIL[1])), ((1, *TAIL[2]),))
        inputs = {}
        joined = []
        for n, part in enumerate(parts):
            width = sum(j1 - j0 for b, j0, j1 in part)
            joined.append(tile([P, width * PACK], BF16, "woven1_%d" % n))
            at = 0
            for b, j0, j1 in part:
                inputs[b, j0] = joined[n][:, at * PACK : (at + j1 - j0) * PACK]
                at += j1 - j0
        weave_lines(nc.scalar.copy, inputs[0, 0], slices10[:, :, 0:cut])
        weave_lines(nc.scalar.copy, inputs[0, cut], slices10[:, :, cut:])

        quant_w4(W3_DEALT_AT)
        quant_h(first_half[:].rearrange("p b c -> p (b c)"), 0, ((0, 0, BANK), (1, 0, BANK)), W3_DEALT_AT + BANK)
        stage_y(e_banks[:2], 0, 0, BANK)
        multiply_last(*TAIL[0], inputs[1, TAIL[0][0]])
        multiply_last(*TAIL[1], inputs[1, TAIL[1][0]])
        quant_h(joined[0][:], 1, parts[0])
        multiply_last(*TAIL[2], inputs[1, TAIL[2][0]])
        quant_h(joined[1][:], 1, parts[1])
        quant_h(joined[2][:], 1, parts[2])
        for piece, banks in zip(TAIL, (e_banks[2:], d_banks[:2], d_banks[2:])):
            stage_y(banks, 1, *piece, shared_out=(piece != TAIL[0]), last=(piece == TAIL[-1]))
